import numpy as np, ml_dtypes
CORES = [36,164,52,180,100,228,116,244]
N = 8
import mx_ref
BF = ml_dtypes.bfloat16
def gcols(t, e):
    v = np.concatenate([t.reshape(8, 16, -1, 4), np.zeros((8, 16, 1, 4), BF)], axis=2)
    return np.ascontiguousarray(np.stack([v[g][:, e[g]] for g in range(8)])).reshape(128, -1)
def tile(rs):
    return np.stack(rs, axis=2).reshape(128, -1).astype(BF)
def pick(q, e):
    c = np.concatenate([q[0].reshape(128, -1, 4), np.zeros((128, 1, 4), np.uint8)], axis=1); s = np.concatenate([q[1], np.ones((16, 1), np.uint8)], axis=1)
    return (np.ascontiguousarray(c[:, e].reshape(128, -1)), np.ascontiguousarray(s[:, e]))
def join(*qs):
    return (np.concatenate([q[0] for q in qs], axis=1), np.concatenate([q[1] for q in qs], axis=1))
def put(q, e, v):
    c, s = q[0].reshape(128, -1, 4).copy(), q[1].copy(); c[:, e] = v[0].reshape(128, -1, 4); s[:, e] = v[1]
    return (c.reshape(128, -1), s)
def pk(c, s):
    return (np.ascontiguousarray(c), mx_ref.live(s))
def emit(q):
    return q[0], q[1]
def packed(v, rng):
    q = [mx_ref.quantize(np.ascontiguousarray(v[r])) for r in range(N)]
    return np.stack([a for a, b in q]), np.stack([mx_ref.plane(b, rng) for a, b in q])
def values_of_codes():
    e, c = np.zeros((128, 128, 4), np.float32), np.zeros((128, 2, 4), np.uint8)
    e[np.arange(128), np.arange(128), 0] = 1
    c[:127, :, 0] = np.arange(256).reshape(2, 128).T[:127]
    return mx_ref.matmul(mx_ref.quantize(e.reshape(128, 512).astype(BF)), (c.reshape(128, 8), np.full((16, 2), 127, np.uint8))).T.reshape(-1).astype(np.float64)
CODE_VALUE, SCALE_VALUE = values_of_codes(), 2.0 ** (np.arange(256) - 127.0)
def decode(q):
    return (CODE_VALUE[q[0]].reshape(16, 8, -1, 4) * SCALE_VALUE[q[1]][:, None, :, None] + 0.0).reshape(128, -1).astype(np.float32)
def f(rng, *shape):
    return mx_ref.flush((rng.standard_normal(shape, dtype=np.float32) * np.exp2(rng.integers(-2, 3, shape[:-1] + (1,)))).astype(BF))
def wide(rng, *shape, cols=0):
    v = rng.standard_normal(shape, dtype=np.float32) * np.exp2(rng.integers(-12, 13, shape)).astype(np.float32)
    if cols: v *= np.repeat(np.exp2(rng.integers(-cols, cols + 1, shape[:-2] + (1, shape[-1] // 4))) * (rng.random(shape[:-2] + (1, shape[-1] // 4)) > 0.0625), 4, axis=-1).astype(np.float32)
    return mx_ref.flush(v.astype(BF))
C, E = 352, 10
def big(v):
    v = v.astype(np.float32)
    v[np.abs(v) < np.float32(2.0 ** -16)] = 0
    return v.astype(BF)
def numbers_of(rng):
    return big(f(rng, N, 128, 4 * C)), big(f(rng, N, 128, 128)), np.array(f(rng, N, 128, 512)), np.array(f(rng, N, 128, 512))
def layers(rng):
    return big(f(rng, N, 128, 2048)).reshape(N, 8, 16, 4, 8, 16, 4)
def some(rng, k):
    return np.argsort(np.argsort(rng.random((8, 32)), axis=1), axis=1) < k
def flags(rng):
    k = np.where(some(rng, E // 2), -1.0, rng.random((N, 8, 32)))
    fl = np.ones((N, 8, 32), np.int32)
    np.put_along_axis(fl, np.argsort(k, axis=2)[:, :, :E], 0, axis=2)
    return fl
def relabels(rng):
    return np.argsort(rng.random((N, 7, 32, 32)), axis=3)
def drawn(rng, x, tr, u, v, fl, w, ti=None):
    t = tr.astype(np.float32).reshape(N, 8, 16, 32, 4).copy()
    t[np.broadcast_to((fl == 0)[:, :, None, :, None], t.shape)] = 0
    if ti is None: ti = relabels(rng)
    c, p = packed(np.ascontiguousarray(w).reshape(N, 128, 2048), rng)
    return {"x": np.ascontiguousarray(x).reshape(N, 128, 4 * C).astype(BF), "tr": t.reshape(N, 128, 128).astype(BF), "u": np.ascontiguousarray(u).reshape(N, 128, 512), "v": v, "fl": fl, "ti": ti.reshape(N, 7, 1024).astype(np.int32), "wc": c, "ws": p}
def setup_inputs(rng):
    x, tr, u, v = numbers_of(rng)
    return drawn(rng, x, tr, u, v, flags(rng), layers(rng))
def setup_inputs_ties(rng):
    x, tr, u, v = numbers_of(rng)
    o = rng.permutation(N)
    x = x.reshape(N, 8, 16, C, 4)
    for r in range(N):
        a = x[r][:, :8, :24].copy()
        a[:, :, 23] = 0
        k = rng.permutation(C) % 24
        if r == o[0]: k = np.zeros(C, int)
        if r == o[1]: k = np.full(C, 23)
        x[r][:, :8] = a[:, :, k]
    u = u.reshape(N, 8, 16, 128, 4)
    for i in range(5): u[:, :, 8:, i::16] = 0
    w = layers(rng)
    w[:, :, :, :, :, :8] = 0
    return drawn(rng, x, tr, u, v, flags(rng), w)
def setup_inputs_near(rng):
    x, tr, u, v = numbers_of(rng)
    fl, ti = flags(rng), relabels(rng)
    a = int(rng.integers(N))
    fl[(a + 1) % N] = fl[a]
    o = rng.permutation(N) % 2
    x = x.astype(np.float32).reshape(N, 8, 16, C, 4)
    tr = tr.astype(np.float32).reshape(N, 8, 16, 32, 4)
    x[:, :, :8] = 0
    tr[:, :, :8] = 0
    u = u.reshape(N, 128, 128, 4)
    for i in range(5): u[:, :, i::16] = 0
    for r in range(N):
        k = 2.0 ** -30 if o[r] == 0 else 1.0
        x[r, :, :5, :, 0] = k * rng.integers(-1, 2, (8, 5, C))
        tr[r, :, :5, :, 0] = k * rng.integers(-1, 2, (8, 5, 32))
        for g in rng.permutation(8)[:4]: x[r, g, :5, rng.integers(C), 0] = 2.0 ** 27 * rng.choice([-1.0, 1.0], 5)
        for h in range(0, 128, 16):
            for i in range(5): u[r, h + i, h + i, 0] = k
    hole = np.stack([np.flatnonzero(fl[a, g] == 0) for g in range(8)])
    held = np.stack([np.flatnonzero(fl[a, g] == 1) for g in range(8)])
    n = np.arange(8 * E)
    b = held[np.arange(8)[:, None], rng.integers(0, 32 - E, (8, 8 * E))]
    b[n // E, n] = hole[n // E, n % E]
    back = np.argsort(ti[a], axis=2)
    e = b.copy()
    for g in range(8):
        for h in range(g - 1, -1, -1): e[g] = back[h, b[h], e[g]]
    bit = (e[:, None] >> np.arange(4, -1, -1)[:, None]) & 1
    j = rng.permutation(C)[:8 * E]
    s = x[a, :, :5, :, 0]
    m = np.abs(s[:, :, j])
    s[:, :, j] = np.where(bit == 1, np.maximum(m, 2.0 ** -30 if o[a] == 0 else 1.0), 0.0 - m)
    x[a, :, :5, :, 0] = s
    w = layers(rng)
    w[:, :, :8] = 0
    w[:, :, :, :, :, :8] = 0
    return drawn(rng, x, tr, u, v, fl, w, ti)
def setup_inputs_deep(rng):
    x, tr, u, v = numbers_of(rng)
    x = (rng.integers(0, 2, x.shape) * 2.0 - 1.0) * (0.8 + 0.2 * rng.random(x.shape)) * 2.0 ** 26
    tr = (rng.integers(0, 2, tr.shape) * 2.0 - 1.0) * (0.8 + 0.2 * rng.random(tr.shape)) * 2.0 ** 26
    u = (rng.integers(0, 2, u.shape) * 2.0 - 1.0) * (0.9 + 0.1 * rng.random(u.shape)) * 2.0 ** 30
    o = rng.permutation(N)
    m = some(rng, E)
    fl = np.ones((N, 8, 32), np.int32)
    for r in range(N):
        if r == o[1]: fl[r, 7][m[7]] = 0
        elif r == o[2]: fl[r, 0][m[0]] = 0
        elif r != o[0]: fl[r][m] = 0
    w = (layers(rng).astype(np.float32) * np.float32(0.0625)).astype(BF)
    return drawn(rng, x.astype(np.float32), tr.astype(np.float32), u.astype(np.float32).astype(BF), v, fl, w)
def setup_inputs_odd(rng):
    x, tr, u, v = numbers_of(rng)
    x = (1.125 + 0.25 * rng.integers(0, 4, (N, 16, 8, C, 4))) * np.exp2(-rng.integers(8, 15, (N, 16, 8, C, 4)).astype(np.float32))
    x[:, :, 0, :, 0] = 1.96875
    x = x * (rng.integers(0, 2, x.shape) * 2.0 - 1.0) * np.exp2(rng.integers(-2, 3, (N, 16, 1, C, 1)).astype(np.float32))
    return drawn(rng, x.astype(np.float32), tr, u, v, flags(rng), layers(rng))
def setup_inputs_spread(rng):
    x, tr, u, v = numbers_of(rng)
    return drawn(rng, big(wide(rng, N, 128, 4 * C, cols=6)), big(wide(rng, N, 128, 128)), u, v, flags(rng), layers(rng))
def check_inputs(d):
    b = []
    for k in ("x", "tr", "u", "v"):
        a = np.abs(d[k].astype(np.float32))
        if not (np.isfinite(a).all() and ((a == 0) | (a >= 2.0 ** -30) & (a <= 2.0 ** 30)).all()): b.append("a value of " + k)
    fl = d["fl"]
    if not ((fl == 0) | (fl == 1)).all(): b.append("a flag of fl")
    if (np.sum(fl == 0, axis=2) > E).any(): b.append("too many empty slots in a level")
    if ((d["tr"].astype(np.float32).reshape(N, 8, 16, 32, 4) != 0) & (fl == 0)[:, :, None, :, None]).any(): b.append("tr isn't zero at an empty slot")
    if (np.sort(d["ti"].reshape(N, 7, 32, 32), axis=3) != np.arange(32)).any(): b.append("ti: not the points in some order")
    none, least, most = [emit(mx_ref.quantize(np.full((128, 16), k, np.float32).astype(BF)))[1][0, 0] for k in (0.0, 2.0 ** -30, 2.0 ** 30)]
    for r in range(N):
        if ((d["wc"][r] == 0x7F) | (d["wc"][r] == 0xFF)).any(): b.append("wc: a code that is no number")
        s = mx_ref.live(d["ws"][r])
        if ((s != none) & ((s < least) | (s > most))).any(): b.append("ws: a scale out of range")
    return b
def reference(x, tr, u, v, fl, ti, wc, ws):
    qu = [mx_ref.quantize(u[r]) for r in range(N)]
    lay = [pk(wc[r], ws[r]) for r in range(N)]
    now = [x[r] for r in range(N)]
    slot = [decode(mx_ref.quantize(tr[r])).astype(BF) for r in range(N)]
    full = fl > 0
    way = np.zeros((N, 8, C), np.int64)
    for t in range(3):
        claim, came = [], []
        for r in range(N):
            q = mx_ref.quantize(now[r])
            own = decode(q)
            s = mx_ref.matmul(qu[r], q)
            e = 16 * (s[0::16] > 0) + 8 * (s[1::16] > 0) + 4 * (s[2::16] > 0) + 2 * (s[3::16] > 0) + (s[4::16] > 0)
            fail = np.full(C, 8)
            for g in range(8):
                going = fail == 8
                way[r, g] = np.where(going, e[g], -1)
                fail = np.where(going & ~full[r, g][e[g]], g, fail)
                if g < 7: e[g + 1:] = ti[r, g][32 * e[g] + e[g + 1:]]
            passed = np.where(np.arange(8)[:, None] < fail, way[r], -1)
            z = (own - gcols(slot[r], passed).astype(np.float32)).astype(BF)
            q = mx_ref.quantize(z)
            c = np.full((8, 32), C)
            j = np.flatnonzero(fail < 8)
            np.minimum.at(c, (fail[j], way[r][fail[j], j]), j)
            claim.append(c < C)
            came.append(gcols(decode(q).astype(BF), np.where(c < C, c, -1)))
            now[r] = tile([mx_ref.matmul(pick(lay[r], np.arange(128 * b, 128 * b + 128)), q) * np.float32(0.015625) + z[:, b::4].astype(np.float32) for b in range(4)])
        for r in range(N):
            take = claim[(r - 1) % N] & ~full[r]
            slot[r] = gcols(np.concatenate([slot[r], came[(r - 1) % N]], axis=1), np.arange(32) + 32 * take)
            full[r] = full[r] | take
    y, bp, rt = np.zeros((N, 128, C), np.float32), np.zeros((N, 8, C + 32), np.float32), np.zeros((N, 128, 128), np.float32)
    oc, osc = np.zeros((N, 128, 4 * C), np.uint8), np.zeros((N, 16, C), np.uint8)
    for r in range(N):
        q = mx_ref.quantize(now[r])
        y[r] = mx_ref.matmul(mx_ref.quantize(v[r]), q)
        bp[r] = np.concatenate([way[r], full[r]], axis=1)
        rt[r] = slot[r].astype(np.float32)
        oc[r], osc[r] = emit(q)
    return {"y": y, "bp": bp, "rt": rt, "oc": oc, "osc": osc}

@@ -1,0 +1,428 @@
+from concourse.bass import IndirectOffsetOnAxis
+from concourse.mybir import dt, AluOpType as OP, AxisListType, ActivationFunctionType
+
+COPY = ActivationFunctionType.Copy
+NV = [128, 128, 96]
+PW, CAME = 160, 112
+NF = 2
+SMALL = {"KI": "pI1 iI1 gI1 c5I1 m7I1 cnI1 rem1 nI2 la2 lb2 lc2 ld2 le2 lf2 ma2 mb2 mc2 md2 me2 mf2",
+         "KF": "iF1 gF1 c5F1 a5F1 nW2 nV2 kF8 gc8",
+         "KL": "flf2 ua2 uk2 uf2 esta2 estb2 estc2 estd2 mxa1 mxb1 cnt1"}
+ALIAS = {}
+for _b, _s in SMALL.items():
+    _k = 0
+    for _n in _s.split():
+        ALIAS[_n[:-1]] = (_b, _k)
+        _k += int(_n[-1])
+EST = ["esta", "estb", "estc", "estd"]
+
+
+def _scratch():
+    f, h, i, u, q, b = "float32", "bfloat16", "int32", "uint16", "float8_e4m3fn_x4", "uint8"
+    s = {"tabd": ("dram", [1, 7424], h), "fdr0": ("dram", [128, 2], h), "fdr1": ("dram", [128, 2], h)}
+    for d, names in ((i, "KI:40 zix:2 tic:64 t32:2048 flI:2"),
+                     (f, "KF:32 KL:32 pF:1 tt:128 dd:128 ge:128 eq:128 qa:128 qb:128 qc:128 qd:128 ix:128 rel:112 wa:112 wb:112 wc1:112 MB:112 wt:352 of1:24 "
+                         "jk:352 MV:352 RT:128 BPO:352 FO:2 YO:384"),
+                     (u, "R1:2 R2:2 UP:8 OF:192 OC:24 L:32 CL:2 UL:2 UL3:4"),
+                     (h, "MS:128 MC:128 hd:128 WM:112 WN:112 r64:8 ET:2048 tib:64 TAB:7424 flc:2 UT:512 VT:512 TT:512 ZT:512 XT:1536 AB:384 SC:3456 GO0:128 GO1:128 GO2:128 "
+                         "CO:384 DS:32 AM:64 FP:768 TG:768 ZS:1536 ZP:1536 TV0:640 TV1:640 TV2:640 CT1:256 CT2:256 CB:256 crow:256 CLT:512 "
+                         "w_0:2 w_1:2 w_2:2 fw0:2 fw1:2 fw2:2")):
+        for n in names.split():
+            n, w = n.split(":")
+            s[n] = ("sbuf", [128, int(w)], d)
+    for n in "EQ:512 QU:128 QP:128 QV:128 QT:128 WC:512 QO:128 QX:384 QZ:384 CQ0:128 CQ1:128 CQ2:128 LC:192".split():
+        n, w = n.split(":")
+        s[n] = ("sbuf", [128, int(w)], q)
+        s[n + "s"] = ("sbuf", [128, int(w)], b)
+    for n, w in (("psS", 1024), ("psF", 1024), ("psR", 2048)):
+        s[n] = ("psum", [128, w], f)
+    return s
+
+
+SCRATCH = _scratch()
+SEMAPHORES = ["sV", "sS", "sT", "sG", "sent", "rf0", "rf1", "rf2", "rc0", "rc1", "rc2"] + ["d%d" % k for k in range(60)]
+PLAN = {}
+WAKE, DMALAT, NETLAT, CYC = 0.1, 2.0, 3.0, 0.00083
+
+
+def bits(v):
+    n, a, b, st = v[:4]
+    if n in ALIAS:
+        n, o = ALIAS[n]
+        a, b = a + o, b + o
+    if n[:2] == "ps":
+        a, b, st = a - a % 512, a - a % 512 + 512, 1
+    return (n, ((1 << (b - a)) - 1) << a if st == 1 else sum(1 << k for k in range(a, b, st)))
+
+
+def plan(ops):
+    hist, deps, n = {}, [], len(ops)
+    for k, o in enumerate(ops):
+        d = set()
+        acc = [bits(v) + (False,) for v in o["R"]] + [bits(v) + (True,) for v in o["W"]]
+        for buf, m, w in acc:
+            d.update(k2 for m2, k2, w2 in hist.get(buf, ()) if (w or w2) and m & m2)
+        for buf, m, w in acc:
+            hist.setdefault(buf, []).append((m, k, w))
+        deps.append(sorted(d))
+    succ = [[] for _ in ops]
+    for k in range(n):
+        for j in deps[k]: succ[j].append(k)
+    prio = [0.0] * n
+    for k in range(n - 1, -1, -1):
+        prio[k] = min(ops[k]["dur"].values()) + ops[k]["lat"] + max([prio[j] for j in succ[k]] + [0.0])
+    left = [len(d) for d in deps]
+    ready = {k: 0.0 for k in range(n) if not left[k]}
+    avail, fin, order = {}, [0.0] * n, []
+    while ready:
+        opts = []
+        for k, r in ready.items():
+            end, st, q = min((max(r, avail.get(q, 0.0)) + du, max(r, avail.get(q, 0.0)), q) for q, du in ops[k]["dur"].items())
+            opts.append((st, -prio[k] - ops[k]["boost"], k, q, end))
+        lo = min(opts)[0] + 0.03
+        st, _, k, q, end = min((o for o in opts if o[0] <= lo), key=lambda o: o[1])
+        del ready[k]
+        avail[q] = end
+        fin[k] = end + ops[k]["lat"]
+        order.append((k, q, st))
+        for j in succ[k]:
+            left[j] -= 1
+            if not left[j]: ready[j] = max(fin[i] for i in deps[j])
+    return order, deps, max(fin)
+
+
+def build(g, core, T, topo, nxt):
+    ops = []
+
+    def ap(v):
+        n, a, b, st = v[:4]
+        if n in ALIAS:
+            n, o = ALIAS[n]
+            a, b = a + o, b + o
+        r = T[n][:, a:b] if st == 1 else T[n][:, a:b:st]
+        if len(v) > 4 and v[4] == "c": return r.bitcast(dt.uint8)
+        return r.indirect(ap(v[4])) if len(v) > 4 else r
+
+    def vw(n, a, b=None, st=1):
+        return (n, a, a + 1 if b is None else b, st)
+
+    def ind(v, *off):
+        return v + (vw(*off),)
+
+    def add(dur, fn, ins, outs, lat=WAKE, kind="c", nd=0, boost=0.0):
+        R = [v[:4] for v in ins] + [v[4][:4] for v in ins if len(v) > 4 and v[4] != "c"]
+        ops.append({"dur": dur, "fn": fn, "R": R, "W": [v[:4] for v in outs], "lat": lat, "kind": kind, "nd": nd, "boost": boost})
+
+    def cost(v, k):
+        n = len(range(v[1], v[2], v[3]))
+        return n, max(64, n * k) * CYC
+
+    def isind(*vs):
+        return any(len(v) > 4 and v[4] != "c" for v in vs)
+
+    def ts(out, in0, s1, s2, op0, op1=None):
+        n, d = cost(out, 1.0)
+        sc = [s for s in (s1, s2) if isinstance(s, tuple)]
+        if isind(in0): d = 0.05 + n * 1.5 * CYC
+        val = lambda s: ap(s) if isinstance(s, tuple) else s
+        if op1 is None: fn = lambda: g.vector.tensor_scalar(ap(out), ap(in0), val(s1), None, op0)
+        else: fn = lambda: g.vector.tensor_scalar(ap(out), ap(in0), val(s1), val(s2), op0, op1)
+        add({"V": d}, {"V": fn}, [in0] + sc, [out])
+
+    def tt(out, a, b, op):
+        n, d = cost(out, 1.0 if a[0][:2] == "ps" else 2.0)
+        if isind(a): d = 0.05 + n * 1.5 * CYC
+        add({"V": d}, {"V": lambda: g.vector.tensor_tensor(ap(out), ap(a), ap(b), op)}, [a, b], [out])
+
+    def cp(out, a, q="V", scale=1.0, acc=None):
+        n, d = cost(out, 1.0)
+        i = isind(a)
+        kw = {}
+        if scale != 1.0: kw["scale"] = scale
+        fns = {"V": lambda: g.vector.tensor_copy(ap(out), ap(a)),
+               "S": lambda: g.scalar.activation(ap(out), ap(a), COPY, accum_out=ap(acc)) if acc else g.scalar.activation(ap(out), ap(a), COPY, **kw)}
+        durs = {"V": 0.05 + n * 1.5 * CYC if i else d, "S": 0.065 + n * 1.5 * CYC if i else d}
+        add({k: durs[k] for k in q}, {k: fns[k] for k in q}, [a], [out] + ([acc] if acc else []))
+
+    def scan(out, d0, d1, init, op0, op1):
+        add({"V": cost(out, 0.5)[1]}, {"V": lambda: g.vector.tensor_tensor_scan(ap(out), ap(d0), ap(d1), init, op0, op1)}, [d0, d1], [out])
+
+    def fill(out, val):
+        add({"V": cost(out, 0.5)[1]}, {"V": lambda: g.vector.memset(ap(out), val)}, [], [out])
+
+    def quant(q, a, t, ta, n=128):
+        c, s, i = vw(q, a, a + n), vw(q + "s", a, a + n), vw(t, ta, ta + 4 * n)
+        add({"V": 0.012 + 0.88e-3 * n}, {"V": lambda: g.vector.quantize_mx(ap(c), ap(s), ap(i))}, [i], [c, s])
+
+    def mm(ps, pa, lq, la, rq, ra, n=128):
+        o = vw(ps, pa, pa + n)
+        i = [vw(lq, la, la + 128), vw(lq + "s", la, la + 128), vw(rq, ra, ra + n), vw(rq + "s", ra, ra + n)]
+        add({"T": (n + 16) * 0.00085}, {"T": lambda: g.tensor.matmul_mx(ap(o), ap(i[0]), ap(i[1]), ap(i[2]), ap(i[3]), True, True)}, i, [o])
+
+    def iota(out, pattern, base, cm, small=True):
+        kw = {"allow_small_or_imprecise_dtypes": True} if small else {}
+        add({"G": 0.13 + cost(out, 2.0)[0] * 2 * CYC}, {"G": lambda: g.iota(ap(out), pattern, base, cm, **kw)}, [], [out])
+
+    def ld(q, pairs, ins, outs, nd=1, boost=0.0):
+        add({q: 0.06 * nd}, {q: lambda: [(g.sync if q == "Y" else g.scalar).dma_start(o, i) for o, i in pairs()]}, ins, outs, DMALAT, "d", nd, boost)
+
+    def rows(out, src, dep, col, last, lat, boost=0.0):
+        ix = vw("zix", col)
+        add({"G": 1.7}, {"G": lambda: g.indirect_dma_start(ap(out), None, T[src][:], IndirectOffsetOnAxis(ap=ap(ix), axis=0), bounds_check=last)}, [ix] + dep, [out], lat, "d", 1, boost)
+
+    def send(out, in_, sem, boost=0.0):
+        ne = 8 if T is None else len(topo.engines(core, nxt))
+        def fn():
+            rid, pid = topo.addr(nxt, core)
+            g.remote_dma(ap(out) if out[0][:3] != "fdr" else T[out[0]][:], ap(in_), T.sem[sem], T.sem.sent, pid, rid, topo.mask(core, nxt))
+        add({"G": 0.3}, {"G": fn}, [in_], [out], NETLAT, "n", (sem, ne), boost)
+
+    iota(vw("zix", 0, 2), [[1, 2]], 0, 0, False)
+    iota(vw("pI", 0), [[0, 1]], 0, 1, False)
+    ld("Y", lambda: [(T.tic[0:112, :], T.ti[:])], [], [vw("tic", 0, 64)], boost=50.0)
+    ld("S", lambda: [(T.UT[:], T.u[:])], [], [vw("UT", 0, 512)], boost=40.0)
+    for c in range(3):
+        v = vw("XT", 512 * c, 512 * c + 4 * NV[c])
+        ld("YSY"[c], lambda v=v: [(ap(v), T.x[:, v[1]:v[2]])], [], [v], boost=45.0 - c)
+    ld("S", lambda: [(T.flI[:], T.fl[:])], [], [vw("flI", 0, 2)], boost=38.0)
+    for l in range(2): rows(vw("t32", 1024 * l, 1024 * l + 1024), "ti", [], l, 6, 3.5, boost=50.0)
+    for o, i, s, op in (("iI", "pI", 15, OP.bitwise_and), ("gI", "pI", 4, OP.arith_shift_right), ("a5F", "pI", 5.0, OP.add)):
+        ts(vw(o, 0), vw(i, 0), s, None, op)
+    cp(vw("c5I", 0), vw("a5F", 0))
+    ts(vw("m7I", 0), vw("c5I", 0), 15, None, OP.bitwise_and)
+    for o, i in (("pF", "pI"), ("iF", "iI"), ("gF", "gI"), ("c5F", "m7I")): cp(vw(o, 0), vw(i, 0))
+    iota(vw("kF", 0, 8), [[16, 8]], 0, 0)
+    iota(vw("tt", 0, 128), [[0, 8], [1, 16]], 0, 0)
+    iota(vw("ix", 0, 128), [[1, 128]], 0, 0)
+    iota(vw("gc", 0, 8), [[1024, 8]], -32, 0)
+    iF, gF = vw("iF", 0), vw("gF", 0)
+    full = lambda n, w=128: vw(n, 0, w)
+    ts(full("UP", 8), full("kF", 8), vw("c5F", 0), None, OP.add)
+    quant("QU", 0, "UT", 0)
+    for s, d in (("QU", "QP"), ("QUs", "QPs")):
+        fn = (lambda: g.vector.tensor_copy(T.QP[:].bitcast(dt.uint32), T.QU[:].bitcast(dt.uint32).indirect(T.UP[:, 0:8]))) if s == "QU" else \
+             (lambda: g.vector.tensor_copy(T.QPs[:], T.QUs[:].indirect(T.UP[:, 0:8])))
+        add({"V": 0.2}, {"V": fn}, [full(s), full("UP", 8)], [full(d)])
+    ts(full("hd"), full("tt"), 12.0, 2.0, OP.is_ge, OP.mult)
+    add({"V": 0.06}, {"V": lambda: g.vector.tensor_scalar(T.tib[0:112, :], T.tic[0:112, :], 1.0, -1.0, OP.add, OP.mult)}, [full("tic", 64)], [full("tib", 64)])
+    ts(full("nW", 2), full("kF", 2), iF, None, OP.add)
+    ts(full("flf", 2), full("flI", 2), -33.0, -127.0, OP.mult, OP.add)
+    tt(full("flc", 2), full("flf", 2), full("nW", 2), OP.add)
+    ts(full(EST[0], 2), full("flI", 2), 0.0, float(CAME), OP.is_equal, OP.mult)
+    ld("Y", lambda: [(T.tabd[0:1, 0:7168], T.tib[0:112, :])], [full("tib", 64)], [vw("tabd", 0, 7168)])
+    ld("Y", lambda: [(T.tabd[0:1, 7168:7424], T.flc[:])], [full("flc", 2)], [vw("tabd", 7168, 7424)])
+    rows(full("TAB", 7424), "tabd", [full("tabd", 7424)], 0, 0, 5.0)
+    ts(full("dd"), full("tt"), iF, None, OP.subtract)
+    ts(full("ge"), full("dd"), 0.0, None, OP.is_ge)
+    ts(full("qa"), full("dd"), 0.0, 31.0, OP.is_equal, OP.mult)
+    tt(full("qb"), full("ge"), full("qa"), OP.add)
+    ts(vw("eq", 0, 16), vw("tt", 0, 16), 15.0, -2.0, OP.is_equal, OP.mult)
+    ts(vw("eq", 16, 128), vw("tt", 16, 128), 15.0, -33.0 / 32.0, OP.is_equal, OP.mult)
+    ts(full("qc"), full("eq"), 1.0, None, OP.add)
+    tt(full("MS"), full("qb"), full("qc"), OP.mult)
+    fill(full("ET", 2048), 0.0)
+    for k in range(4):
+        ts(vw("ET", 513 * k, 512 * k + 512, 4), full("ix"), vw("pF", 0), 0.015625, OP.is_equal, OP.mult)
+        quant("EQ", 128 * k, "ET", 512 * k)
+    ts(full("qa"), full("ge"), -128.0, 128.0, OP.mult, OP.add)
+    ts(full("qb"), full("dd"), 0.0, -64.0, OP.is_equal, OP.mult)
+    ts(full("qc"), full("tt"), 15.0, 192.0, OP.is_equal, OP.mult)
+    tt(full("qd"), full("qa"), full("qb"), OP.add)
+    tt(full("MC"), full("qd"), full("qc"), OP.add)
+    fill(full("r64", 8), 64.0)
+    fill(full("AM", 64), 0.0)
+    fill(vw("XT", 1408, 1536), 0.0)
+    fill(vw("ZS", 1408, 1536), 0.0)
+    for k in range(4): fill(vw("ZP", 384 * k + 352, 384 * k + 384), 0.0)
+    fill(vw("TT", 128, 512), 0.0)
+    ld("S", lambda: [(T.TT[:, 0:128], T.tr[:])], [], [full("TT")], boost=20.0)
+    quant("QT", 0, "TT", 0)
+    for t in range(3): fill(full("TV%d" % t, 640), 0.0)
+    for k in range(4):
+        b = 512 * (k % 2)
+        mm("psF", b, "EQ", 128 * k, "QT", 0)
+        for s in range(2): cp(vw("TV0", PW * k + 16 * s, PW * k + 16 * s + 16), vw("psF", b + s, b + 32, 2), "S", -1.0)
+    two = lambda n: vw(n, 0, 2)
+    cp(two("nI"), two("nW"))
+    for o, i, s, s2, op, op2 in (("la", "nI", 11.0, None, OP.mult, None), ("lb", "la", 5, None, OP.arith_shift_right, None), ("lc", "lb", -24.0, None, OP.mult, None),
+                                 ("ld", "lb", gF, None, OP.add, None), ("le", "ld", 7, None, OP.bitwise_and, None), ("lf", "nI", 8.0, None, OP.mult, None)):
+        ts(two(o), two(i), s, s2, op, op2)
+    tt(two("la"), two("lc"), two("lf"), OP.add)
+    tt(two("ld"), two("la"), two("le"), OP.add)
+    cp(two("R1"), two("ld"))
+    for o, i, s, s2, op, op2 in (("ma", "nI", 3, None, OP.arith_shift_right, None), ("mb", "nI", 7, None, OP.bitwise_and, None), ("mc", "mb", -1.0, gF, OP.mult, OP.add),
+                                 ("md", "mc", 8.0, None, OP.add, None), ("me", "md", 7, None, OP.bitwise_and, None), ("mf", "me", 0.0, 32.0, OP.is_gt, OP.mult),
+                                 ("mb", "me", 3.0, None, OP.mult, None)):
+        ts(two(o), two(i), s, s2, op, op2)
+    tt(two("mc"), two("mb"), two("ma"), OP.add)
+    tt(two("md"), two("mc"), two("mf"), OP.add)
+    cp(two("R2"), two("md"))
+    ts(full("rel", 112), full("ix", 112), iF, -33.0, OP.subtract, OP.add)
+    ts(full("wa", 112), full("rel", 112), 0.0, None, OP.is_equal)
+    ts(full("wb", 112), full("rel", 112), 16.0, None, OP.is_equal)
+    ts(full("wc1", 112), full("rel", 112), 16.0, 1024.0, OP.is_equal, OP.mult)
+    tt(full("WM", 112), full("wa", 112), full("wb", 112), OP.subtract)
+    tt(full("WN", 112), full("wa", 112), full("wc1", 112), OP.add)
+    iota(full("wt", 352), [[-1, 352]], 352, 0)
+    ts(two("nV"), two("nW"), -160.0, None, OP.add)
+    fill(vw("CLT", 128, 512), 0.0)
+    fill(full("ZT", 512), 0.0)
+    quant("QO", 0, "ZT", 0)
+    ld("Y", lambda: [(T.LC[:, 32:128].bitcast(dt.uint8), T.QO[:, 0:96].bitcast(dt.uint8))], [full("QO", 96)], [vw("LC", 32, 128)])
+    ld("Y", lambda: [(T.LCs[:, 32:128], T.QOs[:, 0:96])], [full("QOs", 96)], [vw("LCs", 32, 128)])
+    ld("Y", lambda: [(T.WC[:].bitcast(dt.uint8), T.wc[:])], [], [full("WC", 512)])
+    ld("S", lambda: [(T.WCs[:], T.ws[:])], [], [full("WCs", 512)])
+    fill(full("MB", 112), -1.0)
+    for a in (0, 33): iota(vw("MB", a, a + 32), [[1, 2], [2, 16]], 0, 0)
+    ld("S", lambda: [(T.VT[:], T.v[:])], [], [full("VT", 512)])
+    quant("QV", 0, "VT", 0)
+
+    ctn, cta = "TAB", 7168
+    for t in range(3):
+        for c in range(3):
+            quant("QX", 128 * c, "XT", 512 * c)
+            b, s0 = 512 * (c % 2), 1152 * c
+            mm("psS", b, "QX", 128 * c, "QP", 0)
+            ab = vw("AB", 128 * c, 128 * c + 128)
+            ts(ab, vw("psS", b, b + 128), 0.0, None, OP.is_gt)
+            scan(vw("SC", s0, s0 + 128), full("hd"), ab, 0.0, OP.mult, OP.add)
+            ts(vw("SC", s0 + 15), vw("SC", s0 + 15), 32.0, 32.0, OP.mult, OP.add)
+        for l in range(7):
+            for c in range(3):
+                s0, n, o0, go = 1152 * c, 7 - l, 64 * c + 8 * l, "GO%d" % c
+                ts(vw("OF", o0, o0 + n), vw("SC", s0 + 144 * l + 31, s0 + 128 * l + 128, 16), vw("SC", s0 + 144 * l + 15), -32.0 if l == 0 else -33.0, OP.add, OP.add)
+                gout = full(go, 16 * n)
+                if t == 0 and l < 2: ts(gout, ind(vw("t32", 1024 * l, 1024 * l + 1024), "OF", o0, o0 + n), 1.0, -1.0, OP.add, OP.mult)
+                else: cp(gout, ind(vw("TAB", 1024 * l, 1024 * l + 1024), "OF", o0, o0 + n), "VS")
+                scan(vw("SC", s0 + 144 * (l + 1), s0 + 128 * (l + 2)), gout, full("MS", 16 * n), 0.0, OP.min, OP.mult)
+        for k in range(NF):
+            mm("psF", 512 * (k % 2), "EQ", 128 * k, "QX", 0, 384)
+            cp(vw("FP", 384 * k, 384 * k + 352), vw("psF", 512 * (k % 2), 512 * (k % 2) + 352), "S")
+        if t:
+            fd, nn = "fdr%d" % (t - 1), "CT%d" % t
+            ld("Y", lambda fd=fd: [(T.crow[0:1, :], T[fd][:])], [two(fd)], [full("crow", 256)])
+            add({"G": 1.0}, {"G": lambda: g.partition_broadcast(T.CB[:], T.crow[0:1, :], 128)}, [full("crow", 256)], [full("CB", 256)])
+            tt(full(nn, 256), vw(ctn, cta, cta + 256), full("CB", 256), OP.min)
+            ctn, cta = nn, 0
+        for c in range(3):
+            s0, c8, go = 1152 * c, vw("of1", 8 * c, 8 * c + 8), "GO%d" % c
+            tt(c8, vw("SC", s0 + 15, s0 + 1024, 144), full("gc", 8), OP.add)
+            ts(vw("OC", 8 * c, 8 * c + 8), c8, 0.03125, None, OP.mult)
+            cp(full(go), ind(vw(ctn, cta, cta + 256), "OC", 8 * c, 8 * c + 8), "VS")
+            scan(vw("CO", 128 * c, 128 * c + 128), full(go), full("MC"), 0.0, OP.min, OP.add)
+            scan(vw("DS", 8 * c, 8 * c + 8), full("r64", 8), vw("CO", 128 * c + 15, 128 * c + 128, 16), -1.0, OP.mult, OP.max)
+        ts(full("AM", 32), ind(full("DS", 24), "R1", 0, 2), 64.0, 32.0, OP.min, OP.add)
+        for q, ds in (("Y", [1, 2, 3, 4]), ("S", [5, 6, 7])):
+            def turn(ds=ds):
+                r = []
+                for d in ds:
+                    a, b = 32 + 3 * d, 35 + 3 * d
+                    r += [(T.AM[16 * d:128, a:b], T.AM[0:128 - 16 * d, 3 * d:3 * d + 3]), (T.AM[0:16 * d, a:b], T.AM[128 - 16 * d:128, 3 * d:3 * d + 3])]
+                return r
+            ld(q, turn, [full("AM", 32)], [vw("AM", 32 + 3 * d, 35 + 3 * d) for d in ds], 2 * len(ds))
+        cp(full("L", 32), ind(full("AM", 64), "R2", 0, 2))
+
+        lall = ("L", 0, 22)
+        cp(full("jk", 352), ind(full("WN", 112), *lall), "S", acc=vw("cnt", 0))
+        cp(vw("cnI", 0), vw("cnt", 0))
+        ts(vw("rem", 0), vw("cnI", 0), 1023, None, OP.bitwise_and)
+        wn = "w_%d" % t
+        ts(vw(wn, 0), vw("rem", 0), 0.0, vw("nV", 0), OP.is_gt, OP.mult)
+        ts(vw(wn, 1), vw("cnt", 0), 1024.0, vw("nV", 1), OP.is_ge, OP.mult)
+        fland, fw = "fdr%d" % t if t < 2 else "fw2", "fw%d" % t
+        send(two(fland), two(wn), "rf%d" % t, boost=5.0)
+
+        tv = "TV%d" % t
+        for c in range(3):
+            n, j = NV[c], 128 * c
+            for k in range(4):
+                z, b = vw("ZS", 512 * c + k, 512 * c + 4 * n, 4), 512 * (k % 2)
+                pick = ind(vw(tv, PW * k, PW * k + CAME), "L", 8 * c, 8 * c + n // 16)
+                if k < NF: tt(z, pick, vw("FP", 384 * k + j, 384 * k + j + n), OP.add)
+                else:
+                    tg = vw("TG", 384 * (k - NF) + j, 384 * (k - NF) + j + n)
+                    mm("psF", b, "EQ", 128 * k, "QX", j)
+                    cp(tg, pick, "S")
+                    tt(z, vw("psF", b, b + n), tg, OP.add)
+                cp(vw("ZP", 384 * k + j, 384 * k + j + n), z, "S", 64.0)
+            quant("QZ", j, "ZS", 512 * c)
+            for k in range(4):
+                mm("psR", 512 * k, "WC", 128 * k, "QZ", j)
+                tt(vw("XT", 512 * c + k, 512 * c + 4 * n, 4), vw("psR", 512 * k, 512 * k + n), vw("ZP", 384 * k + j, 384 * k + j + n), OP.add)
+
+        tt(full("MV", 352), ind(full("WM", 112), *lall), full("wt", 352), OP.mult)
+        for nm, op, sg, s in (("mxa", OP.max, -1.0, 0), ("mxb", OP.min, 1.0, 1)):
+            add({"V": 352 * CYC}, {"V": lambda nm=nm, op=op: g.vector.tensor_reduce(ap(vw(nm, 0)), T.MV[:], AxisListType.X, op)}, [full("MV", 352)], [vw(nm, 0)])
+            ts(vw("CL", s), vw(nm, 0), sg, 352.0, OP.mult, OP.add)
+        for k in range(4): cp(vw("CLT", k, 128, 4), ind(vw("ZP", 384 * k, 384 * k + 384), "CL", 0, 2), "S")
+        cq, la = "CQ%d" % t, (0, 128, 160)[t]
+        quant(cq, 0, "CLT", 0)
+        send(vw("LC", la, la + 32) + ("c",), vw(cq, 0, 32) + ("c",), "rc%d" % t)
+        send(vw("LCs", la, la + 32), vw(cq + "s", 0, 32), "rc%d" % t)
+
+        if t < 2: ld("Y", lambda fw=fw, fl=fland: [(T[fw][:], T[fl][:])], [two(fland)], [two(fw)])
+        ts(two("ua"), two(fw), 0.0, float(CAME), OP.is_lt, OP.mult)
+        tt(two("uk"), two("ua"), two(EST[t]), OP.min)
+        tt(two("uf"), two("uk"), two("nW"), OP.add)
+        tt(two(EST[t + 1]), two(EST[t]), two("uk"), OP.subtract)
+        if t < 2: cp(two("UL"), two("uf"))
+        else:
+            for s in range(2): cp(vw("UL3", 2 * s), vw("uf", s))
+        lv, off = ((0, 0), (32, 96), (64, 96))[t]
+        for k in range(4):
+            b = 512 * (k % 2)
+            mm("psF", b, "EQ", 128 * k, "LC", lv)
+            cp(vw(tv, PW * k + CAME, PW * k + CAME + 32), vw("psF", b + off, b + off + 32), "S", -1.0)
+            win = vw(tv, PW * k, PW * k + CAME + 32)
+            if t < 2: cp(vw("TV%d" % (t + 1), PW * k, PW * k + 32), ind(win, "UL", 0, 2), "S")
+            else:
+                for s in range(2): cp(vw("RT", 4 * s + k, 128, 8), ind(win, "UL3", 2 * s, 2 * s + 1), "S", -64.0)
+
+    cp(full("BPO", 352), ind(full("MB", 112), "L", 0, 22), "S")
+    ld("Y", lambda: [(T.bp[:, 0:352], T.BPO[0:128:16, :])], [full("BPO", 352)], [])
+    ts(two("FO"), two(EST[3]), 0.0, None, OP.is_equal)
+    ld("Y", lambda: [(T.bp[:, 352:384], T.FO[:])], [two("FO")], [])
+    ld("Y", lambda: [(T.rt[:], T.RT[:])], [full("RT")], [])
+    for c in range(3):
+        n, j, b = NV[c], 128 * c, 512 * (c % 2)
+        quant("QX", j, "XT", 512 * c)
+        mm("psS", b, "QV", 0, "QX", j)
+        cp(vw("YO", j, j + n), vw("psS", b, b + n))
+        ld("Y", lambda j=j, n=n: [(T.y[:, j:j + n], T.YO[:, j:j + n])], [vw("YO", j, j + n)], [])
+        ld("S", lambda j=j, n=n: [(T.oc[:, 4 * j:4 * j + 4 * n], T.QX[:, j:j + n].bitcast(dt.uint8))], [vw("QX", j, j + n)], [])
+    ld("S", lambda: [(T.osc[4 * k:4 * k + 4, :], T.QXs[32 * k:32 * k + 4, 0:352]) for k in range(4)], [full("QXs", 352)], [], 4)
+    return ops
+
+
+def rank_program(g, core, T, topo):
+    rank = T.rank_of(core)
+    if rank is None: return
+    ops = build(g, core, T, topo, T.cores[(rank + 1) % len(T.cores)])
+    if "o" not in PLAN: PLAN["o"] = plan(ops)
+    order, deps, _ = PLAN["o"]
+    eng = {"V": g.vector, "S": g.scalar, "T": g.tensor, "G": g, "Y": g.sync}
+    cnt, done, snap, know, nd = {}, {}, {}, {q: {} for q in eng}, 0
+    for k, q, _ in order:
+        o, kn = ops[k], know[q]
+        for (s, v), d in sorted(((done[d], d) for d in deps[k]), key=lambda x: -x[0][1]):
+            if kn.get(s, 0) < v:
+                eng[q].wait_ge(T.sem[s], v)
+                for s2, v2 in list(snap[d].items()) + [(s, v)]: kn[s2] = max(kn.get(s2, 0), v2)
+        r = o["fn"][q]()
+        if o["kind"] == "c":
+            s = "s" + q
+            cnt[s] = cnt.get(s, 0) + 1
+            r.then_inc(T.sem[s], 1)
+        elif o["kind"] == "d":
+            s = "d%d" % nd
+            nd += 1
+            for i in (r if isinstance(r, list) else [r]): i.then_inc(T.sem[s], 16)
+            cnt[s] = 16 * o["nd"]
+        else:
+            s, ne = o["nd"]
+            cnt[s] = cnt.get(s, 0) + ne
+            cnt["sent"] = cnt.get("sent", 0) + ne
+        done[k] = (s, cnt[s])
+        snap[k] = dict(kn) if o["kind"] != "n" else {}
+    for s in sorted(cnt):
+        if know["G"].get(s, 0) < cnt[s]: g.wait_ge(T.sem[s], cnt[s])

@@ -1,48 +1,51 @@
-from concourse.bass import IndirectOffsetOnAxis
-from concourse.mybir import dt, AluOpType as OP, AxisListType, ActivationFunctionType
+from concourse.mybir import dt, AluOpType as OP, ActivationFunctionType as AF
 
-COPY = ActivationFunctionType.Copy
-NV = [128, 128, 96]
-PW, CAME = 160, 112
-NF = 2
-SMALL = {"KI": "pI1 iI1 gI1 c5I1 m7I1 cnI1 rem1 nI2 la2 lb2 lc2 ld2 le2 lf2 ma2 mb2 mc2 md2 me2 mf2",
-         "KF": "iF1 gF1 c5F1 a5F1 nW2 nV2 kF8 gc8",
-         "KL": "flf2 ua2 uk2 uf2 esta2 estb2 estc2 estd2 mxa1 mxb1 cnt1"}
+COPY = AF.Copy
+C = 352
+CH = [(0, 192), (192, 160)]
+SL = [0, 128, 224]
+PW, CAME = 80, 34
+PS = 1152
+TW = 1104
+SMALL = {"KI": "bI4 pI1 BI8 flI2 fl8_32 g1I2 g2I2 GoI2 Gm2 al2 dI2 dm2 cnI1 rem1",
+         "KF": "BF8 c41_2 c02_2 c10_2 c28_2 c16_2 nW2 u1_2 u2_2 u3_2 k1_1 k2_1 ph1 phi1 be2 bm2 de2 t1_2 e1_2 e2_2 e3_2 e4_2 kF4 cA4 cB4 c01_2",
+         "KL": "oca2 ocb2 occ2 ocd2 tk2 cnt1"}
 ALIAS = {}
 for _b, _s in SMALL.items():
     _k = 0
     for _n in _s.split():
-        ALIAS[_n[:-1]] = (_b, _k)
-        _k += int(_n[-1])
-EST = ["esta", "estb", "estc", "estd"]
+        _m, _w = _n.rsplit("_", 1) if "_" in _n else (_n[:-1], _n[-1])
+        ALIAS[_m] = (_b, _k)
+        _k += int(_w)
+OCC = ["oca", "ocb", "occ", "ocd"]
 
 
 def _scratch():
     f, h, i, u, q, b = "float32", "bfloat16", "int32", "uint16", "float8_e4m3fn_x4", "uint8"
-    s = {"tabd": ("dram", [1, 7424], h), "fdr0": ("dram", [128, 2], h), "fdr1": ("dram", [128, 2], h)}
-    for d, names in ((i, "KI:40 zix:2 tic:64 t32:2048 flI:2"),
-                     (f, "KF:32 KL:32 pF:1 tt:128 dd:128 ge:128 eq:128 qa:128 qb:128 qc:128 qd:128 ix:128 rel:112 wa:112 wb:112 wc1:112 MB:112 wt:352 of1:24 "
-                         "jk:352 MV:352 RT:128 BPO:352 FO:2 YO:384"),
-                     (u, "R1:2 R2:2 UP:8 OF:192 OC:24 L:32 CL:2 UL:2 UL3:4"),
-                     (h, "MS:128 MC:128 hd:128 WM:112 WN:112 r64:8 ET:2048 tib:64 TAB:7424 flc:2 UT:512 VT:512 TT:512 ZT:512 XT:1536 AB:384 SC:3456 GO0:128 GO1:128 GO2:128 "
-                         "CO:384 DS:32 AM:64 FP:768 TG:768 ZS:1536 ZP:1536 TV0:640 TV1:640 TV2:640 CT1:256 CT2:256 CB:256 crow:256 CLT:512 "
-                         "w_0:2 w_1:2 w_2:2 fw0:2 fw1:2 fw2:2")):
+    s = {"fdr0": ("dram", [128, 2], h), "fdr1": ("dram", [128, 2], h)}
+    for d, names in ((i, "KI:80 tic:64"),
+                     (f, "KF:72 KL:16 rr:128 ix:48 wa:48 wb:48 MB:48 SA:352 SB:352 RT:128 BPO:352 YO:352"),
+                     (u, "R1:2 R2:2 PM:2 OF:144 L:32 CL:8 UL:2"),
+                     (h, "hd:128 WJ:48 ET:520 tib:64 tbt:64 TAB:%d STG:32 UT:512 VT:512 TT:512 XT:1408 AB:384 SC:432 GO0:256 GO1:256 O:%d AM:64 TG:1408 "
+                         "ZS:1424 ZP:1408 TV:960 FP:1408 JK:352 one:352 stp:352 CLT:512 w_0:2 w_1:2 w_2:2 fw0:2 fw1:2 fw2:2" % (TW, 2 * PS))):
         for n in names.split():
             n, w = n.split(":")
             s[n] = ("sbuf", [128, int(w)], d)
-    for n in "EQ:512 QU:128 QP:128 QV:128 QT:128 WC:512 QO:128 QX:384 QZ:384 CQ0:128 CQ1:128 CQ2:128 LC:192".split():
+    for n in "EQ:512 QU:128 QV:128 WC:512 QX:352 QZ:352 CQ0:128 CQ1:128 CQ2:128 LC:224".split():
         n, w = n.split(":")
         s[n] = ("sbuf", [128, int(w)], q)
         s[n + "s"] = ("sbuf", [128, int(w)], b)
-    for n, w in (("psS", 1024), ("psF", 1024), ("psR", 2048)):
-        s[n] = ("psum", [128, w], f)
+    s["ps"] = ("psum", [128, 4096], f)
     return s
 
 
 SCRATCH = _scratch()
 SEMAPHORES = ["sV", "sS", "sT", "sG", "sent", "rf0", "rf1", "rf2", "rc0", "rc1", "rc2"] + ["d%d" % k for k in range(60)]
 PLAN = {}
-WAKE, DMALAT, NETLAT, CYC = 0.1, 2.0, 3.0, 0.00083
+TRIES = 3000
+PC = 118
+NF = 2
+WAKE, DMALAT, NETLAT, CYC, PECYC = 0.1, 1.8, 2.5, 0.001, 0.0012
 
 
 def bits(v):
@@ -50,7 +53,7 @@ def bits(v):
     if n in ALIAS:
         n, o = ALIAS[n]
         a, b = a + o, b + o
-    if n[:2] == "ps":
+    if n == "ps":
         a, b, st = a - a % 512, a - a % 512 + 512, 1
     return (n, ((1 << (b - a)) - 1) << a if st == 1 else sum(1 << k for k in range(a, b, st)))
 
@@ -71,24 +74,47 @@ def plan(ops):
     prio = [0.0] * n
     for k in range(n - 1, -1, -1):
         prio[k] = min(ops[k]["dur"].values()) + ops[k]["lat"] + max([prio[j] for j in succ[k]] + [0.0])
-    left = [len(d) for d in deps]
-    ready = {k: 0.0 for k in range(n) if not left[k]}
-    avail, fin, order = {}, [0.0] * n, []
-    while ready:
-        opts = []
-        for k, r in ready.items():
-            end, st, q = min((max(r, avail.get(q, 0.0)) + du, max(r, avail.get(q, 0.0)), q) for q, du in ops[k]["dur"].items())
-            opts.append((st, -prio[k] - ops[k]["boost"], k, q, end))
-        lo = min(opts)[0] + 0.03
-        st, _, k, q, end = min((o for o in opts if o[0] <= lo), key=lambda o: o[1])
-        del ready[k]
-        avail[q] = end
-        fin[k] = end + ops[k]["lat"]
-        order.append((k, q, st))
-        for j in succ[k]:
-            left[j] -= 1
-            if not left[j]: ready[j] = max(fin[i] for i in deps[j])
-    return order, deps, max(fin)
+
+    def place(pr, pref):
+        left = [len(d) for d in deps]
+        ready = {k: 0.0 for k in range(n) if not left[k]}
+        busy, fin, order = {}, [0.0] * n, []
+        while ready:
+            k = max(ready, key=lambda x: pr[x])
+            opts = []
+            for q, du in ops[k]["dur"].items():
+                st, bq = ready[k], busy.setdefault(q, [])
+                i = len(bq)
+                while i and bq[i - 1][1] > st: i -= 1
+                while i < len(bq) and st + du > bq[i][0] + 1e-9:
+                    st = max(st, bq[i][1])
+                    i += 1
+                opts.append((st + du + (pref[k] if q == "V" else 0.0), st, q, i))
+            _, st, q, i = min(opts)
+            del ready[k]
+            busy[q].insert(i, (st, st + ops[k]["dur"][q]))
+            fin[k] = st + ops[k]["dur"][q] + ops[k]["lat"]
+            order.append((k, q, st))
+            for j in succ[k]:
+                left[j] -= 1
+                if not left[j]: ready[j] = max(fin[x] for x in deps[j])
+        return max(fin) + 1e-4 * sum(fin) / n, sorted(order, key=lambda o: o[2])
+
+    seed = [12345]
+    def rnd():
+        seed[0] = (seed[0] * 1103515245 + 12345) % 2147483648
+        return seed[0] / 2147483648.0
+    pr, pref = [prio[k] + ops[k]["boost"] - 1e-6 * k for k in range(n)], [0.0] * n
+    best = place(pr, pref)
+    for it in range(TRIES):
+        p2, f2 = list(pr), list(pref)
+        for _ in range(1 + int(rnd() * 12)):
+            k = int(rnd() * n)
+            p2[k] += (rnd() - 0.5) * (4.0 if rnd() < 0.3 else 1.0)
+            if len(ops[k]["dur"]) > 1: f2[k] = (rnd() - 0.5) * 0.8
+        r = place(p2, f2)
+        if r[0] <= best[0]: best, pr, pref = r, p2, f2
+    return best[1], deps, best[0]
 
 
 def build(g, core, T, topo, nxt):
@@ -113,62 +139,67 @@ def build(g, core, T, topo, nxt):
         R = [v[:4] for v in ins] + [v[4][:4] for v in ins if len(v) > 4 and v[4] != "c"]
         ops.append({"dur": dur, "fn": fn, "R": R, "W": [v[:4] for v in outs], "lat": lat, "kind": kind, "nd": nd, "boost": boost})
 
+    def wide(*vs):
+        return any(SCRATCH[ALIAS.get(v[0], v)[0]][2] in ("float32", "int32") for v in vs)
+
+    def num(v):
+        return len(range(v[1], v[2], v[3]))
+
     def cost(v, k):
-        n = len(range(v[1], v[2], v[3]))
-        return n, max(64, n * k) * CYC
+        return max(64, num(v) * k) * CYC
 
-    def isind(*vs):
-        return any(len(v) > 4 and v[4] != "c" for v in vs)
+    def isind(v):
+        return len(v) > 4 and v[4] != "c"
 
-    def ts(out, in0, s1, s2, op0, op1=None):
-        n, d = cost(out, 1.0)
+    def gat(v, c):
+        return c + num(v) * 1.5 * CYC
+
+    def ts(out, in0, s1, s2, op0, op1=None, boost=0.0):
         sc = [s for s in (s1, s2) if isinstance(s, tuple)]
-        if isind(in0): d = 0.05 + n * 1.5 * CYC
+        d = gat(out, 0.05) if isind(in0) else cost(out, 1.0 if wide(out, in0) else 0.5)
         val = lambda s: ap(s) if isinstance(s, tuple) else s
         if op1 is None: fn = lambda: g.vector.tensor_scalar(ap(out), ap(in0), val(s1), None, op0)
         else: fn = lambda: g.vector.tensor_scalar(ap(out), ap(in0), val(s1), val(s2), op0, op1)
-        add({"V": d}, {"V": fn}, [in0] + sc, [out])
+        add({"V": d}, {"V": fn}, [in0] + sc, [out], boost=boost)
 
     def tt(out, a, b, op):
-        n, d = cost(out, 1.0 if a[0][:2] == "ps" else 2.0)
-        if isind(a): d = 0.05 + n * 1.5 * CYC
+        d = gat(out, 0.05) if isind(a) else cost(out, 1.0 if a[0] == "ps" else 2.0)
         add({"V": d}, {"V": lambda: g.vector.tensor_tensor(ap(out), ap(a), ap(b), op)}, [a, b], [out])
 
-    def cp(out, a, q="V", scale=1.0, acc=None):
-        n, d = cost(out, 1.0)
+    def cp(out, a, q="V", scale=1.0, acc=None, boost=0.0):
         i = isind(a)
-        kw = {}
-        if scale != 1.0: kw["scale"] = scale
-        fns = {"V": lambda: g.vector.tensor_copy(ap(out), ap(a)),
-               "S": lambda: g.scalar.activation(ap(out), ap(a), COPY, accum_out=ap(acc)) if acc else g.scalar.activation(ap(out), ap(a), COPY, **kw)}
-        durs = {"V": 0.05 + n * 1.5 * CYC if i else d, "S": 0.065 + n * 1.5 * CYC if i else d}
-        add({k: durs[k] for k in q}, {k: fns[k] for k in q}, [a], [out] + ([acc] if acc else []))
+        kw = {"scale": scale} if scale != 1.0 else {}
+        if acc: kw["accum_out"] = acc
+        fns = {"V": lambda: g.vector.tensor_copy(ap(out), ap(a)) if scale == 1.0 else g.vector.tensor_scalar(ap(out), ap(a), scale, None, OP.mult),
+               "S": lambda: g.scalar.activation(ap(out), ap(a), COPY, **{k: ap(x) if k == "accum_out" else x for k, x in kw.items()})}
+        durs = {"V": gat(out, 0.05) if i else cost(out, 1.0 if wide(out, a) else 0.5), "S": (gat(out, 0.065) if i else cost(out, 1.0)) + (0.02 if acc else 0.0)}
+        add({k: durs[k] for k in q}, {k: fns[k] for k in q}, [a], [out] + ([acc] if acc else []), boost=boost)
 
     def scan(out, d0, d1, init, op0, op1):
-        add({"V": cost(out, 0.5)[1]}, {"V": lambda: g.vector.tensor_tensor_scan(ap(out), ap(d0), ap(d1), init, op0, op1)}, [d0, d1], [out])
+        add({"V": cost(out, 1.0 if wide(out, d0, d1) else 0.5)}, {"V": lambda: g.vector.tensor_tensor_scan(ap(out), ap(d0), ap(d1), ap(init) if isinstance(init, tuple) else init, op0, op1)},
+            [d0, d1] + ([init] if isinstance(init, tuple) else []), [out])
 
-    def fill(out, val):
-        add({"V": cost(out, 0.5)[1]}, {"V": lambda: g.vector.memset(ap(out), val)}, [], [out])
+    def turn32(out, a):
+        add({"V": cost(out, 0.5)}, {"V": lambda: g.vector.transpose(ap(out), ap(a))}, [a], [out])
+
+    def fill(out, val, boost=0.0):
+        add({"V": cost(out, 1.0 if wide(out) else 0.5)}, {"V": lambda: g.vector.memset(ap(out), val)}, [], [out], boost=boost)
 
     def quant(q, a, t, ta, n=128):
         c, s, i = vw(q, a, a + n), vw(q + "s", a, a + n), vw(t, ta, ta + 4 * n)
-        add({"V": 0.012 + 0.88e-3 * n}, {"V": lambda: g.vector.quantize_mx(ap(c), ap(s), ap(i))}, [i], [c, s])
+        add({"V": 0.015 + 1.05e-3 * n}, {"V": lambda: g.vector.quantize_mx(ap(c), ap(s), ap(i))}, [i], [c, s])
 
-    def mm(ps, pa, lq, la, rq, ra, n=128):
-        o = vw(ps, pa, pa + n)
+    def mm(bank, lq, la, rq, ra, n=128):
+        o = vw("ps", 512 * bank, 512 * bank + n)
         i = [vw(lq, la, la + 128), vw(lq + "s", la, la + 128), vw(rq, ra, ra + n), vw(rq + "s", ra, ra + n)]
-        add({"T": (n + 16) * 0.00085}, {"T": lambda: g.tensor.matmul_mx(ap(o), ap(i[0]), ap(i[1]), ap(i[2]), ap(i[3]), True, True)}, i, [o])
+        add({"T": (n + 16) * PECYC}, {"T": lambda: g.tensor.matmul_mx(ap(o), ap(i[0]), ap(i[1]), ap(i[2]), ap(i[3]), True, True)}, i, [o])
 
-    def iota(out, pattern, base, cm, small=True):
-        kw = {"allow_small_or_imprecise_dtypes": True} if small else {}
-        add({"G": 0.13 + cost(out, 2.0)[0] * 2 * CYC}, {"G": lambda: g.iota(ap(out), pattern, base, cm, **kw)}, [], [out])
+    def iota(out, pattern, base, cm, boost=0.0):
+        kw = {} if SCRATCH[ALIAS.get(out[0], out)[0]][2] == "int32" else {"allow_small_or_imprecise_dtypes": True}
+        add({"G": 0.15 + num(out) * 2 * CYC}, {"G": lambda: g.iota(ap(out), pattern, base, cm, **kw)}, [], [out], boost=boost)
 
-    def ld(q, pairs, ins, outs, nd=1, boost=0.0):
-        add({q: 0.06 * nd}, {q: lambda: [(g.sync if q == "Y" else g.scalar).dma_start(o, i) for o, i in pairs()]}, ins, outs, DMALAT, "d", nd, boost)
-
-    def rows(out, src, dep, col, last, lat, boost=0.0):
-        ix = vw("zix", col)
-        add({"G": 1.7}, {"G": lambda: g.indirect_dma_start(ap(out), None, T[src][:], IndirectOffsetOnAxis(ap=ap(ix), axis=0), bounds_check=last)}, [ix] + dep, [out], lat, "d", 1, boost)
+    def ld(q, pairs, ins, outs, nd=1, boost=0.0, lat=DMALAT):
+        add({q: 0.06 * nd}, {q: lambda: [(g.sync if q == "Y" else g.scalar).dma_start(o, i) for o, i in pairs()]}, ins, outs, lat, "d", nd, boost)
 
     def send(out, in_, sem, boost=0.0):
         ne = 8 if T is None else len(topo.engines(core, nxt))
@@ -177,220 +208,211 @@ def build(g, core, T, topo, nxt):
             g.remote_dma(ap(out) if out[0][:3] != "fdr" else T[out[0]][:], ap(in_), T.sem[sem], T.sem.sent, pid, rid, topo.mask(core, nxt))
         add({"G": 0.3}, {"G": fn}, [in_], [out], NETLAT, "n", (sem, ne), boost)
 
-    iota(vw("zix", 0, 2), [[1, 2]], 0, 0, False)
-    iota(vw("pI", 0), [[0, 1]], 0, 1, False)
-    ld("Y", lambda: [(T.tic[0:112, :], T.ti[:])], [], [vw("tic", 0, 64)], boost=50.0)
-    ld("S", lambda: [(T.UT[:], T.u[:])], [], [vw("UT", 0, 512)], boost=40.0)
-    for c in range(3):
-        v = vw("XT", 512 * c, 512 * c + 4 * NV[c])
-        ld("YSY"[c], lambda v=v: [(ap(v), T.x[:, v[1]:v[2]])], [], [v], boost=45.0 - c)
-    ld("S", lambda: [(T.flI[:], T.fl[:])], [], [vw("flI", 0, 2)], boost=38.0)
-    for l in range(2): rows(vw("t32", 1024 * l, 1024 * l + 1024), "ti", [], l, 6, 3.5, boost=50.0)
-    for o, i, s, op in (("iI", "pI", 15, OP.bitwise_and), ("gI", "pI", 4, OP.arith_shift_right), ("a5F", "pI", 5.0, OP.add)):
-        ts(vw(o, 0), vw(i, 0), s, None, op)
-    cp(vw("c5I", 0), vw("a5F", 0))
-    ts(vw("m7I", 0), vw("c5I", 0), 15, None, OP.bitwise_and)
-    for o, i in (("pF", "pI"), ("iF", "iI"), ("gF", "gI"), ("c5F", "m7I")): cp(vw(o, 0), vw(i, 0))
-    iota(vw("kF", 0, 8), [[16, 8]], 0, 0)
-    iota(vw("tt", 0, 128), [[0, 8], [1, 16]], 0, 0)
-    iota(vw("ix", 0, 128), [[1, 128]], 0, 0)
-    iota(vw("gc", 0, 8), [[1024, 8]], -32, 0)
-    iF, gF = vw("iF", 0), vw("gF", 0)
     full = lambda n, w=128: vw(n, 0, w)
-    ts(full("UP", 8), full("kF", 8), vw("c5F", 0), None, OP.add)
-    quant("QU", 0, "UT", 0)
-    for s, d in (("QU", "QP"), ("QUs", "QPs")):
-        fn = (lambda: g.vector.tensor_copy(T.QP[:].bitcast(dt.uint32), T.QU[:].bitcast(dt.uint32).indirect(T.UP[:, 0:8]))) if s == "QU" else \
-             (lambda: g.vector.tensor_copy(T.QPs[:], T.QUs[:].indirect(T.UP[:, 0:8])))
-        add({"V": 0.2}, {"V": fn}, [full(s), full("UP", 8)], [full(d)])
-    ts(full("hd"), full("tt"), 12.0, 2.0, OP.is_ge, OP.mult)
-    add({"V": 0.06}, {"V": lambda: g.vector.tensor_scalar(T.tib[0:112, :], T.tic[0:112, :], 1.0, -1.0, OP.add, OP.mult)}, [full("tic", 64)], [full("tib", 64)])
-    ts(full("nW", 2), full("kF", 2), iF, None, OP.add)
-    ts(full("flf", 2), full("flI", 2), -33.0, -127.0, OP.mult, OP.add)
-    tt(full("flc", 2), full("flf", 2), full("nW", 2), OP.add)
-    ts(full(EST[0], 2), full("flI", 2), 0.0, float(CAME), OP.is_equal, OP.mult)
-    ld("Y", lambda: [(T.tabd[0:1, 0:7168], T.tib[0:112, :])], [full("tib", 64)], [vw("tabd", 0, 7168)])
-    ld("Y", lambda: [(T.tabd[0:1, 7168:7424], T.flc[:])], [full("flc", 2)], [vw("tabd", 7168, 7424)])
-    rows(full("TAB", 7424), "tabd", [full("tabd", 7424)], 0, 0, 5.0)
-    ts(full("dd"), full("tt"), iF, None, OP.subtract)
-    ts(full("ge"), full("dd"), 0.0, None, OP.is_ge)
-    ts(full("qa"), full("dd"), 0.0, 31.0, OP.is_equal, OP.mult)
-    tt(full("qb"), full("ge"), full("qa"), OP.add)
-    ts(vw("eq", 0, 16), vw("tt", 0, 16), 15.0, -2.0, OP.is_equal, OP.mult)
-    ts(vw("eq", 16, 128), vw("tt", 16, 128), 15.0, -33.0 / 32.0, OP.is_equal, OP.mult)
-    ts(full("qc"), full("eq"), 1.0, None, OP.add)
-    tt(full("MS"), full("qb"), full("qc"), OP.mult)
-    fill(full("ET", 2048), 0.0)
-    for k in range(4):
-        ts(vw("ET", 513 * k, 512 * k + 512, 4), full("ix"), vw("pF", 0), 0.015625, OP.is_equal, OP.mult)
-        quant("EQ", 128 * k, "ET", 512 * k)
-    ts(full("qa"), full("ge"), -128.0, 128.0, OP.mult, OP.add)
-    ts(full("qb"), full("dd"), 0.0, -64.0, OP.is_equal, OP.mult)
-    ts(full("qc"), full("tt"), 15.0, 192.0, OP.is_equal, OP.mult)
-    tt(full("qd"), full("qa"), full("qb"), OP.add)
-    tt(full("MC"), full("qd"), full("qc"), OP.add)
-    fill(full("r64", 8), 64.0)
-    fill(full("AM", 64), 0.0)
-    fill(vw("XT", 1408, 1536), 0.0)
-    fill(vw("ZS", 1408, 1536), 0.0)
-    for k in range(4): fill(vw("ZP", 384 * k + 352, 384 * k + 384), 0.0)
-    fill(vw("TT", 128, 512), 0.0)
-    ld("S", lambda: [(T.TT[:, 0:128], T.tr[:])], [], [full("TT")], boost=20.0)
-    quant("QT", 0, "TT", 0)
-    for t in range(3): fill(full("TV%d" % t, 640), 0.0)
-    for k in range(4):
-        b = 512 * (k % 2)
-        mm("psF", b, "EQ", 128 * k, "QT", 0)
-        for s in range(2): cp(vw("TV0", PW * k + 16 * s, PW * k + 16 * s + 16), vw("psF", b + s, b + 32, 2), "S", -1.0)
     two = lambda n: vw(n, 0, 2)
-    cp(two("nI"), two("nW"))
-    for o, i, s, s2, op, op2 in (("la", "nI", 11.0, None, OP.mult, None), ("lb", "la", 5, None, OP.arith_shift_right, None), ("lc", "lb", -24.0, None, OP.mult, None),
-                                 ("ld", "lb", gF, None, OP.add, None), ("le", "ld", 7, None, OP.bitwise_and, None), ("lf", "nI", 8.0, None, OP.mult, None)):
-        ts(two(o), two(i), s, s2, op, op2)
-    tt(two("la"), two("lc"), two("lf"), OP.add)
-    tt(two("ld"), two("la"), two("le"), OP.add)
-    cp(two("R1"), two("ld"))
-    for o, i, s, s2, op, op2 in (("ma", "nI", 3, None, OP.arith_shift_right, None), ("mb", "nI", 7, None, OP.bitwise_and, None), ("mc", "mb", -1.0, gF, OP.mult, OP.add),
-                                 ("md", "mc", 8.0, None, OP.add, None), ("me", "md", 7, None, OP.bitwise_and, None), ("mf", "me", 0.0, 32.0, OP.is_gt, OP.mult),
-                                 ("mb", "me", 3.0, None, OP.mult, None)):
-        ts(two(o), two(i), s, s2, op, op2)
-    tt(two("mc"), two("mb"), two("ma"), OP.add)
-    tt(two("md"), two("mc"), two("mf"), OP.add)
-    cp(two("R2"), two("md"))
-    ts(full("rel", 112), full("ix", 112), iF, -33.0, OP.subtract, OP.add)
-    ts(full("wa", 112), full("rel", 112), 0.0, None, OP.is_equal)
-    ts(full("wb", 112), full("rel", 112), 16.0, None, OP.is_equal)
-    ts(full("wc1", 112), full("rel", 112), 16.0, 1024.0, OP.is_equal, OP.mult)
-    tt(full("WM", 112), full("wa", 112), full("wb", 112), OP.subtract)
-    tt(full("WN", 112), full("wa", 112), full("wc1", 112), OP.add)
-    iota(full("wt", 352), [[-1, 352]], 352, 0)
-    ts(two("nV"), two("nW"), -160.0, None, OP.add)
+    one = lambda n: vw(n, 0)
+
+    ld("Y", lambda: [(T.tic[:, 0:32], T.ti[0:4, :]), (T.tic[:, 32:64], T.ti[3:7, :])], [], [full("tic", 64)], 2, boost=50.0)
+    f8 = ALIAS["fl8"][1]
+    ld("Y", lambda: [(T.KI[0:8, f8:f8 + 32], T.fl[:])], [], [full("fl8", 32)], boost=49.0)
+    for c, (j, n) in enumerate(CH):
+        v = vw("XT", 4 * j, 4 * j + 4 * n)
+        ld("S", lambda v=v: [(ap(v), T.x[:, v[1]:v[2]])], [], [v], boost=45.0 - 2 * c)
+    ld("S", lambda: [(T.UT[:], T.u[:])], [], [full("UT", 512)], boost=44.0)
+    fill(full("TAB", TW), 33.0, boost=50.0)
+    iota(full("TAB", 33), [[1, 33]], 0, 0, boost=50.0)
+    ts(full("tib", 64), full("tic", 64), 1.0, None, OP.add)
+    turn32(full("tbt", 64), full("tib", 64))
+    add({"V": 64 * CYC}, {"V": lambda: g.vector.tensor_scalar(T.TAB[0:7, 1:33], T.KI[0:7, f8:f8 + 32], -33.0, 33.0, OP.mult, OP.add)}, [full("fl8", 32)], [vw("TAB", 1, 33)])
+    ld("Y", lambda: [(T.TAB[0:4, 33:1057], T.tbt[:, 0:32]), (T.TAB[4:7, 33:1057], T.tbt[32:128, 32:64])], [full("tbt", 64)], [vw("TAB", 32, 1057)], 2)
+    ld("Y", lambda: [(T.TAB[16 * k:16 * k + 7, 0:1057], T.TAB[0:7, 0:1057]) for k in range(1, 8)], [], [full("TAB", 1072)], 7)
+    late = [vw("TAB", 1060)]
+    ld("S", lambda: [(ap(vw("flI", s)), T.fl[:, 16 * s:16 * s + 16]) for s in range(2)], [], [two("flI")], 2)
+    fill(vw("TT", 128, 512), 0.0)
+    ld("S", lambda: [(T.TT[:, 0:128], T.tr[:])], [], [full("TT")])
+    ld("Y", lambda: [(T.WC[:].bitcast(dt.uint8), T.wc[:]), (T.WCs[:], T.ws[:])], late, [full("WC", 512), full("WCs", 512)], 2)
+    ld("Y", lambda: [(T.VT[:], T.v[:])], late, [full("VT", 512)])
+
+    quant("QU", 0, "UT", 0)
+    iota(full("rr"), [[0, 8], [1, 16]], 0, 0, boost=30.0)
+    ts(full("hd"), full("rr"), 4.0, 2.0, OP.is_lt, OP.mult)
+    fill(vw("hd", 4, 128, 16), 16.0)
+    fill(vw("hd", 4), 0.5)
+    fill(vw("SC", 132, 432, 144), -528.0)
+    fill(full("OF", 144), 0)
+    for k, m in enumerate((16, 8, 2, 1)): iota(vw("bI", k), [[0, 1]], 0, m)
+    ts(vw("BI", 0, 4), vw("bI", 0, 4), 4, 1, OP.arith_shift_right, OP.bitwise_and)
+    ts(vw("BI", 4), vw("bI", 3), 2, 3, OP.arith_shift_right, OP.bitwise_and)
+    ts(vw("BI", 5), vw("bI", 3), 4, None, OP.arith_shift_right)
+    ts(vw("BI", 6), vw("bI", 3), 15, None, OP.bitwise_and)
+    cp(vw("BF", 0, 7), vw("BI", 0, 7))
+    sg, pr, i3, g0, ih, gF, iF = [vw("BF", k) for k in range(7)]
+    for n, st, b in (("c41", 4, 1), ("c02", 2, 0), ("c10", -1, 1), ("c28", 2, 28), ("c16", 16, 1), ("c01", 1, 0)): iota(two(n), [[st, 2]], b, 0)
+    ts(two("nW"), two("c16"), iF, None, OP.add)
+    ts(two("PM"), two("c01"), iF, iF, OP.add, OP.add)
+    ts(two("g1I"), two("c41"), ih, gF, OP.add, OP.add)
+    ts(two("g2I"), two("g1I"), 7, None, OP.bitwise_and)
+    ts(two("u1"), two("g2I"), -1.0, 16.0, OP.mult, OP.add)
+    ts(two("u2"), two("g2I"), 1.0, 16.0, OP.add, OP.mult)
+    tt(two("u3"), two("u1"), two("u2"), OP.mult)
+    ts(one("k1"), pr, float(PS), -25.0, OP.mult, OP.add)
+    ts(one("k2"), sg, 16.0, one("k1"), OP.mult, OP.add)
+    ts(two("R1"), two("u3"), one("k2"), None, OP.add)
+    ts(two("GoI"), two("c02"), iF, None, OP.add)
+    ts(two("Gm"), two("GoI"), 7, None, OP.bitwise_and)
+    ts(two("al"), two("GoI"), 1, None, OP.bitwise_and)
+    ts(two("be"), two("c10"), i3, None, OP.mult)
+    ts(one("ph"), gF, 7.0, g0, OP.is_equal, OP.subtract)
+    ts(one("phi"), one("ph"), 1.0, None, OP.add)
+    tt(two("bm"), two("be"), two("al"), OP.subtract)
+    ts(two("de"), two("bm"), one("phi"), None, OP.mult)
+    tt(two("t1"), two("de"), two("Gm"), OP.add)
+    ts(two("dI"), two("t1"), -1.0, gF, OP.mult, OP.add)
+    ts(two("dm"), two("dI"), 7, None, OP.bitwise_and)
+    tt(two("e1"), two("be"), two("de"), OP.subtract)
+    tt(two("e2"), two("e1"), two("c28"), OP.add)
+    ts(two("e3"), two("dm"), 4.0, None, OP.mult)
+    tt(two("e4"), two("e3"), two("e2"), OP.add)
+    cp(two("R2"), two("e4"))
+    for p in range(2): iota(vw("O", PS * p + 1120, PS * p + 1152), [[0, 32]], 0, 0)
+    iota(vw("AM", 60, 64), [[0, 4]], 0, 0)
+    iota(full("STG", 32), [[0, 32]], 1, 0)
+    fill(full("ET", 520), 0.0)
+    add({"G": 0.2 + 1040 * CYC}, {"G": lambda: g.affine_select(T.ET[:], T.ET[:], [[1, 520]], OP.not_equal, 0.015625, -3, -4)}, [], [full("ET", 520)])
+    for k in range(4): quant("EQ", 128 * k, "ET", 3 - k)
+    for a in (0, 33): fill(vw("TV", a, 960, PW), 0.0)
+    quant("LC", 32, "TT", 0)
+    for k in range(4):
+        mm(4 + k, "EQ", 128 * k, "LC", 32)
+        cp(vw("TV", PW * k + 1, PW * k + 33), vw("ps", 512 * (4 + k), 512 * (4 + k) + 32), "S", -1.0)
+    cp(two(OCC[0]), two("flI"))
+    iota(full("ix", 48), [[1, 48]], 0, 0)
+    ts(full("wa", 48), full("ix", 48), vw("nW", 0), 512.0, OP.is_equal, OP.mult)
+    ts(full("wb", 48), full("ix", 48), vw("nW", 1), None, OP.is_equal)
+    tt(full("WJ", 48), full("wa", 48), full("wb", 48), OP.subtract)
+    iota(full("one", C), [[0, C]], 1, 0)
+    fill(full("stp", C), -1.0 / 512)
+    iota(full("kF", 4), [[1, 4]], 3456, 0)
+    ts(full("cA", 4), full("kF", 4), -0.25, None, OP.mult)
+    ts(full("cB", 4), full("kF", 4), 1.0 / 2048, None, OP.mult)
+    fill(vw("ZS", 1408, 1424), 0.0)
     fill(vw("CLT", 128, 512), 0.0)
-    fill(full("ZT", 512), 0.0)
-    quant("QO", 0, "ZT", 0)
-    ld("Y", lambda: [(T.LC[:, 32:128].bitcast(dt.uint8), T.QO[:, 0:96].bitcast(dt.uint8))], [full("QO", 96)], [vw("LC", 32, 128)])
-    ld("Y", lambda: [(T.LCs[:, 32:128], T.QOs[:, 0:96])], [full("QOs", 96)], [vw("LCs", 32, 128)])
-    ld("Y", lambda: [(T.WC[:].bitcast(dt.uint8), T.wc[:])], [], [full("WC", 512)])
-    ld("S", lambda: [(T.WCs[:], T.ws[:])], [], [full("WCs", 512)])
-    fill(full("MB", 112), -1.0)
-    for a in (0, 33): iota(vw("MB", a, a + 32), [[1, 2], [2, 16]], 0, 0)
-    ld("S", lambda: [(T.VT[:], T.v[:])], [], [full("VT", 512)])
+    iota(full("MB", 33), [[1, 33]], -1, 0)
+    iota(vw("MB", 33), [[0, 1]], -1, 0)
     quant("QV", 0, "VT", 0)
 
-    ctn, cta = "TAB", 7168
+    def came(t):
+        fw, tv = "fw%d" % t, 4 * PW * t
+        if t < 2: ld("Y", lambda: [(T[fw][:], T["fdr%d" % t][:])], [two("fdr%d" % t)], [two(fw)])
+        tt(two(OCC[t + 1]), two(fw), two(OCC[t]), OP.is_le)
+        tt(two("tk"), two(OCC[t + 1]), two(OCC[t]), OP.subtract)
+        for s in range(2): ts(vw("UL", s), vw("tk", s), CAME - 1.0, vw("nW", s), OP.mult, OP.add)
+        lv, off = ((0, 0), (64, 96), (96, 96))[t]
+        for k in range(4):
+            b = 512 * (4 + k) + off
+            mm(4 + k, "EQ", 128 * k, "LC", lv)
+            cp(vw("TV", tv + PW * k + CAME, tv + PW * k + CAME + 32), vw("ps", b, b + 32), "S", -1.0)
+            win = ind(vw("TV", tv + PW * k, tv + PW * k + CAME + 32), "UL", 0, 2)
+            if t < 2: cp(vw("TV", tv + PW * (k + 4) + 1, tv + PW * (k + 4) + 33), win, "VS")
+            else: cp(vw("RT", k, 128, 4), win, "VS", -64.0)
+
     for t in range(3):
+        for j, n in CH: quant("QX", j, "XT", 4 * j, n)
         for c in range(3):
-            quant("QX", 128 * c, "XT", 512 * c)
-            b, s0 = 512 * (c % 2), 1152 * c
-            mm("psS", b, "QX", 128 * c, "QP", 0)
-            ab = vw("AB", 128 * c, 128 * c + 128)
-            ts(ab, vw("psS", b, b + 128), 0.0, None, OP.is_gt)
-            scan(vw("SC", s0, s0 + 128), full("hd"), ab, 0.0, OP.mult, OP.add)
-            ts(vw("SC", s0 + 15), vw("SC", s0 + 15), 32.0, 32.0, OP.mult, OP.add)
-        for l in range(7):
-            for c in range(3):
-                s0, n, o0, go = 1152 * c, 7 - l, 64 * c + 8 * l, "GO%d" % c
-                ts(vw("OF", o0, o0 + n), vw("SC", s0 + 144 * l + 31, s0 + 128 * l + 128, 16), vw("SC", s0 + 144 * l + 15), -32.0 if l == 0 else -33.0, OP.add, OP.add)
-                gout = full(go, 16 * n)
-                if t == 0 and l < 2: ts(gout, ind(vw("t32", 1024 * l, 1024 * l + 1024), "OF", o0, o0 + n), 1.0, -1.0, OP.add, OP.mult)
-                else: cp(gout, ind(vw("TAB", 1024 * l, 1024 * l + 1024), "OF", o0, o0 + n), "VS")
-                scan(vw("SC", s0 + 144 * (l + 1), s0 + 128 * (l + 2)), gout, full("MS", 16 * n), 0.0, OP.min, OP.mult)
-        for k in range(NF):
-            mm("psF", 512 * (k % 2), "EQ", 128 * k, "QX", 0, 384)
-            cp(vw("FP", 384 * k, 384 * k + 352), vw("psF", 512 * (k % 2), 512 * (k % 2) + 352), "S")
+            mm(4 + c, "QX", SL[c], "QU", 0)
+            ab, pv = vw("AB", 128 * c, 128 * c + 117), vw("ps", 512 * (4 + c), 512 * (4 + c) + 117)
+            add({"S": 117 * CYC}, {"S": lambda ab=ab, pv=pv: g.scalar.activation(ap(ab), ap(pv), AF.Sign, bias=-1e-36)}, [pv], [ab])
+            scan(vw("SC", 144 * c, 144 * c + 117), ab, full("hd", 117), 0.0, OP.add, OP.mult)
         if t:
-            fd, nn = "fdr%d" % (t - 1), "CT%d" % t
-            ld("Y", lambda fd=fd: [(T.crow[0:1, :], T[fd][:])], [two(fd)], [full("crow", 256)])
-            add({"G": 1.0}, {"G": lambda: g.partition_broadcast(T.CB[:], T.crow[0:1, :], 128)}, [full("crow", 256)], [full("CB", 256)])
-            tt(full(nn, 256), vw(ctn, cta, cta + 256), full("CB", 256), OP.min)
-            ctn, cta = nn, 0
-        for c in range(3):
-            s0, c8, go = 1152 * c, vw("of1", 8 * c, 8 * c + 8), "GO%d" % c
-            tt(c8, vw("SC", s0 + 15, s0 + 1024, 144), full("gc", 8), OP.add)
-            ts(vw("OC", 8 * c, 8 * c + 8), c8, 0.03125, None, OP.mult)
-            cp(full(go), ind(vw(ctn, cta, cta + 256), "OC", 8 * c, 8 * c + 8), "VS")
-            scan(vw("CO", 128 * c, 128 * c + 128), full(go), full("MC"), 0.0, OP.min, OP.add)
-            scan(vw("DS", 8 * c, 8 * c + 8), full("r64", 8), vw("CO", 128 * c + 15, 128 * c + 128, 16), -1.0, OP.mult, OP.max)
-        ts(full("AM", 32), ind(full("DS", 24), "R1", 0, 2), 64.0, 32.0, OP.min, OP.add)
+            came(t - 1)
+            fd = "fdr%d" % (t - 1)
+            ld("Y", lambda fd=fd: [(T.STG[16 * k:16 * k + 7, :], T[fd][0:112, :]) for k in range(8)], [two(fd)], [full("STG", 32)], 8)
+            tt(vw("TAB", 1, 33), ind(full("STG", 32), "PM", 0, 2), vw("TAB", 1, 33), OP.mult)
+        for l in range(7):
+            n = 8 - l
+            for p in range(2):
+                o0, b0, b1 = 72 * p + l * (17 - l), PS * p + 16 * (l - 1) * (18 - l), PS * p + 16 * l * (17 - l)
+                for s in range(2):
+                    if p == 1 and s == 1 and l % 2 == 0: continue
+                    out = vw("OF", o0 + s, o0 + 2 * n, 2)
+                    if l == 0:
+                        s0 = 144 * (2 * p + s)
+                        ts(out, vw("SC", s0 + 20, s0 + 133, 16), vw("SC", s0 + 4), 544.5, OP.add, OP.add)
+                    else:
+                        a = b0 + 16 * s + l - 1
+                        ts(out, vw("O", a + 32, a + 32 * n + 1, 32), 32.0, vw("O", a), OP.mult, OP.add)
+                go = full("GO%d" % p, 32 * n)
+                cp(go, ind(full("TAB", TW), "OF", o0, o0 + 2 * n), "S")
+                turn32(vw("O", b1, b1 + 32 * n), go)
+        for p in range(2):
+            b = PS * p + 1056
+            tt(vw("O", b + 71, b + 96, 16), vw("O", b + 6, b + 32, 16), vw("O", b + 38, b + 64, 16), OP.max)
+        for k in range(4):
+            mm(k, "EQ", 128 * k, "QX", 0, C)
+            if k < NF:
+                for j, n in CH: cp(vw("FP", C * k + j, C * k + j + n), vw("ps", 512 * k + j, 512 * k + j + n), "S")
+        cp(full("AM", 32), ind(full("O", 2 * PS), "R1", 0, 2))
         for q, ds in (("Y", [1, 2, 3, 4]), ("S", [5, 6, 7])):
             def turn(ds=ds):
                 r = []
                 for d in ds:
-                    a, b = 32 + 3 * d, 35 + 3 * d
-                    r += [(T.AM[16 * d:128, a:b], T.AM[0:128 - 16 * d, 3 * d:3 * d + 3]), (T.AM[0:16 * d, a:b], T.AM[128 - 16 * d:128, 3 * d:3 * d + 3])]
+                    a, b = 4 * d - 4, 28 + 4 * d
+                    r += [(T.AM[16 * d:128, b:b + 4], T.AM[0:128 - 16 * d, a:a + 4]), (T.AM[0:16 * d, b:b + 4], T.AM[128 - 16 * d:128, a:a + 4])]
                 return r
-            ld(q, turn, [full("AM", 32)], [vw("AM", 32 + 3 * d, 35 + 3 * d) for d in ds], 2 * len(ds))
+            ld(q, turn, [full("AM", 32)], [vw("AM", 28 + 4 * d, 32 + 4 * d) for d in ds], 2 * len(ds))
         cp(full("L", 32), ind(full("AM", 64), "R2", 0, 2))
 
         lall = ("L", 0, 22)
-        cp(full("jk", 352), ind(full("WN", 112), *lall), "S", acc=vw("cnt", 0))
-        cp(vw("cnI", 0), vw("cnt", 0))
-        ts(vw("rem", 0), vw("cnI", 0), 1023, None, OP.bitwise_and)
+        cp(full("JK", C), ind(full("WJ", 34), *lall), "S", acc=one("cnt"))
+        cp(one("cnI"), one("cnt"))
+        ts(one("rem"), one("cnI"), 511, None, OP.bitwise_and)
         wn = "w_%d" % t
-        ts(vw(wn, 0), vw("rem", 0), 0.0, vw("nV", 0), OP.is_gt, OP.mult)
-        ts(vw(wn, 1), vw("cnt", 0), 1024.0, vw("nV", 1), OP.is_ge, OP.mult)
-        fland, fw = "fdr%d" % t if t < 2 else "fw2", "fw%d" % t
+        ts(vw(wn, 0), one("cnt"), 0.0, vw(OCC[t], 0), OP.is_le, OP.max)
+        ts(vw(wn, 1), one("rem"), 0.0, vw(OCC[t], 1), OP.is_equal, OP.max)
+        fland = "fdr%d" % t if t < 2 else "fw2"
         send(two(fland), two(wn), "rf%d" % t, boost=5.0)
 
-        tv = "TV%d" % t
-        for c in range(3):
-            n, j = NV[c], 128 * c
+        tv = 4 * PW * t
+        for c, (j, n) in enumerate(CH):
             for k in range(4):
-                z, b = vw("ZS", 512 * c + k, 512 * c + 4 * n, 4), 512 * (k % 2)
-                pick = ind(vw(tv, PW * k, PW * k + CAME), "L", 8 * c, 8 * c + n // 16)
-                if k < NF: tt(z, pick, vw("FP", 384 * k + j, 384 * k + j + n), OP.add)
+                tg, z = vw("TG", C * k + j, C * k + j + n), vw("ZS", 4 * j + k, 4 * j + 4 * n, 4)
+                pick = ind(vw("TV", tv + PW * k, tv + PW * k + CAME), "L", j // 16, (j + n) // 16)
+                if k < NF: tt(z, pick, vw("FP", C * k + j, C * k + j + n), OP.add)
                 else:
-                    tg = vw("TG", 384 * (k - NF) + j, 384 * (k - NF) + j + n)
-                    mm("psF", b, "EQ", 128 * k, "QX", j)
                     cp(tg, pick, "S")
-                    tt(z, vw("psF", b, b + n), tg, OP.add)
-                cp(vw("ZP", 384 * k + j, 384 * k + j + n), z, "S", 64.0)
-            quant("QZ", j, "ZS", 512 * c)
+                    tt(z, vw("ps", 512 * k + j, 512 * k + j + n), tg, OP.add)
+            quant("QZ", j, "ZS", 4 * j, n)
+            cp(vw("ZP", 4 * j, 4 * j + 4 * n), vw("ZS", 4 * j, 4 * j + 4 * n), "VS", 64.0)
+        for c, (j, n) in enumerate(CH):
             for k in range(4):
-                mm("psR", 512 * k, "WC", 128 * k, "QZ", j)
-                tt(vw("XT", 512 * c + k, 512 * c + 4 * n, 4), vw("psR", 512 * k, 512 * k + n), vw("ZP", 384 * k + j, 384 * k + j + n), OP.add)
+                b = 4 * (1 - c % 2) + k
+                mm(b, "WC", 128 * k, "QZ", j, n)
+                tt(vw("XT", 4 * j + k, 4 * j + 4 * n, 4), vw("ps", 512 * b, 512 * b + n), vw("ZP", 4 * j + k, 4 * j + 4 * n, 4), OP.add)
 
-        tt(full("MV", 352), ind(full("WM", 112), *lall), full("wt", 352), OP.mult)
-        for nm, op, sg, s in (("mxa", OP.max, -1.0, 0), ("mxb", OP.min, 1.0, 1)):
-            add({"V": 352 * CYC}, {"V": lambda nm=nm, op=op: g.vector.tensor_reduce(ap(vw(nm, 0)), T.MV[:], AxisListType.X, op)}, [full("MV", 352)], [vw(nm, 0)])
-            ts(vw("CL", s), vw(nm, 0), sg, 352.0, OP.mult, OP.add)
-        for k in range(4): cp(vw("CLT", k, 128, 4), ind(vw("ZP", 384 * k, 384 * k + 384), "CL", 0, 2), "S")
-        cq, la = "CQ%d" % t, (0, 128, 160)[t]
+        for a in range(0, C, PC):
+            b = min(a + PC, C)
+            scan(vw("SA", a, b), vw("JK", a, b), vw("one", a, b), vw("SA", a - 1) if a else 160.0, OP.max, OP.add)
+            scan(vw("SB", a, b), vw("JK", a, b), vw("stp", a, b), vw("SB", a - 1) if a else -160.0 / 512, OP.min, OP.add)
+        ts(vw("CL", 0, 8, 2), full("cA", 4), vw("SA", C - 1), -4.0, OP.add, OP.mult)
+        ts(vw("CL", 1, 8, 2), full("cB", 4), vw("SB", C - 1), 2048.0, OP.add, OP.mult)
+        for k in range(4): cp(vw("CLT", k, 128, 4), ind(full("ZS", 1412), "CL", 2 * k, 2 * k + 2), "S", 64.0)
+        cq, la = "CQ%d" % t, (0, 160, 192)[t]
         quant(cq, 0, "CLT", 0)
         send(vw("LC", la, la + 32) + ("c",), vw(cq, 0, 32) + ("c",), "rc%d" % t)
         send(vw("LCs", la, la + 32), vw(cq + "s", 0, 32), "rc%d" % t)
 
-        if t < 2: ld("Y", lambda fw=fw, fl=fland: [(T[fw][:], T[fl][:])], [two(fland)], [two(fw)])
-        ts(two("ua"), two(fw), 0.0, float(CAME), OP.is_lt, OP.mult)
-        tt(two("uk"), two("ua"), two(EST[t]), OP.min)
-        tt(two("uf"), two("uk"), two("nW"), OP.add)
-        tt(two(EST[t + 1]), two(EST[t]), two("uk"), OP.subtract)
-        if t < 2: cp(two("UL"), two("uf"))
-        else:
-            for s in range(2): cp(vw("UL3", 2 * s), vw("uf", s))
-        lv, off = ((0, 0), (32, 96), (64, 96))[t]
-        for k in range(4):
-            b = 512 * (k % 2)
-            mm("psF", b, "EQ", 128 * k, "LC", lv)
-            cp(vw(tv, PW * k + CAME, PW * k + CAME + 32), vw("psF", b + off, b + off + 32), "S", -1.0)
-            win = vw(tv, PW * k, PW * k + CAME + 32)
-            if t < 2: cp(vw("TV%d" % (t + 1), PW * k, PW * k + 32), ind(win, "UL", 0, 2), "S")
-            else:
-                for s in range(2): cp(vw("RT", 4 * s + k, 128, 8), ind(win, "UL3", 2 * s, 2 * s + 1), "S", -64.0)
-
-    cp(full("BPO", 352), ind(full("MB", 112), "L", 0, 22), "S")
-    ld("Y", lambda: [(T.bp[:, 0:352], T.BPO[0:128:16, :])], [full("BPO", 352)], [])
-    ts(two("FO"), two(EST[3]), 0.0, None, OP.is_equal)
-    ld("Y", lambda: [(T.bp[:, 352:384], T.FO[:])], [two("FO")], [])
+    came(2)
+    cp(full("BPO", C), ind(full("MB", 34), "L", 0, 22), "S")
+    ld("Y", lambda: [(T.bp[:, 0:C], T.BPO[0:128:16, :])], [full("BPO", C)], [])
+    ld("Y", lambda: [(T.bp[:, C + 16 * s:C + 16 * s + 16], ap(vw(OCC[3], s))) for s in range(2)], [two(OCC[3])], [], 2)
     ld("Y", lambda: [(T.rt[:], T.RT[:])], [full("RT")], [])
-    for c in range(3):
-        n, j, b = NV[c], 128 * c, 512 * (c % 2)
-        quant("QX", j, "XT", 512 * c)
-        mm("psS", b, "QV", 0, "QX", j)
-        cp(vw("YO", j, j + n), vw("psS", b, b + n))
+    for c, (j, n) in enumerate(CH):
+        quant("QX", j, "XT", 4 * j, n)
+        mm(c, "QV", 0, "QX", j, n)
+        cp(vw("YO", j, j + n), vw("ps", 512 * c, 512 * c + n), "VS")
         ld("Y", lambda j=j, n=n: [(T.y[:, j:j + n], T.YO[:, j:j + n])], [vw("YO", j, j + n)], [])
-        ld("S", lambda j=j, n=n: [(T.oc[:, 4 * j:4 * j + 4 * n], T.QX[:, j:j + n].bitcast(dt.uint8))], [vw("QX", j, j + n)], [])
-    ld("S", lambda: [(T.osc[4 * k:4 * k + 4, :], T.QXs[32 * k:32 * k + 4, 0:352]) for k in range(4)], [full("QXs", 352)], [], 4)
+        ld("Y", lambda j=j, n=n: [(T.oc[:, 4 * j:4 * j + 4 * n], T.QX[:, j:j + n].bitcast(dt.uint8))], [vw("QX", j, j + n)], [])
+    ld("Y", lambda: [(T.osc[4 * k:4 * k + 4, :], T.QXs[32 * k:32 * k + 4, 0:C]) for k in range(4)], [full("QXs", C)], [], 4)
     return ops
 
 

@@ -2,14 +2,14 @@ from concourse.mybir import dt, AluOpType as OP, ActivationFunctionType as AF
 
 COPY = AF.Copy
 C = 352
-CH = [(0, 192), (192, 160)]
+CH = [(0, 224), (224, 128)]
 SL = [0, 128, 224]
 PW, CAME = 80, 34
 PS = 1152
 TW = 1104
-SMALL = {"KI": "bI4 pI1 BI8 flI2 fl8_32 g1I2 g2I2 GoI2 Gm2 al2 dI2 dm2 cnI1 rem1",
-         "KF": "BF8 c41_2 c02_2 c10_2 c28_2 c16_2 nW2 u1_2 u2_2 u3_2 k1_1 k2_1 ph1 phi1 be2 bm2 de2 t1_2 e1_2 e2_2 e3_2 e4_2 kF4 cA4 cB4 c01_2",
-         "KL": "oca2 ocb2 occ2 ocd2 tk2 cnt1"}
+SMALL = {"KI": "flI4 fl8_32 bI4 BI_10 GoI2 Gm2 al2 dI2 dm2 t1_2 qs2 gs2",
+         "KF": "BF_10 c02_2 c10_2 c16_2 nW2 u1_4 u2_4 u3_4 k1_1 k2_1 k3_1 k4_1 ph1 phi1 be2 bm2 de2 e1_2 e2_2 e3_2 e4_2 e5_2 e6_2 e7_2 e8_2 kF4 cA4 cB4 c01_2 cs4 cc4 g1_4 g2_4",
+         "KL": "oca2 ocb2 occ2 ocd2 tk2 cnt1 rem1"}
 ALIAS = {}
 for _b, _s in SMALL.items():
     _k = 0
@@ -24,9 +24,9 @@ def _scratch():
     f, h, i, u, q, b = "float32", "bfloat16", "int32", "uint16", "float8_e4m3fn_x4", "uint8"
     s = {"fdr0": ("dram", [128, 2], h), "fdr1": ("dram", [128, 2], h)}
     for d, names in ((i, "KI:80 tic:64"),
-                     (f, "KF:72 KL:16 rr:128 ix:48 wa:48 wb:48 MB:48 SA:352 SB:352 RT:128 BPO:352 YO:352"),
-                     (u, "R1:2 R2:2 PM:2 OF:144 L:32 CL:8 UL:2"),
-                     (h, "hd:128 WJ:48 ET:520 tib:64 tbt:64 TAB:%d STG:32 UT:512 VT:512 TT:512 XT:1408 AB:384 SC:432 GO0:256 GO1:256 O:%d AM:64 TG:1408 "
+                     (f, "KF:96 KL:16 rr:128 ix:48 wa:48 wb:48 MB:48 SA:352 SB:352 RT:128 BPO:352 YO:352"),
+                     (u, "R1:4 R2:2 PM:2 OF:144 L:32 CL:8 UL:2"),
+                     (h, "hd:128 WJ:48 ET:520 tib:64 tbt:64 TAB:%d STG:32 UT:512 VT:512 TT:512 XT:1408 AB:384 SC:432 GO0:256 GO1:256 O:%d AM:168 TB:64 TG:1408 "
                          "ZS:1424 ZP:1408 TV:960 FP:1408 JK:352 one:352 stp:352 CLT:512 w_0:2 w_1:2 w_2:2 fw0:2 fw1:2 fw2:2" % (TW, 2 * PS))):
         for n in names.split():
             n, w = n.split(":")
@@ -44,7 +44,7 @@ SEMAPHORES = ["sV", "sS", "sT", "sG", "sent", "rf0", "rf1", "rf2", "rc0", "rc1",
 PLAN = {}
 TRIES = 3000
 PC = 118
-NF = 2
+NF = 1
 WAKE, DMALAT, NETLAT, CYC, PECYC = 0.1, 1.8, 2.5, 0.001, 0.0012
 
 
@@ -242,22 +242,23 @@ def build(g, core, T, topo, nxt):
     fill(full("OF", 144), 0)
     for k, m in enumerate((16, 8, 2, 1)): iota(vw("bI", k), [[0, 1]], 0, m)
     ts(vw("BI", 0, 4), vw("bI", 0, 4), 4, 1, OP.arith_shift_right, OP.bitwise_and)
-    ts(vw("BI", 4), vw("bI", 3), 2, 3, OP.arith_shift_right, OP.bitwise_and)
-    ts(vw("BI", 5), vw("bI", 3), 4, None, OP.arith_shift_right)
-    ts(vw("BI", 6), vw("bI", 3), 15, None, OP.bitwise_and)
-    cp(vw("BF", 0, 7), vw("BI", 0, 7))
-    sg, pr, i3, g0, ih, gF, iF = [vw("BF", k) for k in range(7)]
-    for n, st, b in (("c41", 4, 1), ("c02", 2, 0), ("c10", -1, 1), ("c28", 2, 28), ("c16", 16, 1), ("c01", 1, 0)): iota(two(n), [[st, 2]], b, 0)
+    for k, (sh, m) in enumerate(((1, 6), (4, 7), (0, 15), (5, 3), (5, 1), (6, 1))): ts(vw("BI", 4 + k), vw("bI", 3), sh, m, OP.arith_shift_right, OP.bitwise_and)
+    cp(vw("BF", 0, 10), vw("BI", 0, 10))
+    sg, pr, i3, g0, ih, gF, iF, qF, q1, aF = [vw("BF", k) for k in range(10)]
+    for n, st, b in (("c02", 2, 0), ("c10", -1, 1), ("c16", 16, 1), ("c01", 1, 0)): iota(two(n), [[st, 2]], b, 0)
+    four = lambda n: vw(n, 0, 4)
+    iota(four("cs"), [[0, 2], [2, 2]], -1, 0)
+    iota(four("cc"), [[0, 2], [-1, 2]], 1, 0)
     ts(two("nW"), two("c16"), iF, None, OP.add)
     ts(two("PM"), two("c01"), iF, iF, OP.add, OP.add)
-    ts(two("g1I"), two("c41"), ih, gF, OP.add, OP.add)
-    ts(two("g2I"), two("g1I"), 7, None, OP.bitwise_and)
-    ts(two("u1"), two("g2I"), -1.0, 16.0, OP.mult, OP.add)
-    ts(two("u2"), two("g2I"), 1.0, 16.0, OP.add, OP.mult)
-    tt(two("u3"), two("u1"), two("u2"), OP.mult)
+    ts(four("g1"), four("cs"), g0, ih, OP.mult, OP.add)
+    tt(four("g2"), four("g1"), four("cc"), OP.add)
+    ts(four("u1"), four("g2"), -1.0, 16.0, OP.mult, OP.add)
+    ts(four("u2"), four("g2"), 1.0, 16.0, OP.add, OP.mult)
+    tt(four("u3"), four("u1"), four("u2"), OP.mult)
     ts(one("k1"), pr, float(PS), -25.0, OP.mult, OP.add)
     ts(one("k2"), sg, 16.0, one("k1"), OP.mult, OP.add)
-    ts(two("R1"), two("u3"), one("k2"), None, OP.add)
+    ts(four("R1"), four("u3"), one("k2"), None, OP.add)
     ts(two("GoI"), two("c02"), iF, None, OP.add)
     ts(two("Gm"), two("GoI"), 7, None, OP.bitwise_and)
     ts(two("al"), two("GoI"), 1, None, OP.bitwise_and)
@@ -267,15 +268,22 @@ def build(g, core, T, topo, nxt):
     tt(two("bm"), two("be"), two("al"), OP.subtract)
     ts(two("de"), two("bm"), one("phi"), None, OP.mult)
     tt(two("t1"), two("de"), two("Gm"), OP.add)
-    ts(two("dI"), two("t1"), -1.0, gF, OP.mult, OP.add)
-    ts(two("dm"), two("dI"), 7, None, OP.bitwise_and)
+    ts(two("qs"), two("t1"), 1, None, OP.arith_shift_right)
+    ts(two("gs"), two("t1"), 1, None, OP.bitwise_and)
+    ts(two("dI"), two("qs"), -1.0, qF, OP.mult, OP.add)
+    ts(two("dm"), two("dI"), 3, None, OP.bitwise_and)
+    ts(one("k3"), aF, 8.0, -24.0, OP.mult, OP.add)
+    ts(one("k4"), q1, 4.0, 72.0, OP.mult, OP.add)
     tt(two("e1"), two("be"), two("de"), OP.subtract)
-    tt(two("e2"), two("e1"), two("c28"), OP.add)
-    ts(two("e3"), two("dm"), 4.0, None, OP.mult)
-    tt(two("e4"), two("e3"), two("e2"), OP.add)
-    cp(two("R2"), two("e4"))
+    tt(two("e2"), two("e1"), two("c02"), OP.add)
+    ts(two("e3"), two("dm"), 24.0, one("k4"), OP.mult, OP.add)
+    ts(two("e4"), two("dm"), 0.0, one("k3"), OP.is_equal, OP.mult)
+    ts(two("e5"), two("gs"), g0, 16.0, OP.not_equal, OP.mult)
+    tt(two("e6"), two("e3"), two("e2"), OP.add)
+    tt(two("e7"), two("e4"), two("e5"), OP.add)
+    tt(two("e8"), two("e6"), two("e7"), OP.add)
+    cp(two("R2"), two("e8"))
     for p in range(2): iota(vw("O", PS * p + 1120, PS * p + 1152), [[0, 32]], 0, 0)
-    iota(vw("AM", 60, 64), [[0, 4]], 0, 0)
     iota(full("STG", 32), [[0, 32]], 1, 0)
     fill(full("ET", 520), 0.0)
     add({"G": 0.2 + 1040 * CYC}, {"G": lambda: g.affine_select(T.ET[:], T.ET[:], [[1, 520]], OP.not_equal, 0.015625, -3, -4)}, [], [full("ET", 520)])
@@ -351,24 +359,22 @@ def build(g, core, T, topo, nxt):
             mm(k, "EQ", 128 * k, "QX", 0, C)
             if k < NF:
                 for j, n in CH: cp(vw("FP", C * k + j, C * k + j + n), vw("ps", 512 * k + j, 512 * k + j + n), "S")
-        cp(full("AM", 32), ind(full("O", 2 * PS), "R1", 0, 2))
-        for q, ds in (("Y", [1, 2, 3, 4]), ("S", [5, 6, 7])):
-            def turn(ds=ds):
-                r = []
-                for d in ds:
-                    a, b = 4 * d - 4, 28 + 4 * d
-                    r += [(T.AM[16 * d:128, b:b + 4], T.AM[0:128 - 16 * d, a:a + 4]), (T.AM[0:16 * d, b:b + 4], T.AM[128 - 16 * d:128, a:a + 4])]
-                return r
-            ld(q, turn, [full("AM", 32)], [vw("AM", 28 + 4 * d, 32 + 4 * d) for d in ds], 2 * len(ds))
-        cp(full("L", 32), ind(full("AM", 64), "R2", 0, 2))
+        cp(full("AM", 64), ind(full("O", 2 * PS), "R1", 0, 4))
+        turn32(full("TB", 64), full("AM", 64))
+        turn32(vw("AM", 64, 96), vw("TB", 16, 48))
+        moves = [(2, 64 * a, 64 - 64 * a, 64) for a in range(2)] + [(x, 32 * q, 32 * ((q + x) % 4), 32) for x in (1, 3) for q in range(4)]
+        for k, (x, p0, p1, np_) in enumerate(moves):
+            a, b = 48 + 8 * (p1 // 64), 72 + 24 * x
+            io = lambda a=a, b=b, p0=p0, p1=p1, np_=np_: (T.AM[p1:p1 + np_, b:b + 24], T.AM[p0:p0 + np_, a:a + 24])
+            add({"V": 64 * CYC, "S": 64 * CYC}, {"V": lambda io=io: g.vector.tensor_copy(*io()), "S": lambda io=io: g.scalar.activation(*io(), COPY)}, [vw("AM", 48, 96)], [vw("mv", k)])
+        add({"V": 0.05 + 48 * CYC}, {"V": lambda: g.vector.tensor_copy(T.L[:], T.AM[:].indirect(T.R2[:]))}, [full("AM", 96), two("R2"), full("mv", 10)], [full("L", 32)])
 
         lall = ("L", 0, 22)
         cp(full("JK", C), ind(full("WJ", 34), *lall), "S", acc=one("cnt"))
-        cp(one("cnI"), one("cnt"))
-        ts(one("rem"), one("cnI"), 511, None, OP.bitwise_and)
+        ts(one("rem"), one("cnt"), 3.0 * 2 ** 31, -3.0 * 2 ** 31, OP.add, OP.add)
         wn = "w_%d" % t
         ts(vw(wn, 0), one("cnt"), 0.0, vw(OCC[t], 0), OP.is_le, OP.max)
-        ts(vw(wn, 1), one("rem"), 0.0, vw(OCC[t], 1), OP.is_equal, OP.max)
+        ts(vw(wn, 1), one("rem"), one("cnt"), vw(OCC[t], 1), OP.is_equal, OP.max)
         fland = "fdr%d" % t if t < 2 else "fw2"
         send(two(fland), two(wn), "rf%d" % t, boost=5.0)
 

@@ -7,9 +7,10 @@ SL = [0, 128, 224]
 PW, CAME = 80, 34
 PS = 1152
 TW = 1104
-SMALL = {"KI": "flI4 fl8_32 bI4 BI_10 GoI2 Gm2 al2 dI2 dm2 t1_2 qs2 gs2",
-         "KF": "BF_10 c02_2 c10_2 c16_2 nW2 u1_4 u2_4 u3_4 k1_1 k2_1 k3_1 k4_1 ph1 phi1 be2 bm2 de2 e1_2 e2_2 e3_2 e4_2 e5_2 e6_2 e7_2 e8_2 kF4 cA4 cB4 c01_2 cs4 cc4 g1_4 g2_4",
-         "KL": "oca2 ocb2 occ2 ocd2 tk2 cnt1 rem1"}
+IP = [0, 8, 2, 10, 1, 9, 3]
+SMALL = {"KI": "flI4 bI4 BI_11 GoI2 Gm2 al2 dI2 dm2 t1_2 qs2 gs2",
+         "KF": "BF_11 c02_2 c10_2 c16_2 nW2 u1_4 u2_4 u3_4 k1_1 k2_1 k3_1 k4_1 ph1 phi1 be2 bm2 de2 e1_2 e2_2 e3_2 e4_2 e5_2 e6_2 e7_2 e8_2 kF4 cA4 cB4 c00_2 cs4 cc4 g1_4 g2_4 cM2",
+         "KL": "oca2 ocb2 occ2 ocd2 tk2 cnt1 rem2"}
 ALIAS = {}
 for _b, _s in SMALL.items():
     _k = 0
@@ -22,12 +23,12 @@ OCC = ["oca", "ocb", "occ", "ocd"]
 
 def _scratch():
     f, h, i, u, q, b = "float32", "bfloat16", "int32", "uint16", "float8_e4m3fn_x4", "uint8"
-    s = {"fdr0": ("dram", [128, 2], h), "fdr1": ("dram", [128, 2], h)}
-    for d, names in ((i, "KI:80 tic:64"),
+    s = {}
+    for d, names in ((i, "KI:48 tic:64"),
                      (f, "KF:96 KL:16 rr:128 ix:48 wa:48 wb:48 MB:48 SA:352 SB:352 RT:128 BPO:352 YO:352"),
-                     (u, "R1:4 R2:2 PM:2 OF:144 L:32 CL:8 UL:2"),
-                     (h, "hd:128 WJ:48 ET:520 tib:64 tbt:64 TAB:%d STG:32 UT:512 VT:512 TT:512 XT:1408 AB:384 SC:432 GO0:256 GO1:256 O:%d AM:168 TB:64 TG:1408 "
-                         "ZS:1424 ZP:1408 TV:960 FP:1408 JK:352 one:352 stp:352 CLT:512 w_0:2 w_1:2 w_2:2 fw0:2 fw1:2 fw2:2" % (TW, 2 * PS))):
+                     (u, "R1:4 R2:2 FL:4 OF:144 L:32 CL:8 UL:2 w_0:4 w_1:4 w_2:4 fw0:4 fw1:4 fw2:4"),
+                     (h, "hd:128 WJ:48 ET:520 tib:64 tbt:64 TAB:%d WN:16 RW:64 MA:64 MC:32 UT:512 VT:512 TT:512 XT:1408 AB:384 SC:432 GO0:256 GO1:256 O:%d AM:168 TB:64 TG:1408 "
+                         "ZS:1424 ZP:1408 TV:960 FP:1424 JK:352 one:352 stp:352 CLT:512" % (TW, 2 * PS))):
         for n in names.split():
             n, w = n.split(":")
             s[n] = ("sbuf", [128, int(w)], d)
@@ -42,10 +43,11 @@ def _scratch():
 SCRATCH = _scratch()
 SEMAPHORES = ["sV", "sS", "sT", "sG", "sent", "rf0", "rf1", "rf2", "rc0", "rc1", "rc2"] + ["d%d" % k for k in range(60)]
 PLAN = {}
-TRIES = 3000
+TRIES = 6000
+SPLIT = [3, 2, 2, 1, 1, 1, 0]
 PC = 118
-NF = 1
-WAKE, DMALAT, NETLAT, CYC, PECYC = 0.1, 1.8, 2.5, 0.001, 0.0012
+NF = 2
+WAKE, DMALAT, NETLAT, CYC, PECYC = 0.15, 2.0, 3.0, 0.00104, 0.0012
 
 
 def bits(v):
@@ -104,7 +106,7 @@ def plan(ops):
     def rnd():
         seed[0] = (seed[0] * 1103515245 + 12345) % 2147483648
         return seed[0] / 2147483648.0
-    pr, pref = [prio[k] + ops[k]["boost"] - 1e-6 * k for k in range(n)], [0.0] * n
+    pr, pref = [prio[k] + ops[k]["boost"] - 1e-6 * k for k in range(n)], [0.4] * n
     best = place(pr, pref)
     for it in range(TRIES):
         p2, f2 = list(pr), list(pref)
@@ -160,20 +162,25 @@ def build(g, core, T, topo, nxt):
         val = lambda s: ap(s) if isinstance(s, tuple) else s
         if op1 is None: fn = lambda: g.vector.tensor_scalar(ap(out), ap(in0), val(s1), None, op0)
         else: fn = lambda: g.vector.tensor_scalar(ap(out), ap(in0), val(s1), val(s2), op0, op1)
-        add({"V": d}, {"V": fn}, [in0] + sc, [out], boost=boost)
+        dur, fns = {"V": d}, {"V": fn}
+        kind = lambda v: SCRATCH[ALIAS.get(v[0], v)[0]][2]
+        if not isind(in0) and all(kind(v) == "float32" for v in [out, in0] + sc) and (op0, op1) in ((OP.mult, OP.add), (OP.mult, None), (OP.add, None)):
+            a, b = (s1, s2) if op1 is not None else (s1, 0.0) if op0 == OP.mult else (1.0, s1)
+            dur["S"], fns["S"] = d, lambda: g.scalar.activation(ap(out), ap(in0), AF.Identity, bias=val(b), scale=val(a))
+        add(dur, fns, [in0] + sc, [out], boost=boost)
 
     def tt(out, a, b, op):
         d = gat(out, 0.05) if isind(a) else cost(out, 1.0 if a[0] == "ps" else 2.0)
         add({"V": d}, {"V": lambda: g.vector.tensor_tensor(ap(out), ap(a), ap(b), op)}, [a, b], [out])
 
-    def cp(out, a, q="V", scale=1.0, acc=None, boost=0.0):
+    def cp(out, a, q="V", scale=1.0, acc=None, boost=0.0, more=[]):
         i = isind(a)
         kw = {"scale": scale} if scale != 1.0 else {}
         if acc: kw["accum_out"] = acc
         fns = {"V": lambda: g.vector.tensor_copy(ap(out), ap(a)) if scale == 1.0 else g.vector.tensor_scalar(ap(out), ap(a), scale, None, OP.mult),
                "S": lambda: g.scalar.activation(ap(out), ap(a), COPY, **{k: ap(x) if k == "accum_out" else x for k, x in kw.items()})}
         durs = {"V": gat(out, 0.05) if i else cost(out, 1.0 if wide(out, a) else 0.5), "S": (gat(out, 0.065) if i else cost(out, 1.0)) + (0.02 if acc else 0.0)}
-        add({k: durs[k] for k in q}, {k: fns[k] for k in q}, [a], [out] + ([acc] if acc else []), boost=boost)
+        add({k: durs[k] for k in q}, {k: fns[k] for k in q}, [a] + more, [out] + ([acc] if acc else []), boost=boost)
 
     def scan(out, d0, d1, init, op0, op1):
         add({"V": cost(out, 1.0 if wide(out, d0, d1) else 0.5)}, {"V": lambda: g.vector.tensor_tensor_scan(ap(out), ap(d0), ap(d1), ap(init) if isinstance(init, tuple) else init, op0, op1)},
@@ -181,6 +188,9 @@ def build(g, core, T, topo, nxt):
 
     def turn32(out, a):
         add({"V": cost(out, 0.5)}, {"V": lambda: g.vector.transpose(ap(out), ap(a))}, [a], [out])
+
+    def move(io, ins, outs):
+        add({"V": 64 * CYC, "S": 64 * CYC}, {"V": lambda: g.vector.tensor_copy(*io), "S": lambda: g.scalar.activation(*io, COPY)}, ins, outs)
 
     def fill(out, val, boost=0.0):
         add({"V": cost(out, 1.0 if wide(out) else 0.5)}, {"V": lambda: g.vector.memset(ap(out), val)}, [], [out], boost=boost)
@@ -205,29 +215,31 @@ def build(g, core, T, topo, nxt):
         ne = 8 if T is None else len(topo.engines(core, nxt))
         def fn():
             rid, pid = topo.addr(nxt, core)
-            g.remote_dma(ap(out) if out[0][:3] != "fdr" else T[out[0]][:], ap(in_), T.sem[sem], T.sem.sent, pid, rid, topo.mask(core, nxt))
+            g.remote_dma(ap(out), ap(in_), T.sem[sem], T.sem.sent, pid, rid, topo.mask(core, nxt))
         add({"G": 0.3}, {"G": fn}, [in_], [out], NETLAT, "n", (sem, ne), boost)
 
     full = lambda n, w=128: vw(n, 0, w)
     two = lambda n: vw(n, 0, 2)
     one = lambda n: vw(n, 0)
 
-    ld("Y", lambda: [(T.tic[:, 0:32], T.ti[0:4, :]), (T.tic[:, 32:64], T.ti[3:7, :])], [], [full("tic", 64)], 2, boost=50.0)
-    f8 = ALIAS["fl8"][1]
-    ld("Y", lambda: [(T.KI[0:8, f8:f8 + 32], T.fl[:])], [], [full("fl8", 32)], boost=49.0)
+    ld("Y", lambda: [(T.tic[0:64, 0:32], T.ti[0:5:4, :]), (T.tic[64:128, 0:32], T.ti[2:7:4, :]), (T.tic[0:64, 32:64], T.ti[1:6:4, :]), (T.tic[64:128, 32:64], T.ti[3:5, :])],
+       [], [full("tic", 64)], 4, boost=50.0)
+    ld("Y", lambda: [(ap(vw("flI", s)), T.fl[:, 16 * (s % 2):16 * (s % 2) + 16]) for s in range(4)], [], [full("flI", 4)], 4, boost=49.0)
     for c, (j, n) in enumerate(CH):
         v = vw("XT", 4 * j, 4 * j + 4 * n)
         ld("S", lambda v=v: [(ap(v), T.x[:, v[1]:v[2]])], [], [v], boost=45.0 - 2 * c)
     ld("S", lambda: [(T.UT[:], T.u[:])], [], [full("UT", 512)], boost=44.0)
     fill(full("TAB", TW), 33.0, boost=50.0)
-    iota(full("TAB", 33), [[1, 33]], 0, 0, boost=50.0)
     ts(full("tib", 64), full("tic", 64), 1.0, None, OP.add)
     turn32(full("tbt", 64), full("tib", 64))
-    add({"V": 64 * CYC}, {"V": lambda: g.vector.tensor_scalar(T.TAB[0:7, 1:33], T.KI[0:7, f8:f8 + 32], -33.0, 33.0, OP.mult, OP.add)}, [full("fl8", 32)], [vw("TAB", 1, 33)])
-    ld("Y", lambda: [(T.TAB[0:4, 33:1057], T.tbt[:, 0:32]), (T.TAB[4:7, 33:1057], T.tbt[32:128, 32:64])], [full("tbt", 64)], [vw("TAB", 32, 1057)], 2)
-    ld("Y", lambda: [(T.TAB[16 * k:16 * k + 7, 0:1057], T.TAB[0:7, 0:1057]) for k in range(1, 8)], [], [full("TAB", 1072)], 7)
-    late = [vw("TAB", 1060)]
-    ld("S", lambda: [(ap(vw("flI", s)), T.fl[:, 16 * s:16 * s + 16]) for s in range(2)], [], [two("flI")], 2)
+    for k in range(2):
+        ld("YS"[k], lambda k=k: [(T.TAB[16 * k:16 * k + 4, 33:1057], T.tbt[:, 0:32]), (T.TAB[16 * k + 8:16 * k + 11, 33:1057], T.tbt[0:96, 32:64])],
+           [full("tbt", 64), vw("TAB", 40)], [vw("tb", k)], 2)
+    for k in range(2):
+        n = 32 * k + 32
+        add({"V": 350 * CYC}, {"V": lambda n=n: g.vector.tensor_copy(T.TAB[n:2 * n, 33:733], T.TAB[0:n, 33:733])}, [vw("tb", 0, 2 + k)], [vw("tb", 2 + 2 * k)])
+        add({"S": 324 * CYC}, {"S": lambda n=n: g.scalar.activation(T.TAB[n:2 * n, 733:1057], T.TAB[0:n, 733:1057], COPY)}, [vw("tb", 0, 2), vw("tb", 3 * k)], [vw("tb", 3 + 2 * k)])
+    late = [vw("tb", 0, 2)]
     fill(vw("TT", 128, 512), 0.0)
     ld("S", lambda: [(T.TT[:, 0:128], T.tr[:])], [], [full("TT")])
     ld("Y", lambda: [(T.WC[:].bitcast(dt.uint8), T.wc[:]), (T.WCs[:], T.ws[:])], late, [full("WC", 512), full("WCs", 512)], 2)
@@ -242,15 +254,15 @@ def build(g, core, T, topo, nxt):
     fill(full("OF", 144), 0)
     for k, m in enumerate((16, 8, 2, 1)): iota(vw("bI", k), [[0, 1]], 0, m)
     ts(vw("BI", 0, 4), vw("bI", 0, 4), 4, 1, OP.arith_shift_right, OP.bitwise_and)
-    for k, (sh, m) in enumerate(((1, 6), (4, 7), (0, 15), (5, 3), (5, 1), (6, 1))): ts(vw("BI", 4 + k), vw("bI", 3), sh, m, OP.arith_shift_right, OP.bitwise_and)
+    for k, (sh, m) in enumerate(((1, 6), (4, 7), (0, 15), (5, 3), (5, 1), (6, 1), (0, 31))): ts(vw("BI", 4 + k), vw("bI", 3), sh, m, OP.arith_shift_right, OP.bitwise_and)
     cp(vw("BF", 0, 10), vw("BI", 0, 10))
-    sg, pr, i3, g0, ih, gF, iF, qF, q1, aF = [vw("BF", k) for k in range(10)]
-    for n, st, b in (("c02", 2, 0), ("c10", -1, 1), ("c16", 16, 1), ("c01", 1, 0)): iota(two(n), [[st, 2]], b, 0)
+    cp(vw("BF", 10), vw("BI", 10))
+    sg, pr, i3, g0, ih, gF, iF, qF, q1, aF, p31 = [vw("BF", k) for k in range(11)]
+    for n, st, b in (("c02", 2, 0), ("c10", -1, 1), ("c16", 16, 1), ("c00", 0, 0)): iota(two(n), [[st, 2]], b, 0)
     four = lambda n: vw(n, 0, 4)
     iota(four("cs"), [[0, 2], [2, 2]], -1, 0)
     iota(four("cc"), [[0, 2], [-1, 2]], 1, 0)
     ts(two("nW"), two("c16"), iF, None, OP.add)
-    ts(two("PM"), two("c01"), iF, iF, OP.add, OP.add)
     ts(four("g1"), four("cs"), g0, ih, OP.mult, OP.add)
     tt(four("g2"), four("g1"), four("cc"), OP.add)
     ts(four("u1"), four("g2"), -1.0, 16.0, OP.mult, OP.add)
@@ -284,7 +296,23 @@ def build(g, core, T, topo, nxt):
     tt(two("e8"), two("e6"), two("e7"), OP.add)
     cp(two("R2"), two("e8"))
     for p in range(2): iota(vw("O", PS * p + 1120, PS * p + 1152), [[0, 32]], 0, 0)
-    iota(full("STG", 32), [[0, 32]], 1, 0)
+
+    def spread():
+        turn32(full("MA", 64), full("RW", 64))
+        for k in range(8):
+            a, c, q = k // 4, k // 2 % 2, k // 4 * 2 + k % 2
+            move((T and T.MC[32 * q:32 * q + 32, 2 * c + a:32:8], T and T.MA[64 * a + 32 * c:64 * a + 32 * c + 32, 0:64:16]), [full("MA", 64), full("MC", 32)], [vw("mw", k)])
+        for a in range(2):
+            move((T and T.MC[64 - 64 * a:128 - 64 * a, a:32:2], T and T.MC[64 * a:64 * a + 64, a:32:2]), [vw("mw", 4 * a, 4 * a + 4)], [vw("mw", 8 + a)])
+        add({"V": 64 * CYC}, {"V": lambda: g.vector.transpose(T.TAB[:, 1:33], T.MC[:])}, [full("mw", 10), vw("tb", 0, 2)], [vw("TAB", 1, 33)])
+
+    iota(full("WN", 16), [[1, 16]], 0, 0, boost=30.0)
+    iota(full("MC", 32), [[0, 32]], 33, 0, boost=30.0)
+    ts(vw("MC", 7, 32, 16), two("c00"), p31, 1.0, OP.add, OP.add)
+    fill(two("cM"), 3.0 * 2 ** 31)
+    cp(four("FL"), four("flI"))
+    ts(full("RW", 64), ind(full("WN", 16), "FL", 0, 4), -33.0, 33.0, OP.mult, OP.add)
+    spread()
     fill(full("ET", 520), 0.0)
     add({"G": 0.2 + 1040 * CYC}, {"G": lambda: g.affine_select(T.ET[:], T.ET[:], [[1, 520]], OP.not_equal, 0.015625, -3, -4)}, [], [full("ET", 520)])
     for k in range(4): quant("EQ", 128 * k, "ET", 3 - k)
@@ -304,6 +332,7 @@ def build(g, core, T, topo, nxt):
     ts(full("cA", 4), full("kF", 4), -0.25, None, OP.mult)
     ts(full("cB", 4), full("kF", 4), 1.0 / 2048, None, OP.mult)
     fill(vw("ZS", 1408, 1424), 0.0)
+    fill(vw("FP", 1408, 1424), 0.0)
     fill(vw("CLT", 128, 512), 0.0)
     iota(full("MB", 33), [[1, 33]], -1, 0)
     iota(vw("MB", 33), [[0, 1]], -1, 0)
@@ -311,8 +340,7 @@ def build(g, core, T, topo, nxt):
 
     def came(t):
         fw, tv = "fw%d" % t, 4 * PW * t
-        if t < 2: ld("Y", lambda: [(T[fw][:], T["fdr%d" % t][:])], [two("fdr%d" % t)], [two(fw)])
-        tt(two(OCC[t + 1]), two(fw), two(OCC[t]), OP.is_le)
+        for s in range(2): ts(vw(OCC[t + 1], s), vw(fw, s), vw(OCC[t], s), None, OP.is_le)
         tt(two("tk"), two(OCC[t + 1]), two(OCC[t]), OP.subtract)
         for s in range(2): ts(vw("UL", s), vw("tk", s), CAME - 1.0, vw("nW", s), OP.mult, OP.add)
         lv, off = ((0, 0), (64, 96), (96, 96))[t]
@@ -333,9 +361,8 @@ def build(g, core, T, topo, nxt):
             scan(vw("SC", 144 * c, 144 * c + 117), ab, full("hd", 117), 0.0, OP.add, OP.mult)
         if t:
             came(t - 1)
-            fd = "fdr%d" % (t - 1)
-            ld("Y", lambda fd=fd: [(T.STG[16 * k:16 * k + 7, :], T[fd][0:112, :]) for k in range(8)], [two(fd)], [full("STG", 32)], 8)
-            tt(vw("TAB", 1, 33), ind(full("STG", 32), "PM", 0, 2), vw("TAB", 1, 33), OP.mult)
+            tt(full("RW", 64), ind(full("WN", 16), "fw%d" % (t - 1), 0, 4), full("RW", 64), OP.mult)
+            spread()
         for l in range(7):
             n = 8 - l
             for p in range(2):
@@ -347,17 +374,18 @@ def build(g, core, T, topo, nxt):
                         s0 = 144 * (2 * p + s)
                         ts(out, vw("SC", s0 + 20, s0 + 133, 16), vw("SC", s0 + 4), 544.5, OP.add, OP.add)
                     else:
-                        a = b0 + 16 * s + l - 1
+                        a = b0 + 16 * s + IP[l - 1]
                         ts(out, vw("O", a + 32, a + 32 * n + 1, 32), 32.0, vw("O", a), OP.mult, OP.add)
-                go = full("GO%d" % p, 32 * n)
-                cp(go, ind(full("TAB", TW), "OF", o0, o0 + 2 * n), "S")
+                go, h = full("GO%d" % p, 32 * n), n - SPLIT[l]
+                cp(vw(go[0], 0, 32 * h), ind(full("TAB", TW), "OF", o0, o0 + 2 * h), "S", more=[full("tb", 6)])
+                if h < n: cp(vw(go[0], 32 * h, 32 * n), ind(full("TAB", TW), "OF", o0 + 2 * h, o0 + 2 * n), "V", more=[full("tb", 6)])
                 turn32(vw("O", b1, b1 + 32 * n), go)
         for p in range(2):
             b = PS * p + 1056
-            tt(vw("O", b + 71, b + 96, 16), vw("O", b + 6, b + 32, 16), vw("O", b + 38, b + 64, 16), OP.max)
+            tt(vw("O", b + 71, b + 96, 16), vw("O", b + IP[6], b + 32, 16), vw("O", b + 32 + IP[6], b + 64, 16), OP.max)
         for k in range(4):
             mm(k, "EQ", 128 * k, "QX", 0, C)
-            if k < NF:
+            if k < NF or t == 2:
                 for j, n in CH: cp(vw("FP", C * k + j, C * k + j + n), vw("ps", 512 * k + j, 512 * k + j + n), "S")
         cp(full("AM", 64), ind(full("O", 2 * PS), "R1", 0, 4))
         turn32(full("TB", 64), full("AM", 64))
@@ -365,18 +393,16 @@ def build(g, core, T, topo, nxt):
         moves = [(2, 64 * a, 64 - 64 * a, 64) for a in range(2)] + [(x, 32 * q, 32 * ((q + x) % 4), 32) for x in (1, 3) for q in range(4)]
         for k, (x, p0, p1, np_) in enumerate(moves):
             a, b = 48 + 8 * (p1 // 64), 72 + 24 * x
-            io = lambda a=a, b=b, p0=p0, p1=p1, np_=np_: (T.AM[p1:p1 + np_, b:b + 24], T.AM[p0:p0 + np_, a:a + 24])
-            add({"V": 64 * CYC, "S": 64 * CYC}, {"V": lambda io=io: g.vector.tensor_copy(*io()), "S": lambda io=io: g.scalar.activation(*io(), COPY)}, [vw("AM", 48, 96)], [vw("mv", k)])
+            move((T and T.AM[p1:p1 + np_, b:b + 24], T and T.AM[p0:p0 + np_, a:a + 24]), [vw("AM", 48, 96)], [vw("mv", k)])
         add({"V": 0.05 + 48 * CYC}, {"V": lambda: g.vector.tensor_copy(T.L[:], T.AM[:].indirect(T.R2[:]))}, [full("AM", 96), two("R2"), full("mv", 10)], [full("L", 32)])
 
         lall = ("L", 0, 22)
         cp(full("JK", C), ind(full("WJ", 34), *lall), "S", acc=one("cnt"))
-        ts(one("rem"), one("cnt"), 3.0 * 2 ** 31, -3.0 * 2 ** 31, OP.add, OP.add)
+        ts(two("rem"), two("cM"), one("cnt"), -3.0 * 2 ** 31, OP.add, OP.add)
         wn = "w_%d" % t
-        ts(vw(wn, 0), one("cnt"), 0.0, vw(OCC[t], 0), OP.is_le, OP.max)
-        ts(vw(wn, 1), one("rem"), one("cnt"), vw(OCC[t], 1), OP.is_equal, OP.max)
-        fland = "fdr%d" % t if t < 2 else "fw2"
-        send(two(fland), two(wn), "rf%d" % t, boost=5.0)
+        ts(vw(wn, 0, 4, 2), two("c00"), one("cnt"), vw(OCC[t], 0), OP.is_ge, OP.max)
+        ts(vw(wn, 1, 4, 2), two("rem"), one("cnt"), vw(OCC[t], 1), OP.is_equal, OP.max)
+        send(four("fw%d" % t), four(wn), "rf%d" % t, boost=5.0)
 
         tv = 4 * PW * t
         for c, (j, n) in enumerate(CH):
@@ -399,9 +425,14 @@ def build(g, core, T, topo, nxt):
             b = min(a + PC, C)
             scan(vw("SA", a, b), vw("JK", a, b), vw("one", a, b), vw("SA", a - 1) if a else 160.0, OP.max, OP.add)
             scan(vw("SB", a, b), vw("JK", a, b), vw("stp", a, b), vw("SB", a - 1) if a else -160.0 / 512, OP.min, OP.add)
-        ts(vw("CL", 0, 8, 2), full("cA", 4), vw("SA", C - 1), -4.0, OP.add, OP.mult)
-        ts(vw("CL", 1, 8, 2), full("cB", 4), vw("SB", C - 1), 2048.0, OP.add, OP.mult)
-        for k in range(4): cp(vw("CLT", k, 128, 4), ind(full("ZS", 1412), "CL", 2 * k, 2 * k + 2), "S", 64.0)
+        if t < 2:
+            ts(vw("CL", 0, 8, 2), full("cA", 4), vw("SA", C - 1), -4.0, OP.add, OP.mult)
+            ts(vw("CL", 1, 8, 2), full("cB", 4), vw("SB", C - 1), 2048.0, OP.add, OP.mult)
+            for k in range(4): cp(vw("CLT", k, 128, 4), ind(full("ZS", 1412), "CL", 2 * k, 2 * k + 2), "VS", 64.0)
+        else:
+            ts(vw("CL", 0), vw("SA", C - 1), -1.0, 864.0, OP.mult, OP.add)
+            ts(vw("CL", 1), vw("SB", C - 1), 512.0, 864.0, OP.mult, OP.add)
+            for k in range(4): cp(vw("CLT", k, 128, 4), ind(vw("FP", C * k, C * k + C + 1), "CL", 0, 2), "VS", 64.0)
         cq, la = "CQ%d" % t, (0, 160, 192)[t]
         quant(cq, 0, "CLT", 0)
         send(vw("LC", la, la + 32) + ("c",), vw(cq, 0, 32) + ("c",), "rc%d" % t)

@@ -1,3 +1,4 @@
+from concourse.bass import DstId, RemoteDMATransfer
 from concourse.mybir import dt, AluOpType as OP, ActivationFunctionType as AF
 
 COPY = AF.Copy
@@ -10,7 +11,7 @@ TW = 1104
 IP = [0, 8, 2, 10, 1, 9, 3]
 SMALL = {"KI": "flI4 bI4 BI_11 GoI2 Gm2 al2 dI2 dm2 t1_2 qs2 gs2",
          "KF": "BF_11 c02_2 c10_2 c16_2 nW2 u1_4 u2_4 u3_4 k1_1 k2_1 k3_1 k4_1 ph1 phi1 be2 bm2 de2 e1_2 e2_2 e3_2 e4_2 e5_2 e6_2 e7_2 e8_2 kF4 cA4 cB4 c00_2 cs4 cc4 g1_4 g2_4 cM2",
-         "KL": "oca2 ocb2 occ2 ocd2 tk2 cnt1 rem2"}
+         "KL": "oca2 ocb2 occ2 ocd2 tk2 cnt1 rem2 cna1 rea2"}
 ALIAS = {}
 for _b, _s in SMALL.items():
     _k = 0
@@ -26,13 +27,13 @@ def _scratch():
     s = {}
     for d, names in ((i, "KI:48 tic:64"),
                      (f, "KF:96 KL:16 rr:128 ix:48 wa:48 wb:48 MB:48 SA:352 SB:352 RT:128 BPO:352 YO:352"),
-                     (u, "R1:4 R2:2 FL:4 OF:144 L:32 CL:8 UL:2 w_0:4 w_1:4 w_2:4 fw0:4 fw1:4 fw2:4"),
-                     (h, "hd:128 WJ:48 ET:520 tib:64 tbt:64 TAB:%d WN:16 RW:64 MA:64 MC:32 UT:512 VT:512 TT:512 XT:1408 AB:384 SC:432 GO0:256 GO1:256 O:%d AM:168 TB:64 TG:1408 "
+                     (u, "R1:4 R2:4 FL:4 OF:144 L:32 LA:32 CL:8 UL:2 wa0:4 wa1:4 fa0:4 fa1:4 w_0:4 w_1:4 w_2:4 fw0:4 fw1:4 fw2:4"),
+                     (h, "hd:128 WJ:48 ET:520 tib:64 tbt:64 TAB:%d WN:16 RW:128 MA:128 JKA:352 MC:32 UT:512 VT:512 TT:512 XT:1408 AB:384 SC:432 GO0:256 GO1:256 O:%d AM:168 TB:64 TG:1408 "
                          "ZS:1424 ZP:1408 TV:960 FP:1424 JK:352 one:352 stp:352 CLT:512" % (TW, 2 * PS))):
         for n in names.split():
             n, w = n.split(":")
             s[n] = ("sbuf", [128, int(w)], d)
-    for n in "EQ:512 QU:128 QV:128 WC:512 QX:352 QZ:352 CQ0:128 CQ1:128 CQ2:128 LC:224".split():
+    for n in "EQ:512 QU:128 QV:128 WC:512 QX:352 QZ:352 CQ0:128 CQ1:128 CQ2:128 LC:320".split():
         n, w = n.split(":")
         s[n] = ("sbuf", [128, int(w)], q)
         s[n + "s"] = ("sbuf", [128, int(w)], b)
@@ -41,13 +42,13 @@ def _scratch():
 
 
 SCRATCH = _scratch()
-SEMAPHORES = ["sV", "sS", "sT", "sG", "sent", "rf0", "rf1", "rf2", "rc0", "rc1", "rc2"] + ["d%d" % k for k in range(60)]
+SEMAPHORES = ["sV", "sS", "sT", "sG", "sent", "ra0", "ra1", "rf0", "rf1", "rf2", "rc0", "rc1", "rc2"] + ["d%d" % k for k in range(60)]
 PLAN = {}
 TRIES = 6000
-SPLIT = [3, 2, 2, 1, 1, 1, 0]
-PC = 118
+SPLIT = [[4, 3, 3, 2, 2, 1, 1], [4, 3, 3, 2, 2, 1, 1]]
+PC = [118, 118, 352]
 NF = 2
-WAKE, DMALAT, NETLAT, CYC, PECYC = 0.15, 2.0, 3.0, 0.00104, 0.0012
+WAKE, DMALAT, NETLAT, CYC, PECYC = 0.22, 1.8, 3.0, 0.00087, 0.001
 
 
 def bits(v):
@@ -108,7 +109,27 @@ def plan(ops):
         return seed[0] / 2147483648.0
     pr, pref = [prio[k] + ops[k]["boost"] - 1e-6 * k for k in range(n)], [0.4] * n
     best = place(pr, pref)
+
+    def back(order):
+        late, busy = [0.0] * n, {}
+        for k, q, _ in sorted(order, key=lambda o: -o[2] - ops[o[0]]["dur"][o[1]]):
+            du, bq = ops[k]["dur"][q], busy.setdefault(q, [])
+            st = max([late[j] for j in succ[k]] + [0.0]) + ops[k]["lat"]
+            i = len(bq)
+            while i and bq[i - 1][1] > st: i -= 1
+            while i < len(bq) and st + du > bq[i][0] + 1e-9:
+                st = max(st, bq[i][1])
+                i += 1
+            bq.insert(i, (st, st + du))
+            late[k] = st + du
+        return late
+
     for it in range(TRIES):
+        if it % 50 == 0:
+            p2, f2 = back(best[1]), list(pref)
+            for k, q, _ in best[1]: f2[k] = -5.0 if q == "V" else 5.0
+            r = place(p2, f2)
+            if r[0] < best[0]: best, pr, pref = r, p2, f2
         p2, f2 = list(pr), list(pref)
         for _ in range(1 + int(rnd() * 12)):
             k = int(rnd() * n)
@@ -218,6 +239,14 @@ def build(g, core, T, topo, nxt):
             g.remote_dma(ap(out), ap(in_), T.sem[sem], T.sem.sent, pid, rid, topo.mask(core, nxt))
         add({"G": 0.3}, {"G": fn}, [in_], [out], NETLAT, "n", (sem, ne), boost)
 
+    def send2(outs, ins, sem):
+        en = list(range(8)) if T is None else topo.engines(core, nxt)
+        def fn():
+            rid, pid = topo.addr(nxt, core)
+            g.remote_dma_fused([RemoteDMATransfer(dst_ids=[DstId(rid=rid, pnc=pid)], dma_engine_mask=sum(1 << e for e in en[k::2]), remote_sem=T.sem[sem], src=ap(ins[k]), dst=ap(outs[k]))
+                                for k in range(2)], local_sem=T.sem.sent)
+        add({"G": 0.3}, {"G": fn}, ins, outs, NETLAT, "n", (sem, len(en)))
+
     full = lambda n, w=128: vw(n, 0, w)
     two = lambda n: vw(n, 0, 2)
     one = lambda n: vw(n, 0)
@@ -295,24 +324,26 @@ def build(g, core, T, topo, nxt):
     tt(two("e7"), two("e4"), two("e5"), OP.add)
     tt(two("e8"), two("e6"), two("e7"), OP.add)
     cp(two("R2"), two("e8"))
-    for p in range(2): iota(vw("O", PS * p + 1120, PS * p + 1152), [[0, 32]], 0, 0)
+    for p in range(2): iota(vw("O", PS * p + 832, PS * p + 1152), [[0, 320]], 0, 0)
 
-    def spread():
-        turn32(full("MA", 64), full("RW", 64))
-        for k in range(8):
-            a, c, q = k // 4, k // 2 % 2, k // 4 * 2 + k % 2
-            move((T and T.MC[32 * q:32 * q + 32, 2 * c + a:32:8], T and T.MA[64 * a + 32 * c:64 * a + 32 * c + 32, 0:64:16]), [full("MA", 64), full("MC", 32)], [vw("mw", k)])
-        for a in range(2):
-            move((T and T.MC[64 - 64 * a:128 - 64 * a, a:32:2], T and T.MC[64 * a:64 * a + 64, a:32:2]), [vw("mw", 4 * a, 4 * a + 4)], [vw("mw", 8 + a)])
-        add({"V": 64 * CYC}, {"V": lambda: g.vector.transpose(T.TAB[:, 1:33], T.MC[:])}, [full("mw", 10), vw("tb", 0, 2)], [vw("TAB", 1, 33)])
+    def spread(a, put=True):
+        ma = vw("MA", 64 * a, 64 * a + 64)
+        turn32(ma, vw("RW", 64 * a, 64 * a + 64))
+        for k in range(4):
+            c, q = k // 2, 2 * a + k % 2
+            move((T and T.MC[32 * q:32 * q + 32, 2 * c + a:32:8], T and T.MA[64 * a + 32 * c:64 * a + 32 * c + 32, 64 * a:64 * a + 64:16]), [ma, full("MC", 32)], [vw("mw", 4 * a + k)])
+        move((T and T.MC[64 - 64 * a:128 - 64 * a, a:32:2], T and T.MC[64 * a:64 * a + 64, a:32:2]), [vw("mw", 4 * a, 4 * a + 4)], [vw("mw", 8 + a)])
+        if put: add({"V": 64 * CYC}, {"V": lambda: g.vector.transpose(T.TAB[:, 1:33], T.MC[:])}, [full("mw", 10), vw("tb", 0, 2)], [vw("TAB", 1, 33)])
 
     iota(full("WN", 16), [[1, 16]], 0, 0, boost=30.0)
     iota(full("MC", 32), [[0, 32]], 33, 0, boost=30.0)
     ts(vw("MC", 7, 32, 16), two("c00"), p31, 1.0, OP.add, OP.add)
     fill(two("cM"), 3.0 * 2 ** 31)
     cp(four("FL"), four("flI"))
-    ts(full("RW", 64), ind(full("WN", 16), "FL", 0, 4), -33.0, 33.0, OP.mult, OP.add)
-    spread()
+    for a in range(2):
+        ts(vw("RW", 64 * a, 64 * a + 64), ind(full("WN", 16), "FL", 0, 4), -33.0, 33.0, OP.mult, OP.add)
+        spread(a, a == 1)
+    iota(vw("AM", 96, 168), [[0, 72]], 0, 0)
     fill(full("ET", 520), 0.0)
     add({"G": 0.2 + 1040 * CYC}, {"G": lambda: g.affine_select(T.ET[:], T.ET[:], [[1, 520]], OP.not_equal, 0.015625, -3, -4)}, [], [full("ET", 520)])
     for k in range(4): quant("EQ", 128 * k, "ET", 3 - k)
@@ -352,67 +383,69 @@ def build(g, core, T, topo, nxt):
             if t < 2: cp(vw("TV", tv + PW * (k + 4) + 1, tv + PW * (k + 4) + 33), win, "VS")
             else: cp(vw("RT", k, 128, 4), win, "VS", -64.0)
 
-    for t in range(3):
-        for j, n in CH: quant("QX", j, "XT", 4 * j, n)
-        for c in range(3):
-            mm(4 + c, "QX", SL[c], "QU", 0)
-            ab, pv = vw("AB", 128 * c, 128 * c + 117), vw("ps", 512 * (4 + c), 512 * (4 + c) + 117)
-            add({"S": 117 * CYC}, {"S": lambda ab=ab, pv=pv: g.scalar.activation(ap(ab), ap(pv), AF.Sign, bias=-1e-36)}, [pv], [ab])
-            scan(vw("SC", 144 * c, 144 * c + 117), ab, full("hd", 117), 0.0, OP.add, OP.mult)
-        if t:
-            came(t - 1)
-            tt(full("RW", 64), ind(full("WN", 16), "fw%d" % (t - 1), 0, 4), full("RW", 64), OP.mult)
-            spread()
-        for l in range(7):
-            n = 8 - l
-            for p in range(2):
-                o0, b0, b1 = 72 * p + l * (17 - l), PS * p + 16 * (l - 1) * (18 - l), PS * p + 16 * l * (17 - l)
-                for s in range(2):
-                    if p == 1 and s == 1 and l % 2 == 0: continue
-                    out = vw("OF", o0 + s, o0 + 2 * n, 2)
-                    if l == 0:
-                        s0 = 144 * (2 * p + s)
-                        ts(out, vw("SC", s0 + 20, s0 + 133, 16), vw("SC", s0 + 4), 544.5, OP.add, OP.add)
-                    else:
-                        a = b0 + 16 * s + IP[l - 1]
-                        ts(out, vw("O", a + 32, a + 32 * n + 1, 32), 32.0, vw("O", a), OP.mult, OP.add)
-                go, h = full("GO%d" % p, 32 * n), n - SPLIT[l]
-                cp(vw(go[0], 0, 32 * h), ind(full("TAB", TW), "OF", o0, o0 + 2 * h), "S", more=[full("tb", 6)])
-                if h < n: cp(vw(go[0], 32 * h, 32 * n), ind(full("TAB", TW), "OF", o0 + 2 * h, o0 + 2 * n), "V", more=[full("tb", 6)])
-                turn32(vw("O", b1, b1 + 32 * n), go)
-        for p in range(2):
-            b = PS * p + 1056
-            tt(vw("O", b + 71, b + 96, 16), vw("O", b + IP[6], b + 32, 16), vw("O", b + 32 + IP[6], b + 64, 16), OP.max)
-        for k in range(4):
-            mm(k, "EQ", 128 * k, "QX", 0, C)
-            if k < NF or t == 2:
-                for j, n in CH: cp(vw("FP", C * k + j, C * k + j + n), vw("ps", 512 * k + j, 512 * k + j + n), "S")
+    def filled(fw, a):
+        tt(vw("RW", 64 * a, 64 * a + 64), ind(full("WN", 16), fw, 0, 4), vw("RW", 64 * a, 64 * a + 64), OP.mult)
+        spread(a)
+
+    def turn(a0, a1, lst):
         cp(full("AM", 64), ind(full("O", 2 * PS), "R1", 0, 4))
         turn32(full("TB", 64), full("AM", 64))
         turn32(vw("AM", 64, 96), vw("TB", 16, 48))
         moves = [(2, 64 * a, 64 - 64 * a, 64) for a in range(2)] + [(x, 32 * q, 32 * ((q + x) % 4), 32) for x in (1, 3) for q in range(4)]
         for k, (x, p0, p1, np_) in enumerate(moves):
             a, b = 48 + 8 * (p1 // 64), 72 + 24 * x
-            move((T and T.AM[p1:p1 + np_, b:b + 24], T and T.AM[p0:p0 + np_, a:a + 24]), [vw("AM", 48, 96)], [vw("mv", k)])
-        add({"V": 0.05 + 48 * CYC}, {"V": lambda: g.vector.tensor_copy(T.L[:], T.AM[:].indirect(T.R2[:]))}, [full("AM", 96), two("R2"), full("mv", 10)], [full("L", 32)])
+            if a0 <= p1 // 64 < a1: move((T and T.AM[p1:p1 + np_, b:b + 24], T and T.AM[p0:p0 + np_, a:a + 24]), [vw("AM", 48, 96), vw("AM", 100)], [vw("mv", k)])
+        cp(full(lst, 32), ind(full("AM", 168), "R2", 0, 2), more=[full("mv", 10)])
 
-        lall = ("L", 0, 22)
-        cp(full("JK", C), ind(full("WJ", 34), *lall), "S", acc=one("cnt"))
-        ts(two("rem"), two("cM"), one("cnt"), -3.0 * 2 ** 31, OP.add, OP.add)
-        wn = "w_%d" % t
-        ts(vw(wn, 0, 4, 2), two("c00"), one("cnt"), vw(OCC[t], 0), OP.is_ge, OP.max)
-        ts(vw(wn, 1, 4, 2), two("rem"), one("cnt"), vw(OCC[t], 1), OP.is_equal, OP.max)
-        send(four("fw%d" % t), four(wn), "rf%d" % t, boost=5.0)
+    def flags(t, lst, jk, cnt, rem, wn, land, sem):
+        cp(full(jk, C), ind(full("WJ", 34), lst, 0, 22), "S", acc=one(cnt))
+        ts(two(rem), two("cM"), one(cnt), -3.0 * 2 ** 31, OP.add, OP.add)
+        ts(vw(wn, 0, 4, 2), two("c00"), one(cnt), vw(OCC[t], 0), OP.is_ge, OP.max)
+        ts(vw(wn, 1, 4, 2), two(rem), one(cnt), vw(OCC[t], 1), OP.is_equal, OP.max)
+        send(four(land), four(wn), sem)
 
+    def images(t):
+        for j, n in CH: quant("QX", j, "XT", 4 * j, n)
+        for c in range(3):
+            mm(4 + c, "QX", SL[c], "QU", 0)
+            ab, pv = vw("AB", 128 * c, 128 * c + 117), vw("ps", 512 * (4 + c), 512 * (4 + c) + 117)
+            add({"S": 117 * CYC}, {"S": lambda ab=ab, pv=pv: g.scalar.activation(ap(ab), ap(pv), AF.Sign, bias=-1e-36)}, [pv], [ab])
+            scan(vw("SC", 144 * c, 144 * c + 117), ab, full("hd", 117), 0.0, OP.add, OP.mult)
+        for k in range(4):
+            mm(k, "EQ", 128 * k, "QX", 0, C)
+            if k < NF or t == 2:
+                for j, n in CH: cp(vw("FP", C * k + j, C * k + j + n), vw("ps", 512 * k + j, 512 * k + j + n), "S")
+
+    def level(t, p, l):
+        n = 8 - l
+        o0, b0, b1 = 72 * p + l * (17 - l), PS * p + 16 * (l - 1) * (18 - l), PS * p + 16 * l * (17 - l)
+        for s in range(2):
+            if p == 1 and s == 1 and l % 2 == 0: continue
+            out = vw("OF", o0 + s, o0 + 2 * n, 2)
+            if l == 0:
+                s0 = 144 * (2 * p + s)
+                ts(out, vw("SC", s0 + 20, s0 + 133, 16), vw("SC", s0 + 4), 544.5, OP.add, OP.add)
+            else:
+                a = b0 + 16 * s + IP[l - 1]
+                ts(out, vw("O", a + 32, a + 32 * n + 1, 32), 32.0, vw("O", a), OP.mult, OP.add)
+        go, h = full("GO%d" % p, 32 * n), n - SPLIT[p][l]
+        if h: cp(vw(go[0], 0, 32 * h), ind(full("TAB", TW), "OF", o0, o0 + 2 * h), "S", more=[full("tb", 6)])
+        if h < n: cp(vw(go[0], 32 * h, 32 * n), ind(full("TAB", TW), "OF", o0 + 2 * h, o0 + 2 * n), "V", more=[full("tb", 6)])
+        turn32(vw("O", b1, b1 + 32 * n), go)
+        if l == 6:
+            b = PS * p + 1056
+            tt(vw("O", b + 71, b + 96, 16), vw("O", b + IP[6], b + 32, 16), vw("O", b + 32 + IP[6], b + 64, 16), OP.max)
+
+    def layer(t):
         tv = 4 * PW * t
-        for c, (j, n) in enumerate(CH):
+        for j, n in CH:
             for k in range(4):
-                tg, z = vw("TG", C * k + j, C * k + j + n), vw("ZS", 4 * j + k, 4 * j + 4 * n, 4)
+                tg, z, b = vw("TG", C * k + j, C * k + j + n), vw("ZS", 4 * j + k, 4 * j + 4 * n, 4), 512 * k + j
                 pick = ind(vw("TV", tv + PW * k, tv + PW * k + CAME), "L", j // 16, (j + n) // 16)
                 if k < NF: tt(z, pick, vw("FP", C * k + j, C * k + j + n), OP.add)
                 else:
                     cp(tg, pick, "S")
-                    tt(z, vw("ps", 512 * k + j, 512 * k + j + n), tg, OP.add)
+                    tt(z, vw("ps", b, b + n), tg, OP.add)
             quant("QZ", j, "ZS", 4 * j, n)
             cp(vw("ZP", 4 * j, 4 * j + 4 * n), vw("ZS", 4 * j, 4 * j + 4 * n), "VS", 64.0)
         for c, (j, n) in enumerate(CH):
@@ -421,8 +454,23 @@ def build(g, core, T, topo, nxt):
                 mm(b, "WC", 128 * k, "QZ", j, n)
                 tt(vw("XT", 4 * j + k, 4 * j + 4 * n, 4), vw("ps", 512 * b, 512 * b + n), vw("ZP", 4 * j + k, 4 * j + 4 * n, 4), OP.add)
 
-        for a in range(0, C, PC):
-            b = min(a + PC, C)
+    for t in range(3):
+        images(t)
+        if t:
+            came(t - 1)
+            filled("fa%d" % (t - 1), 0)
+        for l in range(7):
+            if l == 4 and t < 2:
+                turn(0, 1, "LA")
+                flags(t, "LA", "JKA", "cna", "rea", "wa%d" % t, "fa%d" % t, "ra%d" % t)
+            if l == 4 and t: filled("fw%d" % (t - 1), 1)
+            for p in range(2): level(t, p, l)
+        turn(int(t < 2), 2, "L")
+        flags(t, "L", "JK", "cnt", "rem", "w_%d" % t, "fw%d" % t, "rf%d" % t)
+        layer(t)
+
+        for a in range(0, C, PC[t]):
+            b = min(a + PC[t], C)
             scan(vw("SA", a, b), vw("JK", a, b), vw("one", a, b), vw("SA", a - 1) if a else 160.0, OP.max, OP.add)
             scan(vw("SB", a, b), vw("JK", a, b), vw("stp", a, b), vw("SB", a - 1) if a else -160.0 / 512, OP.min, OP.add)
         if t < 2:
@@ -435,8 +483,10 @@ def build(g, core, T, topo, nxt):
             for k in range(4): cp(vw("CLT", k, 128, 4), ind(vw("FP", C * k, C * k + C + 1), "CL", 0, 2), "VS", 64.0)
         cq, la = "CQ%d" % t, (0, 160, 192)[t]
         quant(cq, 0, "CLT", 0)
-        send(vw("LC", la, la + 32) + ("c",), vw(cq, 0, 32) + ("c",), "rc%d" % t)
-        send(vw("LCs", la, la + 32), vw(cq + "s", 0, 32), "rc%d" % t)
+        if t < 2:
+            send(vw("LC", la, la + 32) + ("c",), vw(cq, 0, 32) + ("c",), "rc%d" % t)
+            send(vw("LCs", la, la + 32), vw(cq + "s", 0, 32), "rc%d" % t)
+        else: send2([vw("LC", la, la + 32) + ("c",), vw("LCs", la, la + 128)], [vw(cq, 0, 32) + ("c",), vw(cq + "s", 0, 128)], "rc%d" % t)
 
     came(2)
     cp(full("BPO", C), ind(full("MB", 34), "L", 0, 22), "S")

@@ -3,7 +3,8 @@ from concourse.mybir import dt, AluOpType as OP, ActivationFunctionType as AF
 
 COPY = AF.Copy
 C = 352
-CH = [(0, 224), (224, 128)]
+CH = [(0, 128), (128, 224)]
+ZC = [(0, 128, (4, 5, 6, 7)), (128, 224, (0, 1, 2, 3))]
 SL = [0, 128, 224]
 PW, CAME = 80, 34
 PS = 1152
@@ -11,7 +12,7 @@ TW = 1104
 IP = [0, 8, 2, 10, 1, 9, 3]
 SMALL = {"KI": "flI4 bI4 BI_11 GoI2 Gm2 al2 dI2 dm2 t1_2 qs2 gs2",
          "KF": "BF_11 c02_2 c10_2 c16_2 nW2 u1_4 u2_4 u3_4 k1_1 k2_1 k3_1 k4_1 ph1 phi1 be2 bm2 de2 e1_2 e2_2 e3_2 e4_2 e5_2 e6_2 e7_2 e8_2 kF4 cA4 cB4 c00_2 cs4 cc4 g1_4 g2_4 cM2",
-         "KL": "oca2 ocb2 occ2 ocd2 tk2 cnt1 rem2 cna1 rea2"}
+         "KL": "oca2 ocb2 occ2 ocd2 tk2 cnt1 rem2 cna1 rea2 rem0_2 rea0_2 cN1"}
 ALIAS = {}
 for _b, _s in SMALL.items():
     _k = 0
@@ -25,15 +26,15 @@ OCC = ["oca", "ocb", "occ", "ocd"]
 def _scratch():
     f, h, i, u, q, b = "float32", "bfloat16", "int32", "uint16", "float8_e4m3fn_x4", "uint8"
     s = {}
-    for d, names in ((i, "KI:48 tic:64"),
-                     (f, "KF:96 KL:16 rr:128 ix:48 wa:48 wb:48 MB:48 SA:352 SB:352 RT:128 BPO:352 YO:352"),
+    for d, names in ((i, "KI:48 tic:64 TI:1024"),
+                     (f, "KF:96 KL:24 rr:128 ix:48 wa:48 wb:48 MB:48 SA:352 SB:352 RT:128 BPO:352 YO:352"),
                      (u, "R1:4 R2:4 FL:4 OF:144 L:32 LA:32 CL:8 UL:2 wa0:4 wa1:4 fa0:4 fa1:4 w_0:4 w_1:4 w_2:4 fw0:4 fw1:4 fw2:4"),
-                     (h, "hd:128 WJ:48 ET:520 tib:64 tbt:64 TAB:%d WN:16 RW:128 MA:128 JKA:352 MC:32 UT:512 VT:512 TT:512 XT:1408 AB:384 SC:432 GO0:256 GO1:256 O:%d AM:168 TB:64 TG:1408 "
-                         "ZS:1424 ZP:1408 TV:960 FP:1424 JK:352 one:352 stp:352 CLT:512" % (TW, 2 * PS))):
+                     (h, "hd:128 h0:128 TK:48 WJ:48 ET:520 tib:64 tbt:64 TAB:%d WN:16 RW:128 MA:128 JKA:352 MC:32 UT:512 VT:512 TT:512 XT:1408 AB:384 SC:432 GO0:256 GO1:256 O:%d AM:360 TB:64 CW:256 TG:1408 "
+                         "ZS:1424 ZP:1408 TV:960 FP:1424 JK:352 one:520 stp:352 CLT:512" % (TW, 2 * PS))):
         for n in names.split():
             n, w = n.split(":")
             s[n] = ("sbuf", [128, int(w)], d)
-    for n in "EQ:512 QU:128 QV:128 WC:512 QX:352 QZ:352 CQ0:128 CQ1:128 CQ2:128 LC:320".split():
+    for n in "EQ:512 QU:128 QV:128 WC:512 QX:352 QZ:384 CQ0:128 CQ1:128 CQ2:128 LC:320".split():
         n, w = n.split(":")
         s[n] = ("sbuf", [128, int(w)], q)
         s[n + "s"] = ("sbuf", [128, int(w)], b)
@@ -44,11 +45,15 @@ def _scratch():
 SCRATCH = _scratch()
 SEMAPHORES = ["sV", "sS", "sT", "sG", "sent", "ra0", "ra1", "rf0", "rf1", "rf2", "rc0", "rc1", "rc2"] + ["d%d" % k for k in range(60)]
 PLAN = {}
-TRIES = 6000
+TRIES = 600
+TRIES2, HEAT = 22000, 0.05
 SPLIT = [[4, 3, 3, 2, 2, 1, 1], [4, 3, 3, 2, 2, 1, 1]]
 PC = [118, 118, 352]
-NF = 2
-WAKE, DMALAT, NETLAT, CYC, PECYC = 0.22, 1.8, 3.0, 0.00087, 0.001
+NF = [3, 3, 2]
+DUE = 9
+EARLY = {"a": 0.8, "f": 1.0, "c": 1.0}
+CASES = [(0.2, 1.9, 2.8, 1.0), (0.22, 1.8, 3.2, 1.0), (0.23, 2.0, 4.0, 1.2)]
+WAKE, DMALAT, NETLAT, CYC, PECYC = 0.22, 1.9, 3.0, 0.00083, 0.0012
 
 
 def bits(v):
@@ -71,15 +76,22 @@ def plan(ops):
         for buf, m, w in acc:
             hist.setdefault(buf, []).append((m, k, w))
         deps.append(sorted(d))
+    anc, near = [0] * n, []
+    for k in range(n):
+        far = 0
+        for x in deps[k]: far |= anc[x]
+        near.append([x for x in deps[k] if not far >> x & 1])
+        for x in deps[k]: far |= 1 << x
+        anc[k] = far
     succ = [[] for _ in ops]
     for k in range(n):
-        for j in deps[k]: succ[j].append(k)
+        for j in near[k]: succ[j].append(k)
     prio = [0.0] * n
     for k in range(n - 1, -1, -1):
         prio[k] = min(ops[k]["dur"].values()) + ops[k]["lat"] + max([prio[j] for j in succ[k]] + [0.0])
 
     def place(pr, pref):
-        left = [len(d) for d in deps]
+        left = [len(d) for d in near]
         ready = {k: 0.0 for k in range(n) if not left[k]}
         busy, fin, order = {}, [0.0] * n, []
         while ready:
@@ -100,10 +112,21 @@ def plan(ops):
             order.append((k, q, st))
             for j in succ[k]:
                 left[j] -= 1
-                if not left[j]: ready[j] = max(fin[x] for x in deps[j])
-        return max(fin) + 1e-4 * sum(fin) / n, sorted(order, key=lambda o: o[2])
+                if not left[j]: ready[j] = max(fin[x] for x in near[j])
+        order.sort(key=lambda o: o[2])
+        tot = 0.0
+        for w, d, r, f in CASES:
+            lat, free = {"c": w, "d": d, "n": r}, {}
+            for k, q, _ in order:
+                st = free.get(q, 0.0)
+                for x in near[k]:
+                    if fin[x] > st: st = fin[x]
+                free[q] = st + f * ops[k]["dur"][q]
+                fin[k] = free[q] + lat[ops[k]["kind"]]
+            tot += max(fin) / len(CASES)
+        return tot + 1e-4 * sum(fin) / n, order
 
-    seed = [12345]
+    seed = [3]
     def rnd():
         seed[0] = (seed[0] * 1103515245 + 12345) % 2147483648
         return seed[0] / 2147483648.0
@@ -137,7 +160,53 @@ def plan(ops):
             if len(ops[k]["dur"]) > 1: f2[k] = (rnd() - 0.5) * 0.8
         r = place(p2, f2)
         if r[0] <= best[0]: best, pr, pref = r, p2, f2
-    return best[1], deps, best[0]
+
+    lats = [([{"c": w, "d": d, "n": r}[o["kind"]] for o in ops], f) for w, d, r, f in CASES]
+
+    def run(order):
+        tot, chains = 0.0, []
+        for lat, f in lats:
+            fin, by, free, last = [0.0] * n, [None] * n, {}, {}
+            for k, q in order:
+                st, b = free.get(q, 0.0), last.get(q)
+                for x in near[k]:
+                    if fin[x] > st: st, b = fin[x], x
+                free[q] = st = st + f * ops[k]["dur"][q]
+                fin[k], by[k], last[q] = st + lat[k], b, k
+            k = max(range(n), key=lambda x: fin[x])
+            tot += fin[k] / len(lats) + 2e-5 * sum(fin) / n
+            chains.append((k, by))
+        return tot, chains
+
+    order = [(k, q) for k, q, _ in best[1]]
+    now, chains = run(order)
+    top = (now, order)
+    for it in range(TRIES2):
+        k, by = chains[int(rnd() * len(chains))]
+        pairs = []
+        while by[k] is not None:
+            if not anc[k] >> by[k] & 1: pairs.append((by[k], k))
+            k = by[k]
+        if not pairs: break
+        j, k = pairs[int(rnd() * len(pairs))]
+        pos = {x: i for i, (x, _) in enumerate(order)}
+        a, b, u = pos[j], pos[k], rnd()
+        if u < 0.3 and (len(ops[j]["dur"]) > 1 or len(ops[k]["dur"]) > 1):
+            i = a if len(ops[j]["dur"]) > 1 and (len(ops[k]["dur"]) == 1 or u < 0.15) else b
+            new = list(order)
+            new[i] = (order[i][0], "S" if order[i][1] == "V" else "V")
+        elif u < 0.65:
+            mid = order[a:b + 1]
+            new = order[:a] + [o for o in mid if o[0] == k or anc[k] >> o[0] & 1] + [o for o in mid if not (o[0] == k or anc[k] >> o[0] & 1)] + order[b + 1:]
+        else:
+            b = min(n - 1, b + int(rnd() * 12))
+            mid = order[a:b + 1]
+            new = order[:a] + [o for o in mid if not (o[0] == j or anc[o[0]] >> j & 1)] + [o for o in mid if o[0] == j or anc[o[0]] >> j & 1] + order[b + 1:]
+        r, c = run(new)
+        if r <= now + HEAT * (1.0 - it / TRIES2) * rnd():
+            now, chains, order = r, c, new
+            if r < top[0]: top = (r, new)
+    return [(k, q, 0.0) for k, q in top[1]], deps, top[0]
 
 
 def build(g, core, T, topo, nxt):
@@ -175,7 +244,7 @@ def build(g, core, T, topo, nxt):
         return len(v) > 4 and v[4] != "c"
 
     def gat(v, c):
-        return c + num(v) * 1.5 * CYC
+        return c + num(v) * 1.56 * CYC
 
     def ts(out, in0, s1, s2, op0, op1=None, boost=0.0):
         sc = [s for s in (s1, s2) if isinstance(s, tuple)]
@@ -191,6 +260,11 @@ def build(g, core, T, topo, nxt):
         add(dur, fns, [in0] + sc, [out], boost=boost)
 
     def tt(out, a, b, op):
+        if out[0][0] in "egu" and out[0] in ALIAS:
+            for c in range(out[2]):
+                if op == OP.subtract: ts(vw(out[0], c), vw(b[0], c), -1.0, vw(a[0], c), OP.mult, OP.add)
+                else: ts(vw(out[0], c), vw(a[0], c), vw(b[0], c), None, op)
+            return
         d = gat(out, 0.05) if isind(a) else cost(out, 1.0 if a[0] == "ps" else 2.0)
         add({"V": d}, {"V": lambda: g.vector.tensor_tensor(ap(out), ap(a), ap(b), op)}, [a, b], [out])
 
@@ -213,12 +287,14 @@ def build(g, core, T, topo, nxt):
     def move(io, ins, outs):
         add({"V": 64 * CYC, "S": 64 * CYC}, {"V": lambda: g.vector.tensor_copy(*io), "S": lambda: g.scalar.activation(*io, COPY)}, ins, outs)
 
-    def fill(out, val, boost=0.0):
-        add({"V": cost(out, 1.0 if wide(out) else 0.5)}, {"V": lambda: g.vector.memset(ap(out), val)}, [], [out], boost=boost)
+    def fill(out, val, boost=0.0, q="V"):
+        src = vw("one", 0, num(out))
+        add({k: cost(out, 1.0 if k == "S" or wide(out) else 0.5) for k in q},
+            {"V": lambda: g.vector.memset(ap(out), val), "S": lambda: g.scalar.activation(ap(out), ap(src), COPY, scale=val)}, [src] if "S" in q else [], [out], boost=boost)
 
     def quant(q, a, t, ta, n=128):
         c, s, i = vw(q, a, a + n), vw(q + "s", a, a + n), vw(t, ta, ta + 4 * n)
-        add({"V": 0.015 + 1.05e-3 * n}, {"V": lambda: g.vector.quantize_mx(ap(c), ap(s), ap(i))}, [i], [c, s])
+        add({"V": 0.012 + 0.88e-3 * n}, {"V": lambda: g.vector.quantize_mx(ap(c), ap(s), ap(i))}, [i], [c, s])
 
     def mm(bank, lq, la, rq, ra, n=128):
         o = vw("ps", 512 * bank, 512 * bank + n)
@@ -237,7 +313,7 @@ def build(g, core, T, topo, nxt):
         def fn():
             rid, pid = topo.addr(nxt, core)
             g.remote_dma(ap(out), ap(in_), T.sem[sem], T.sem.sent, pid, rid, topo.mask(core, nxt))
-        add({"G": 0.3}, {"G": fn}, [in_], [out], NETLAT, "n", (sem, ne), boost)
+        add({"G": 0.3}, {"G": fn}, [in_], [out], NETLAT + EARLY[sem[1]], "n", (sem, ne), boost)
 
     def send2(outs, ins, sem):
         en = list(range(8)) if T is None else topo.engines(core, nxt)
@@ -258,18 +334,22 @@ def build(g, core, T, topo, nxt):
         v = vw("XT", 4 * j, 4 * j + 4 * n)
         ld("S", lambda v=v: [(ap(v), T.x[:, v[1]:v[2]])], [], [v], boost=45.0 - 2 * c)
     ld("S", lambda: [(T.UT[:], T.u[:])], [], [full("UT", 512)], boost=44.0)
-    fill(full("TAB", TW), 33.0, boost=50.0)
+    fill(full("one", 520), 1.0, boost=60.0)
+    fill(full("TAB", 1057), 0.0, boost=50.0)
+    fill(vw("TAB", 1057, TW), 33.0)
     ts(full("tib", 64), full("tic", 64), 1.0, None, OP.add)
     turn32(full("tbt", 64), full("tib", 64))
     for k in range(2):
         ld("YS"[k], lambda k=k: [(T.TAB[16 * k:16 * k + 4, 33:1057], T.tbt[:, 0:32]), (T.TAB[16 * k + 8:16 * k + 11, 33:1057], T.tbt[0:96, 32:64])],
-           [full("tbt", 64), vw("TAB", 40)], [vw("tb", k)], 2)
+           [full("tbt", 64), vw("TAB", 40), vw("TAB", 1060)], [vw("tb", k)], 2)
     for k in range(2):
         n = 32 * k + 32
         add({"V": 350 * CYC}, {"V": lambda n=n: g.vector.tensor_copy(T.TAB[n:2 * n, 33:733], T.TAB[0:n, 33:733])}, [vw("tb", 0, 2 + k)], [vw("tb", 2 + 2 * k)])
         add({"S": 324 * CYC}, {"S": lambda n=n: g.scalar.activation(T.TAB[n:2 * n, 733:1057], T.TAB[0:n, 733:1057], COPY)}, [vw("tb", 0, 2), vw("tb", 3 * k)], [vw("tb", 3 + 2 * k)])
     late = [vw("tb", 0, 2)]
-    fill(vw("TT", 128, 512), 0.0)
+    fill(full("TI", 1024), 0, boost=55.0)
+    for q in range(2): ld("YS"[q], lambda q=q: [(T.TI[16 * k:16 * k + 1, :], T.ti[0:1, :]) for k in range(q, 8, 2)], [vw("TI", 0)], [vw("tj", q)], 4, boost=50.0)
+    fill(vw("TT", 128, 512), 0.0, q="S")
     ld("S", lambda: [(T.TT[:, 0:128], T.tr[:])], [], [full("TT")])
     ld("Y", lambda: [(T.WC[:].bitcast(dt.uint8), T.wc[:]), (T.WCs[:], T.ws[:])], late, [full("WC", 512), full("WCs", 512)], 2)
     ld("Y", lambda: [(T.VT[:], T.v[:])], late, [full("VT", 512)])
@@ -277,20 +357,23 @@ def build(g, core, T, topo, nxt):
     quant("QU", 0, "UT", 0)
     iota(full("rr"), [[0, 8], [1, 16]], 0, 0, boost=30.0)
     ts(full("hd"), full("rr"), 4.0, 2.0, OP.is_lt, OP.mult)
-    fill(vw("hd", 4, 128, 16), 16.0)
-    fill(vw("hd", 4), 0.5)
-    fill(vw("SC", 132, 432, 144), -528.0)
+    fill(vw("hd", 20, 128, 16), 16.0, q="S")
+    fill(vw("hd", 4), 0.5, q="S")
+    ts(full("h0"), full("rr"), 4.0, 2.0, OP.is_lt, OP.mult)
+    fill(vw("h0", 20, 128, 16), 0.5, q="S")
+    fill(vw("h0", 4), 16.0, q="S")
+    fill(vw("SC", 132, 432, 144), -528.0, q="S")
     fill(full("OF", 144), 0)
-    for k, m in enumerate((16, 8, 2, 1)): iota(vw("bI", k), [[0, 1]], 0, m)
+    for k, m in enumerate((16, 8, 2, 1)): iota(vw("bI", k), [[0, 1]], 0, m, boost=60.0)
     ts(vw("BI", 0, 4), vw("bI", 0, 4), 4, 1, OP.arith_shift_right, OP.bitwise_and)
     for k, (sh, m) in enumerate(((1, 6), (4, 7), (0, 15), (5, 3), (5, 1), (6, 1), (0, 31))): ts(vw("BI", 4 + k), vw("bI", 3), sh, m, OP.arith_shift_right, OP.bitwise_and)
     cp(vw("BF", 0, 10), vw("BI", 0, 10))
     cp(vw("BF", 10), vw("BI", 10))
     sg, pr, i3, g0, ih, gF, iF, qF, q1, aF, p31 = [vw("BF", k) for k in range(11)]
-    for n, st, b in (("c02", 2, 0), ("c10", -1, 1), ("c16", 16, 1), ("c00", 0, 0)): iota(two(n), [[st, 2]], b, 0)
+    for n, st, b in (("c02", 2, 0), ("c10", -1, 1), ("c16", 16, 1), ("c00", 0, 0)): iota(two(n), [[st, 2]], b, 0, boost=20.0)
     four = lambda n: vw(n, 0, 4)
-    iota(four("cs"), [[0, 2], [2, 2]], -1, 0)
-    iota(four("cc"), [[0, 2], [-1, 2]], 1, 0)
+    iota(four("cs"), [[0, 2], [2, 2]], -1, 0, boost=20.0)
+    iota(four("cc"), [[0, 2], [-1, 2]], 1, 0, boost=20.0)
     ts(two("nW"), two("c16"), iF, None, OP.add)
     ts(four("g1"), four("cs"), g0, ih, OP.mult, OP.add)
     tt(four("g2"), four("g1"), four("cc"), OP.add)
@@ -323,7 +406,19 @@ def build(g, core, T, topo, nxt):
     tt(two("e6"), two("e3"), two("e2"), OP.add)
     tt(two("e7"), two("e4"), two("e5"), OP.add)
     tt(two("e8"), two("e6"), two("e7"), OP.add)
-    cp(two("R2"), two("e8"))
+    ts(two("qs"), two("Gm"), 1, None, OP.arith_shift_right)
+    ts(two("e1"), two("qs"), -48.0, 313.0, OP.mult, OP.add)
+    ts(two("e2"), two("c02"), 12.0, g0, OP.mult, OP.subtract)
+    ts(two("e3"), two("be"), g0, 16.0, OP.not_equal, OP.mult)
+    ts(two("e4"), two("al"), 4.0, None, OP.mult)
+    tt(two("e5"), two("e1"), two("e2"), OP.add)
+    tt(two("e6"), two("e3"), two("e4"), OP.add)
+    tt(two("e7"), two("e5"), two("e6"), OP.add)
+    tt(two("e1"), two("e7"), two("e8"), OP.subtract)
+    ts(one("k1"), qF, 3.0, None, OP.is_equal)
+    ts(two("e2"), two("e1"), one("k1"), None, OP.mult)
+    tt(two("e3"), two("e2"), two("e8"), OP.add)
+    cp(two("R2"), two("e3"))
     for p in range(2): iota(vw("O", PS * p + 832, PS * p + 1152), [[0, 320]], 0, 0)
 
     def spread(a, put=True):
@@ -338,33 +433,36 @@ def build(g, core, T, topo, nxt):
     iota(full("WN", 16), [[1, 16]], 0, 0, boost=30.0)
     iota(full("MC", 32), [[0, 32]], 33, 0, boost=30.0)
     ts(vw("MC", 7, 32, 16), two("c00"), p31, 1.0, OP.add, OP.add)
-    fill(two("cM"), 3.0 * 2 ** 31)
+    fill(two("cM"), 3.0 * 2 ** 31, q="S")
+    fill(one("cN"), -3.0 * 2 ** 31, q="S")
     cp(four("FL"), four("flI"))
     for a in range(2):
         ts(vw("RW", 64 * a, 64 * a + 64), ind(full("WN", 16), "FL", 0, 4), -33.0, 33.0, OP.mult, OP.add)
         spread(a, a == 1)
-    iota(vw("AM", 96, 168), [[0, 72]], 0, 0)
-    fill(full("ET", 520), 0.0)
-    add({"G": 0.2 + 1040 * CYC}, {"G": lambda: g.affine_select(T.ET[:], T.ET[:], [[1, 520]], OP.not_equal, 0.015625, -3, -4)}, [], [full("ET", 520)])
+    fill(vw("TK", 0), 0.0, q="S")
+    add({"V": 64 * CYC}, {"V": lambda: g.vector.transpose(T.TK[:, 1:33], T.MC[:])}, [full("mw", 10)], [vw("TK", 1, 33)])
+    iota(vw("AM", 96, 360), [[0, 264]], 0, 0)
+    fill(full("ET", 520), 0.015625, q="S")
+    add({"G": 0.2 + 1040 * CYC}, {"G": lambda: g.affine_select(T.ET[:], T.ET[:], [[1, 520]], OP.is_equal, 0.0, -3, -4)}, [vw("bI", 0, 4), two("c02"), two("c10"), two("c16"), two("c00"), four("cs"), four("cc")],
+        [full("ET", 520)])
     for k in range(4): quant("EQ", 128 * k, "ET", 3 - k)
-    for a in (0, 33): fill(vw("TV", a, 960, PW), 0.0)
+    for a in (0, 33): fill(vw("TV", a, 960, PW), 0.0, q="S")
     quant("LC", 32, "TT", 0)
     for k in range(4):
-        mm(4 + k, "EQ", 128 * k, "LC", 32)
-        cp(vw("TV", PW * k + 1, PW * k + 33), vw("ps", 512 * (4 + k), 512 * (4 + k) + 32), "S", -1.0)
+        mm(k, "EQ", 128 * k, "LC", 32)
+        cp(vw("TV", PW * k + 1, PW * k + 33), vw("ps", 512 * k, 512 * k + 32), "S", -1.0)
     cp(two(OCC[0]), two("flI"))
     iota(full("ix", 48), [[1, 48]], 0, 0)
     ts(full("wa", 48), full("ix", 48), vw("nW", 0), 512.0, OP.is_equal, OP.mult)
     ts(full("wb", 48), full("ix", 48), vw("nW", 1), None, OP.is_equal)
     tt(full("WJ", 48), full("wa", 48), full("wb", 48), OP.subtract)
-    iota(full("one", C), [[0, C]], 1, 0)
-    fill(full("stp", C), -1.0 / 512)
+    fill(full("stp", C), -1.0 / 512, q="S")
     iota(full("kF", 4), [[1, 4]], 3456, 0)
     ts(full("cA", 4), full("kF", 4), -0.25, None, OP.mult)
     ts(full("cB", 4), full("kF", 4), 1.0 / 2048, None, OP.mult)
-    fill(vw("ZS", 1408, 1424), 0.0)
-    fill(vw("FP", 1408, 1424), 0.0)
-    fill(vw("CLT", 128, 512), 0.0)
+    fill(vw("ZS", 1408, 1424), 0.0, q="S")
+    fill(vw("FP", 1408, 1424), 0.0, q="S")
+    fill(vw("CLT", 128, 512), 0.0, q="S")
     iota(full("MB", 33), [[1, 33]], -1, 0)
     iota(vw("MB", 33), [[0, 1]], -1, 0)
     quant("QV", 0, "VT", 0)
@@ -372,8 +470,9 @@ def build(g, core, T, topo, nxt):
     def came(t):
         fw, tv = "fw%d" % t, 4 * PW * t
         for s in range(2): ts(vw(OCC[t + 1], s), vw(fw, s), vw(OCC[t], s), None, OP.is_le)
-        tt(two("tk"), two(OCC[t + 1]), two(OCC[t]), OP.subtract)
-        for s in range(2): ts(vw("UL", s), vw("tk", s), CAME - 1.0, vw("nW", s), OP.mult, OP.add)
+        for s in range(2):
+            ts(vw("tk", s), vw(OCC[t], s), 1.0 - CAME, vw("nW", s), OP.mult, OP.add)
+            ts(vw("UL", s), vw(OCC[t + 1], s), CAME - 1.0, vw("tk", s), OP.mult, OP.add)
         lv, off = ((0, 0), (64, 96), (96, 96))[t]
         for k in range(4):
             b = 512 * (4 + k) + off
@@ -387,19 +486,22 @@ def build(g, core, T, topo, nxt):
         tt(vw("RW", 64 * a, 64 * a + 64), ind(full("WN", 16), fw, 0, 4), vw("RW", 64 * a, 64 * a + 64), OP.mult)
         spread(a)
 
-    def turn(a0, a1, lst):
+    def turn(a):
         cp(full("AM", 64), ind(full("O", 2 * PS), "R1", 0, 4))
         turn32(full("TB", 64), full("AM", 64))
         turn32(vw("AM", 64, 96), vw("TB", 16, 48))
-        moves = [(2, 64 * a, 64 - 64 * a, 64) for a in range(2)] + [(x, 32 * q, 32 * ((q + x) % 4), 32) for x in (1, 3) for q in range(4)]
+        moves = [(2, 64, 0, 64), (1, 96, 0, 32), (1, 0, 32, 32), (3, 32, 0, 32), (3, 64, 32, 32), (2, 0, 64, 32), (1, 32, 64, 32), (3, 96, 64, 32)]
         for k, (x, p0, p1, np_) in enumerate(moves):
-            a, b = 48 + 8 * (p1 // 64), 72 + 24 * x
-            if a0 <= p1 // 64 < a1: move((T and T.AM[p1:p1 + np_, b:b + 24], T and T.AM[p0:p0 + np_, a:a + 24]), [vw("AM", 48, 96), vw("AM", 100)], [vw("mv", k)])
-        cp(full(lst, 32), ind(full("AM", 168), "R2", 0, 2), more=[full("mv", 10)])
+            b = 72 + 24 * x
+            if p1 // 64 == a: move((T and T.AM[p1:p1 + np_, b:b + 24], T and T.AM[p0:p0 + np_, 48 + 8 * a:72 + 8 * a]), [vw("AM", 48, 96), vw("AM", 100)], [vw("mv", k)])
+
+    def lists(lst):
+        cp(full(lst, 32), ind(full("AM", 360), "R2", 0, 2), more=[full("mv", 11)])
 
     def flags(t, lst, jk, cnt, rem, wn, land, sem):
         cp(full(jk, C), ind(full("WJ", 34), lst, 0, 22), "S", acc=one(cnt))
-        ts(two(rem), two("cM"), one(cnt), -3.0 * 2 ** 31, OP.add, OP.add)
+        ts(two(rem + "0"), two("cM"), one(cnt), None, OP.add)
+        ts(two(rem), two(rem + "0"), one("cN"), None, OP.add)
         ts(vw(wn, 0, 4, 2), two("c00"), one(cnt), vw(OCC[t], 0), OP.is_ge, OP.max)
         ts(vw(wn, 1, 4, 2), two(rem), one(cnt), vw(OCC[t], 1), OP.is_equal, OP.max)
         send(four(land), four(wn), sem)
@@ -410,15 +512,24 @@ def build(g, core, T, topo, nxt):
             mm(4 + c, "QX", SL[c], "QU", 0)
             ab, pv = vw("AB", 128 * c, 128 * c + 117), vw("ps", 512 * (4 + c), 512 * (4 + c) + 117)
             add({"S": 117 * CYC}, {"S": lambda ab=ab, pv=pv: g.scalar.activation(ap(ab), ap(pv), AF.Sign, bias=-1e-36)}, [pv], [ab])
-            scan(vw("SC", 144 * c, 144 * c + 117), ab, full("hd", 117), 0.0, OP.add, OP.mult)
+            scan(vw("SC", 144 * c, 144 * c + 117), ab, full("hd" if t else "h0", 117), 0.0, OP.add, OP.mult)
         for k in range(4):
             mm(k, "EQ", 128 * k, "QX", 0, C)
-            if k < NF or t == 2:
+            if k < NF[t] or t == 2:
                 for j, n in CH: cp(vw("FP", C * k + j, C * k + j + n), vw("ps", 512 * k + j, 512 * k + j + n), "S")
 
     def level(t, p, l):
         n = 8 - l
         o0, b0, b1 = 72 * p + l * (17 - l), PS * p + 16 * (l - 1) * (18 - l), PS * p + 16 * l * (17 - l)
+        if t == 0 and l == 0:
+            go, s0 = full("GO%d" % p, 256), 288 * p
+            for s in range(2 - p): ts(vw("OF", o0 + s, o0 + 14, 2), vw("SC", s0 + 144 * s + 20, s0 + 144 * s + 117, 16), vw("SC", s0 + 144 * s + 4), 511.5, OP.add, OP.add)
+            ts(vw("OF", o0 + 14, o0 + 16 - p), vw("SC", s0 + 4, s0 + 149 - 144 * p, 144), 0.03125, 16.5, OP.mult, OP.add)
+            ts(vw(go[0], 0, 224), ind(full("TI", 1024), "OF", o0, o0 + 14), 1.0, None, OP.add)
+            ops[-1]["R"].append(two("tj"))
+            cp(vw(go[0], 224, 256), ind(full("TK", 33), "OF", o0 + 14, o0 + 16), "S")
+            turn32(vw("O", b1, b1 + 256), go)
+            return
         for s in range(2):
             if p == 1 and s == 1 and l % 2 == 0: continue
             out = vw("OF", o0 + s, o0 + 2 * n, 2)
@@ -428,31 +539,37 @@ def build(g, core, T, topo, nxt):
             else:
                 a = b0 + 16 * s + IP[l - 1]
                 ts(out, vw("O", a + 32, a + 32 * n + 1, 32), 32.0, vw("O", a), OP.mult, OP.add)
+            if t and l == DUE: ops[-1]["R"].append(vw("CQ%d" % (t - 1), 0))
         go, h = full("GO%d" % p, 32 * n), n - SPLIT[p][l]
         if h: cp(vw(go[0], 0, 32 * h), ind(full("TAB", TW), "OF", o0, o0 + 2 * h), "S", more=[full("tb", 6)])
         if h < n: cp(vw(go[0], 32 * h, 32 * n), ind(full("TAB", TW), "OF", o0 + 2 * h, o0 + 2 * n), "V", more=[full("tb", 6)])
-        turn32(vw("O", b1, b1 + 32 * n), go)
-        if l == 6:
-            b = PS * p + 1056
-            tt(vw("O", b + 71, b + 96, 16), vw("O", b + IP[6], b + 32, 16), vw("O", b + 32 + IP[6], b + 64, 16), OP.max)
+        if l < 6: turn32(vw("O", b1, b1 + 32 * n), go)
+        else:
+            cp(vw(go[0], 64, 80), ind(full("TAB", TW), "OF", o0, o0 + 1), "VS", more=[full("tb", 6)])
+            turn32(vw("CW", 128 * p, 128 * p + 64), go)
+            turn32(vw("CW", 128 * p + 64, 128 * p + 128), vw(go[0], 16, 80))
+            for x in range(4):
+                a, b, c = 168 + 48 * x + 24 * p, 96 - 32 * x, 128 * p
+                add({"V": 64 * CYC}, {"V": lambda a=a, b=b, c=c: g.vector.tensor_tensor(T.AM[96:128, a:a + 24], T.CW[b:b + 32, c + 3:c + 96:4], T.CW[b:b + 32, c + 35:c + 128:4], OP.max)},
+                    [vw("CW", c, c + 128)], [vw("AM", a, a + 24)])
 
     def layer(t):
         tv = 4 * PW * t
-        for j, n in CH:
+        for j, n, _ in ZC:
             for k in range(4):
                 tg, z, b = vw("TG", C * k + j, C * k + j + n), vw("ZS", 4 * j + k, 4 * j + 4 * n, 4), 512 * k + j
                 pick = ind(vw("TV", tv + PW * k, tv + PW * k + CAME), "L", j // 16, (j + n) // 16)
-                if k < NF: tt(z, pick, vw("FP", C * k + j, C * k + j + n), OP.add)
+                if k < NF[t]: tt(z, pick, vw("FP", C * k + j, C * k + j + n), OP.add)
                 else:
                     cp(tg, pick, "S")
                     tt(z, vw("ps", b, b + n), tg, OP.add)
-            quant("QZ", j, "ZS", 4 * j, n)
+            quant("QZ", j, "ZS", 4 * (j - max(128 - n, 0)), max(n, 128))
             cp(vw("ZP", 4 * j, 4 * j + 4 * n), vw("ZS", 4 * j, 4 * j + 4 * n), "VS", 64.0)
-        for c, (j, n) in enumerate(CH):
-            for k in range(4):
-                b = 4 * (1 - c % 2) + k
-                mm(b, "WC", 128 * k, "QZ", j, n)
-                tt(vw("XT", 4 * j + k, 4 * j + 4 * n, 4), vw("ps", 512 * b, 512 * b + n), vw("ZP", 4 * j + k, 4 * j + 4 * n, 4), OP.add)
+        for j, n, banks in ZC:
+            for k, b in enumerate(banks):
+                mm(b, "WC", 128 * k, "QZ", j, max(n, 128))
+                a = 512 * b + max(128 - n, 0)
+                tt(vw("XT", 4 * j + k, 4 * j + 4 * n, 4), vw("ps", a, a + n), vw("ZP", 4 * j + k, 4 * j + 4 * n, 4), OP.add)
 
     for t in range(3):
         images(t)
@@ -460,13 +577,18 @@ def build(g, core, T, topo, nxt):
             came(t - 1)
             filled("fa%d" % (t - 1), 0)
         for l in range(7):
+            if l == 4: turn(0)
             if l == 4 and t < 2:
-                turn(0, 1, "LA")
+                lists("LA")
                 flags(t, "LA", "JKA", "cna", "rea", "wa%d" % t, "fa%d" % t, "ra%d" % t)
             if l == 4 and t: filled("fw%d" % (t - 1), 1)
+            if l == 6: turn(1)
             for p in range(2): level(t, p, l)
-        turn(int(t < 2), 2, "L")
-        flags(t, "L", "JK", "cnt", "rem", "w_%d" % t, "fw%d" % t, "rf%d" % t)
+        lists("L")
+        if t < 2: flags(t, "L", "JK", "cnt", "rem", "w_%d" % t, "fw%d" % t, "rf%d" % t)
+        else:
+            cp(vw("JK", 0, 160), ind(full("WJ", 34), "L", 0, 10), "S")
+            cp(vw("JK", 160, C), ind(full("WJ", 34), "L", 10, 22), "S")
         layer(t)
 
         for a in range(0, C, PC[t]):
@@ -478,6 +600,9 @@ def build(g, core, T, topo, nxt):
             ts(vw("CL", 1, 8, 2), full("cB", 4), vw("SB", C - 1), 2048.0, OP.add, OP.mult)
             for k in range(4): cp(vw("CLT", k, 128, 4), ind(full("ZS", 1412), "CL", 2 * k, 2 * k + 2), "VS", 64.0)
         else:
+            ts(vw("w_2", 0), vw("SA", C - 1), 512.0, vw(OCC[t], 0), OP.is_le, OP.max)
+            ts(vw("w_2", 1), vw("SB", C - 1), -1.0, vw(OCC[t], 1), OP.is_ge, OP.max)
+            send(two("fw2"), two("w_2"), "rf2")
             ts(vw("CL", 0), vw("SA", C - 1), -1.0, 864.0, OP.mult, OP.add)
             ts(vw("CL", 1), vw("SB", C - 1), 512.0, 864.0, OP.mult, OP.add)
             for k in range(4): cp(vw("CLT", k, 128, 4), ind(vw("FP", C * k, C * k + C + 1), "CL", 0, 2), "VS", 64.0)

from concourse.bass import DstId, RemoteDMATransfer
from concourse.mybir import dt, AluOpType as OP, ActivationFunctionType as AF

COPY = AF.Copy
C = 352
CH = [(0, 128), (128, 224)]
ZC = [(0, 128, (4, 5, 6, 7)), (128, 224, (0, 1, 2, 3))]
SL = [0, 128, 224]
PW, CAME = 80, 34
PS = 1152
TW = 1104
IP = [0, 8, 2, 10, 1, 9, 3]
SMALL = {"KI": "flI4 bI4 BI_11 GoI2 Gm2 al2 dI2 dm2 t1_2 qs2 gs2",
         "KF": "BF_11 c02_2 c10_2 c16_2 nW2 u1_4 u2_4 u3_4 k1_1 k2_1 k3_1 k4_1 ph1 phi1 be2 bm2 de2 e1_2 e2_2 e3_2 e4_2 e5_2 e6_2 e7_2 e8_2 kF4 cA4 cB4 c00_2 cs4 cc4 g1_4 g2_4 cM2",
         "KL": "oca2 ocb2 occ2 ocd2 tk2 cnt1 rem2 cna1 rea2 rem0_2 rea0_2 cN1"}
ALIAS = {}
for _b, _s in SMALL.items():
    _k = 0
    for _n in _s.split():
        _m, _w = _n.rsplit("_", 1) if "_" in _n else (_n[:-1], _n[-1])
        ALIAS[_m] = (_b, _k)
        _k += int(_w)
OCC = ["oca", "ocb", "occ", "ocd"]


def _scratch():
    f, h, i, u, q, b = "float32", "bfloat16", "int32", "uint16", "float8_e4m3fn_x4", "uint8"
    s = {}
    for d, names in ((i, "KI:48 tic:64 TI:1024"),
                     (f, "KF:96 KL:24 rr:128 ix:48 wa:48 wb:48 MB:48 SA:352 SB:352 RT:128 BPO:352 YO:352"),
                     (u, "R1:4 R2:4 FL:4 OF:144 L:32 LA:32 CL:8 UL:2 wa0:4 wa1:4 fa0:4 fa1:4 w_0:4 w_1:4 w_2:4 fw0:4 fw1:4 fw2:4"),
                     (h, "hd:128 h0:128 TK:48 WJ:48 ET:520 tib:64 tbt:64 TAB:%d WN:16 RW:128 MA:128 JKA:352 MC:32 UT:512 VT:512 TT:512 XT:1408 AB:384 SC:432 GO0:256 GO1:256 O:%d AM:360 TB:64 CW:256 TG:1408 "
                         "ZS:1424 ZP:1408 TV:960 FP:1424 JK:352 one:520 stp:352 CLT:512" % (TW, 2 * PS))):
        for n in names.split():
            n, w = n.split(":")
            s[n] = ("sbuf", [128, int(w)], d)
    for n in "EQ:512 QU:128 QV:128 WC:512 QX:352 QZ:384 CQ0:128 CQ1:128 CQ2:128 LC:320".split():
        n, w = n.split(":")
        s[n] = ("sbuf", [128, int(w)], q)
        s[n + "s"] = ("sbuf", [128, int(w)], b)
    s["ps"] = ("psum", [128, 4096], f)
    return s


SCRATCH = _scratch()
SEMAPHORES = ["sV", "sS", "sT", "sG", "sent", "ra0", "ra1", "rf0", "rf1", "rf2", "rc0", "rc1", "rc2"] + ["d%d" % k for k in range(60)]
PLAN = {}
TRIES = 600
TRIES2, HEAT = 22000, 0.05
SPLIT = [[4, 3, 3, 2, 2, 1, 1], [4, 3, 3, 2, 2, 1, 1]]
PC = [118, 118, 352]
NF = [3, 3, 2]
DUE = 9
EARLY = {"a": 0.8, "f": 1.0, "c": 1.0}
CASES = [(0.2, 1.9, 2.8, 1.0), (0.22, 1.8, 3.2, 1.0), (0.23, 2.0, 4.0, 1.2)]
WAKE, DMALAT, NETLAT, CYC, PECYC = 0.22, 1.9, 3.0, 0.00083, 0.0012


def bits(v):
    n, a, b, st = v[:4]
    if n in ALIAS:
        n, o = ALIAS[n]
        a, b = a + o, b + o
    if n == "ps":
        a, b, st = a - a % 512, a - a % 512 + 512, 1
    return (n, ((1 << (b - a)) - 1) << a if st == 1 else sum(1 << k for k in range(a, b, st)))


def plan(ops):
    hist, deps, n = {}, [], len(ops)
    for k, o in enumerate(ops):
        d = set()
        acc = [bits(v) + (False,) for v in o["R"]] + [bits(v) + (True,) for v in o["W"]]
        for buf, m, w in acc:
            d.update(k2 for m2, k2, w2 in hist.get(buf, ()) if (w or w2) and m & m2)
        for buf, m, w in acc:
            hist.setdefault(buf, []).append((m, k, w))
        deps.append(sorted(d))
    anc, near = [0] * n, []
    for k in range(n):
        far = 0
        for x in deps[k]: far |= anc[x]
        near.append([x for x in deps[k] if not far >> x & 1])
        for x in deps[k]: far |= 1 << x
        anc[k] = far
    succ = [[] for _ in ops]
    for k in range(n):
        for j in near[k]: succ[j].append(k)
    prio = [0.0] * n
    for k in range(n - 1, -1, -1):
        prio[k] = min(ops[k]["dur"].values()) + ops[k]["lat"] + max([prio[j] for j in succ[k]] + [0.0])

    def place(pr, pref):
        left = [len(d) for d in near]
        ready = {k: 0.0 for k in range(n) if not left[k]}
        busy, fin, order = {}, [0.0] * n, []
        while ready:
            k = max(ready, key=lambda x: pr[x])
            opts = []
            for q, du in ops[k]["dur"].items():
                st, bq = ready[k], busy.setdefault(q, [])
                i = len(bq)
                while i and bq[i - 1][1] > st: i -= 1
                while i < len(bq) and st + du > bq[i][0] + 1e-9:
                    st = max(st, bq[i][1])
                    i += 1
                opts.append((st + du + (pref[k] if q == "V" else 0.0), st, q, i))
            _, st, q, i = min(opts)
            del ready[k]
            busy[q].insert(i, (st, st + ops[k]["dur"][q]))
            fin[k] = st + ops[k]["dur"][q] + ops[k]["lat"]
            order.append((k, q, st))
            for j in succ[k]:
                left[j] -= 1
                if not left[j]: ready[j] = max(fin[x] for x in near[j])
        order.sort(key=lambda o: o[2])
        tot = 0.0
        for w, d, r, f in CASES:
            lat, free = {"c": w, "d": d, "n": r}, {}
            for k, q, _ in order:
                st = free.get(q, 0.0)
                for x in near[k]:
                    if fin[x] > st: st = fin[x]
                free[q] = st + f * ops[k]["dur"][q]
                fin[k] = free[q] + lat[ops[k]["kind"]]
            tot += max(fin) / len(CASES)
        return tot + 1e-4 * sum(fin) / n, order

    seed = [3]
    def rnd():
        seed[0] = (seed[0] * 1103515245 + 12345) % 2147483648
        return seed[0] / 2147483648.0
    pr, pref = [prio[k] + ops[k]["boost"] - 1e-6 * k for k in range(n)], [0.4] * n
    best = place(pr, pref)

    def back(order):
        late, busy = [0.0] * n, {}
        for k, q, _ in sorted(order, key=lambda o: -o[2] - ops[o[0]]["dur"][o[1]]):
            du, bq = ops[k]["dur"][q], busy.setdefault(q, [])
            st = max([late[j] for j in succ[k]] + [0.0]) + ops[k]["lat"]
            i = len(bq)
            while i and bq[i - 1][1] > st: i -= 1
            while i < len(bq) and st + du > bq[i][0] + 1e-9:
                st = max(st, bq[i][1])
                i += 1
            bq.insert(i, (st, st + du))
            late[k] = st + du
        return late

    for it in range(TRIES):
        if it % 50 == 0:
            p2, f2 = back(best[1]), list(pref)
            for k, q, _ in best[1]: f2[k] = -5.0 if q == "V" else 5.0
            r = place(p2, f2)
            if r[0] < best[0]: best, pr, pref = r, p2, f2
        p2, f2 = list(pr), list(pref)
        for _ in range(1 + int(rnd() * 12)):
            k = int(rnd() * n)
            p2[k] += (rnd() - 0.5) * (4.0 if rnd() < 0.3 else 1.0)
            if len(ops[k]["dur"]) > 1: f2[k] = (rnd() - 0.5) * 0.8
        r = place(p2, f2)
        if r[0] <= best[0]: best, pr, pref = r, p2, f2

    lats = [([{"c": w, "d": d, "n": r}[o["kind"]] for o in ops], f) for w, d, r, f in CASES]

    def run(order):
        tot, chains = 0.0, []
        for lat, f in lats:
            fin, by, free, last = [0.0] * n, [None] * n, {}, {}
            for k, q in order:
                st, b = free.get(q, 0.0), last.get(q)
                for x in near[k]:
                    if fin[x] > st: st, b = fin[x], x
                free[q] = st = st + f * ops[k]["dur"][q]
                fin[k], by[k], last[q] = st + lat[k], b, k
            k = max(range(n), key=lambda x: fin[x])
            tot += fin[k] / len(lats) + 2e-5 * sum(fin) / n
            chains.append((k, by))
        return tot, chains

    order = [(k, q) for k, q, _ in best[1]]
    now, chains = run(order)
    top = (now, order)
    for it in range(TRIES2):
        k, by = chains[int(rnd() * len(chains))]
        pairs = []
        while by[k] is not None:
            if not anc[k] >> by[k] & 1: pairs.append((by[k], k))
            k = by[k]
        if not pairs: break
        j, k = pairs[int(rnd() * len(pairs))]
        pos = {x: i for i, (x, _) in enumerate(order)}
        a, b, u = pos[j], pos[k], rnd()
        if u < 0.3 and (len(ops[j]["dur"]) > 1 or len(ops[k]["dur"]) > 1):
            i = a if len(ops[j]["dur"]) > 1 and (len(ops[k]["dur"]) == 1 or u < 0.15) else b
            new = list(order)
            new[i] = (order[i][0], "S" if order[i][1] == "V" else "V")
        elif u < 0.65:
            mid = order[a:b + 1]
            new = order[:a] + [o for o in mid if o[0] == k or anc[k] >> o[0] & 1] + [o for o in mid if not (o[0] == k or anc[k] >> o[0] & 1)] + order[b + 1:]
        else:
            b = min(n - 1, b + int(rnd() * 12))
            mid = order[a:b + 1]
            new = order[:a] + [o for o in mid if not (o[0] == j or anc[o[0]] >> j & 1)] + [o for o in mid if o[0] == j or anc[o[0]] >> j & 1] + order[b + 1:]
        r, c = run(new)
        if r <= now + HEAT * (1.0 - it / TRIES2) * rnd():
            now, chains, order = r, c, new
            if r < top[0]: top = (r, new)
    return [(k, q, 0.0) for k, q in top[1]], deps, top[0]


def build(g, core, T, topo, nxt):
    ops = []

    def ap(v):
        n, a, b, st = v[:4]
        if n in ALIAS:
            n, o = ALIAS[n]
            a, b = a + o, b + o
        r = T[n][:, a:b] if st == 1 else T[n][:, a:b:st]
        if len(v) > 4 and v[4] == "c": return r.bitcast(dt.uint8)
        return r.indirect(ap(v[4])) if len(v) > 4 else r

    def vw(n, a, b=None, st=1):
        return (n, a, a + 1 if b is None else b, st)

    def ind(v, *off):
        return v + (vw(*off),)

    def add(dur, fn, ins, outs, lat=WAKE, kind="c", nd=0, boost=0.0):
        R = [v[:4] for v in ins] + [v[4][:4] for v in ins if len(v) > 4 and v[4] != "c"]
        ops.append({"dur": dur, "fn": fn, "R": R, "W": [v[:4] for v in outs], "lat": lat, "kind": kind, "nd": nd, "boost": boost})

    def wide(*vs):
        return any(SCRATCH[ALIAS.get(v[0], v)[0]][2] in ("float32", "int32") for v in vs)

    def num(v):
        return len(range(v[1], v[2], v[3]))

    def cost(v, k):
        return max(64, num(v) * k) * CYC

    def isind(v):
        return len(v) > 4 and v[4] != "c"

    def gat(v, c):
        return c + num(v) * 1.56 * CYC

    def ts(out, in0, s1, s2, op0, op1=None, boost=0.0):
        sc = [s for s in (s1, s2) if isinstance(s, tuple)]
        d = gat(out, 0.05) if isind(in0) else cost(out, 1.0 if wide(out, in0) else 0.5)
        val = lambda s: ap(s) if isinstance(s, tuple) else s
        if op1 is None: fn = lambda: g.vector.tensor_scalar(ap(out), ap(in0), val(s1), None, op0)
        else: fn = lambda: g.vector.tensor_scalar(ap(out), ap(in0), val(s1), val(s2), op0, op1)
        dur, fns = {"V": d}, {"V": fn}
        kind = lambda v: SCRATCH[ALIAS.get(v[0], v)[0]][2]
        if not isind(in0) and all(kind(v) == "float32" for v in [out, in0] + sc) and (op0, op1) in ((OP.mult, OP.add), (OP.mult, None), (OP.add, None)):
            a, b = (s1, s2) if op1 is not None else (s1, 0.0) if op0 == OP.mult else (1.0, s1)
            dur["S"], fns["S"] = d, lambda: g.scalar.activation(ap(out), ap(in0), AF.Identity, bias=val(b), scale=val(a))
        add(dur, fns, [in0] + sc, [out], boost=boost)

    def tt(out, a, b, op):
        if out[0][0] in "egu" and out[0] in ALIAS:
            for c in range(out[2]):
                if op == OP.subtract: ts(vw(out[0], c), vw(b[0], c), -1.0, vw(a[0], c), OP.mult, OP.add)
                else: ts(vw(out[0], c), vw(a[0], c), vw(b[0], c), None, op)
            return
        d = gat(out, 0.05) if isind(a) else cost(out, 1.0 if a[0] == "ps" else 2.0)
        add({"V": d}, {"V": lambda: g.vector.tensor_tensor(ap(out), ap(a), ap(b), op)}, [a, b], [out])

    def cp(out, a, q="V", scale=1.0, acc=None, boost=0.0, more=[]):
        i = isind(a)
        kw = {"scale": scale} if scale != 1.0 else {}
        if acc: kw["accum_out"] = acc
        fns = {"V": lambda: g.vector.tensor_copy(ap(out), ap(a)) if scale == 1.0 else g.vector.tensor_scalar(ap(out), ap(a), scale, None, OP.mult),
               "S": lambda: g.scalar.activation(ap(out), ap(a), COPY, **{k: ap(x) if k == "accum_out" else x for k, x in kw.items()})}
        durs = {"V": gat(out, 0.05) if i else cost(out, 1.0 if wide(out, a) else 0.5), "S": (gat(out, 0.065) if i else cost(out, 1.0)) + (0.02 if acc else 0.0)}
        add({k: durs[k] for k in q}, {k: fns[k] for k in q}, [a] + more, [out] + ([acc] if acc else []), boost=boost)

    def scan(out, d0, d1, init, op0, op1):
        add({"V": cost(out, 1.0 if wide(out, d0, d1) else 0.5)}, {"V": lambda: g.vector.tensor_tensor_scan(ap(out), ap(d0), ap(d1), ap(init) if isinstance(init, tuple) else init, op0, op1)},
            [d0, d1] + ([init] if isinstance(init, tuple) else []), [out])

    def turn32(out, a):
        add({"V": cost(out, 0.5)}, {"V": lambda: g.vector.transpose(ap(out), ap(a))}, [a], [out])

    def move(io, ins, outs):
        add({"V": 64 * CYC, "S": 64 * CYC}, {"V": lambda: g.vector.tensor_copy(*io), "S": lambda: g.scalar.activation(*io, COPY)}, ins, outs)

    def fill(out, val, boost=0.0, q="V"):
        src = vw("one", 0, num(out))
        add({k: cost(out, 1.0 if k == "S" or wide(out) else 0.5) for k in q},
            {"V": lambda: g.vector.memset(ap(out), val), "S": lambda: g.scalar.activation(ap(out), ap(src), COPY, scale=val)}, [src] if "S" in q else [], [out], boost=boost)

    def quant(q, a, t, ta, n=128):
        c, s, i = vw(q, a, a + n), vw(q + "s", a, a + n), vw(t, ta, ta + 4 * n)
        add({"V": 0.012 + 0.88e-3 * n}, {"V": lambda: g.vector.quantize_mx(ap(c), ap(s), ap(i))}, [i], [c, s])

    def mm(bank, lq, la, rq, ra, n=128):
        o = vw("ps", 512 * bank, 512 * bank + n)
        i = [vw(lq, la, la + 128), vw(lq + "s", la, la + 128), vw(rq, ra, ra + n), vw(rq + "s", ra, ra + n)]
        add({"T": (n + 16) * PECYC}, {"T": lambda: g.tensor.matmul_mx(ap(o), ap(i[0]), ap(i[1]), ap(i[2]), ap(i[3]), True, True)}, i, [o])

    def iota(out, pattern, base, cm, boost=0.0):
        kw = {} if SCRATCH[ALIAS.get(out[0], out)[0]][2] == "int32" else {"allow_small_or_imprecise_dtypes": True}
        add({"G": 0.15 + num(out) * 2 * CYC}, {"G": lambda: g.iota(ap(out), pattern, base, cm, **kw)}, [], [out], boost=boost)

    def ld(q, pairs, ins, outs, nd=1, boost=0.0, lat=DMALAT):
        add({q: 0.06 * nd}, {q: lambda: [(g.sync if q == "Y" else g.scalar).dma_start(o, i) for o, i in pairs()]}, ins, outs, lat, "d", nd, boost)

    def send(out, in_, sem, boost=0.0):
        ne = 8 if T is None else len(topo.engines(core, nxt))
        def fn():
            rid, pid = topo.addr(nxt, core)
            g.remote_dma(ap(out), ap(in_), T.sem[sem], T.sem.sent, pid, rid, topo.mask(core, nxt))
        add({"G": 0.3}, {"G": fn}, [in_], [out], NETLAT + EARLY[sem[1]], "n", (sem, ne), boost)

    def send2(outs, ins, sem):
        en = list(range(8)) if T is None else topo.engines(core, nxt)
        def fn():
            rid, pid = topo.addr(nxt, core)
            g.remote_dma_fused([RemoteDMATransfer(dst_ids=[DstId(rid=rid, pnc=pid)], dma_engine_mask=sum(1 << e for e in en[k::2]), remote_sem=T.sem[sem], src=ap(ins[k]), dst=ap(outs[k]))
                                for k in range(2)], local_sem=T.sem.sent)
        add({"G": 0.3}, {"G": fn}, ins, outs, NETLAT, "n", (sem, len(en)))

    full = lambda n, w=128: vw(n, 0, w)
    two = lambda n: vw(n, 0, 2)
    one = lambda n: vw(n, 0)

    ld("Y", lambda: [(T.tic[0:64, 0:32], T.ti[0:5:4, :]), (T.tic[64:128, 0:32], T.ti[2:7:4, :]), (T.tic[0:64, 32:64], T.ti[1:6:4, :]), (T.tic[64:128, 32:64], T.ti[3:5, :])],
       [], [full("tic", 64)], 4, boost=50.0)
    ld("Y", lambda: [(ap(vw("flI", s)), T.fl[:, 16 * (s % 2):16 * (s % 2) + 16]) for s in range(4)], [], [full("flI", 4)], 4, boost=49.0)
    for c, (j, n) in enumerate(CH):
        v = vw("XT", 4 * j, 4 * j + 4 * n)
        ld("S", lambda v=v: [(ap(v), T.x[:, v[1]:v[2]])], [], [v], boost=45.0 - 2 * c)
    ld("S", lambda: [(T.UT[:], T.u[:])], [], [full("UT", 512)], boost=44.0)
    fill(full("one", 520), 1.0, boost=60.0)
    fill(full("TAB", 1057), 0.0, boost=50.0)
    fill(vw("TAB", 1057, TW), 33.0)
    ts(full("tib", 64), full("tic", 64), 1.0, None, OP.add)
    turn32(full("tbt", 64), full("tib", 64))
    for k in range(2):
        ld("YS"[k], lambda k=k: [(T.TAB[16 * k:16 * k + 4, 33:1057], T.tbt[:, 0:32]), (T.TAB[16 * k + 8:16 * k + 11, 33:1057], T.tbt[0:96, 32:64])],
           [full("tbt", 64), vw("TAB", 40), vw("TAB", 1060)], [vw("tb", k)], 2)
    for k in range(2):
        n = 32 * k + 32
        add({"V": 350 * CYC}, {"V": lambda n=n: g.vector.tensor_copy(T.TAB[n:2 * n, 33:733], T.TAB[0:n, 33:733])}, [vw("tb", 0, 2 + k)], [vw("tb", 2 + 2 * k)])
        add({"S": 324 * CYC}, {"S": lambda n=n: g.scalar.activation(T.TAB[n:2 * n, 733:1057], T.TAB[0:n, 733:1057], COPY)}, [vw("tb", 0, 2), vw("tb", 3 * k)], [vw("tb", 3 + 2 * k)])
    late = [vw("tb", 0, 2)]
    fill(full("TI", 1024), 0, boost=55.0)
    for q in range(2): ld("YS"[q], lambda q=q: [(T.TI[16 * k:16 * k + 1, :], T.ti[0:1, :]) for k in range(q, 8, 2)], [vw("TI", 0)], [vw("tj", q)], 4, boost=50.0)
    fill(vw("TT", 128, 512), 0.0, q="S")
    ld("S", lambda: [(T.TT[:, 0:128], T.tr[:])], [], [full("TT")])
    ld("Y", lambda: [(T.WC[:].bitcast(dt.uint8), T.wc[:]), (T.WCs[:], T.ws[:])], late, [full("WC", 512), full("WCs", 512)], 2)
    ld("Y", lambda: [(T.VT[:], T.v[:])], late, [full("VT", 512)])

    quant("QU", 0, "UT", 0)
    iota(full("rr"), [[0, 8], [1, 16]], 0, 0, boost=30.0)
    ts(full("hd"), full("rr"), 4.0, 2.0, OP.is_lt, OP.mult)
    fill(vw("hd", 20, 128, 16), 16.0, q="S")
    fill(vw("hd", 4), 0.5, q="S")
    ts(full("h0"), full("rr"), 4.0, 2.0, OP.is_lt, OP.mult)
    fill(vw("h0", 20, 128, 16), 0.5, q="S")
    fill(vw("h0", 4), 16.0, q="S")
    fill(vw("SC", 132, 432, 144), -528.0, q="S")
    fill(full("OF", 144), 0)
    for k, m in enumerate((16, 8, 2, 1)): iota(vw("bI", k), [[0, 1]], 0, m, boost=60.0)
    ts(vw("BI", 0, 4), vw("bI", 0, 4), 4, 1, OP.arith_shift_right, OP.bitwise_and)
    for k, (sh, m) in enumerate(((1, 6), (4, 7), (0, 15), (5, 3), (5, 1), (6, 1), (0, 31))): ts(vw("BI", 4 + k), vw("bI", 3), sh, m, OP.arith_shift_right, OP.bitwise_and)
    cp(vw("BF", 0, 10), vw("BI", 0, 10))
    cp(vw("BF", 10), vw("BI", 10))
    sg, pr, i3, g0, ih, gF, iF, qF, q1, aF, p31 = [vw("BF", k) for k in range(11)]
    for n, st, b in (("c02", 2, 0), ("c10", -1, 1), ("c16", 16, 1), ("c00", 0, 0)): iota(two(n), [[st, 2]], b, 0, boost=20.0)
    four = lambda n: vw(n, 0, 4)
    iota(four("cs"), [[0, 2], [2, 2]], -1, 0, boost=20.0)
    iota(four("cc"), [[0, 2], [-1, 2]], 1, 0, boost=20.0)
    ts(two("nW"), two("c16"), iF, None, OP.add)
    ts(four("g1"), four("cs"), g0, ih, OP.mult, OP.add)
    tt(four("g2"), four("g1"), four("cc"), OP.add)
    ts(four("u1"), four("g2"), -1.0, 16.0, OP.mult, OP.add)
    ts(four("u2"), four("g2"), 1.0, 16.0, OP.add, OP.mult)
    tt(four("u3"), four("u1"), four("u2"), OP.mult)
    ts(one("k1"), pr, float(PS), -25.0, OP.mult, OP.add)
    ts(one("k2"), sg, 16.0, one("k1"), OP.mult, OP.add)
    ts(four("R1"), four("u3"), one("k2"), None, OP.add)
    ts(two("GoI"), two("c02"), iF, None, OP.add)
    ts(two("Gm"), two("GoI"), 7, None, OP.bitwise_and)
    ts(two("al"), two("GoI"), 1, None, OP.bitwise_and)
    ts(two("be"), two("c10"), i3, None, OP.mult)
    ts(one("ph"), gF, 7.0, g0, OP.is_equal, OP.subtract)
    ts(one("phi"), one("ph"), 1.0, None, OP.add)
    tt(two("bm"), two("be"), two("al"), OP.subtract)
    ts(two("de"), two("bm"), one("phi"), None, OP.mult)
    tt(two("t1"), two("de"), two("Gm"), OP.add)
    ts(two("qs"), two("t1"), 1, None, OP.arith_shift_right)
    ts(two("gs"), two("t1"), 1, None, OP.bitwise_and)
    ts(two("dI"), two("qs"), -1.0, qF, OP.mult, OP.add)
    ts(two("dm"), two("dI"), 3, None, OP.bitwise_and)
    ts(one("k3"), aF, 8.0, -24.0, OP.mult, OP.add)
    ts(one("k4"), q1, 4.0, 72.0, OP.mult, OP.add)
    tt(two("e1"), two("be"), two("de"), OP.subtract)
    tt(two("e2"), two("e1"), two("c02"), OP.add)
    ts(two("e3"), two("dm"), 24.0, one("k4"), OP.mult, OP.add)
    ts(two("e4"), two("dm"), 0.0, one("k3"), OP.is_equal, OP.mult)
    ts(two("e5"), two("gs"), g0, 16.0, OP.not_equal, OP.mult)
    tt(two("e6"), two("e3"), two("e2"), OP.add)
    tt(two("e7"), two("e4"), two("e5"), OP.add)
    tt(two("e8"), two("e6"), two("e7"), OP.add)
    ts(two("qs"), two("Gm"), 1, None, OP.arith_shift_right)
    ts(two("e1"), two("qs"), -48.0, 313.0, OP.mult, OP.add)
    ts(two("e2"), two("c02"), 12.0, g0, OP.mult, OP.subtract)
    ts(two("e3"), two("be"), g0, 16.0, OP.not_equal, OP.mult)
    ts(two("e4"), two("al"), 4.0, None, OP.mult)
    tt(two("e5"), two("e1"), two("e2"), OP.add)
    tt(two("e6"), two("e3"), two("e4"), OP.add)
    tt(two("e7"), two("e5"), two("e6"), OP.add)
    tt(two("e1"), two("e7"), two("e8"), OP.subtract)
    ts(one("k1"), qF, 3.0, None, OP.is_equal)
    ts(two("e2"), two("e1"), one("k1"), None, OP.mult)
    tt(two("e3"), two("e2"), two("e8"), OP.add)
    cp(two("R2"), two("e3"))
    for p in range(2): iota(vw("O", PS * p + 832, PS * p + 1152), [[0, 320]], 0, 0)

    def spread(a, put=True):
        ma = vw("MA", 64 * a, 64 * a + 64)
        turn32(ma, vw("RW", 64 * a, 64 * a + 64))
        for k in range(4):
            c, q = k // 2, 2 * a + k % 2
            move((T and T.MC[32 * q:32 * q + 32, 2 * c + a:32:8], T and T.MA[64 * a + 32 * c:64 * a + 32 * c + 32, 64 * a:64 * a + 64:16]), [ma, full("MC", 32)], [vw("mw", 4 * a + k)])
        move((T and T.MC[64 - 64 * a:128 - 64 * a, a:32:2], T and T.MC[64 * a:64 * a + 64, a:32:2]), [vw("mw", 4 * a, 4 * a + 4)], [vw("mw", 8 + a)])
        if put: add({"V": 64 * CYC}, {"V": lambda: g.vector.transpose(T.TAB[:, 1:33], T.MC[:])}, [full("mw", 10), vw("tb", 0, 2)], [vw("TAB", 1, 33)])

    iota(full("WN", 16), [[1, 16]], 0, 0, boost=30.0)
    iota(full("MC", 32), [[0, 32]], 33, 0, boost=30.0)
    ts(vw("MC", 7, 32, 16), two("c00"), p31, 1.0, OP.add, OP.add)
    fill(two("cM"), 3.0 * 2 ** 31, q="S")
    fill(one("cN"), -3.0 * 2 ** 31, q="S")
    cp(four("FL"), four("flI"))
    for a in range(2):
        ts(vw("RW", 64 * a, 64 * a + 64), ind(full("WN", 16), "FL", 0, 4), -33.0, 33.0, OP.mult, OP.add)
        spread(a, a == 1)
    fill(vw("TK", 0), 0.0, q="S")
    add({"V": 64 * CYC}, {"V": lambda: g.vector.transpose(T.TK[:, 1:33], T.MC[:])}, [full("mw", 10)], [vw("TK", 1, 33)])
    iota(vw("AM", 96, 360), [[0, 264]], 0, 0)
    fill(full("ET", 520), 0.015625, q="S")
    add({"G": 0.2 + 1040 * CYC}, {"G": lambda: g.affine_select(T.ET[:], T.ET[:], [[1, 520]], OP.is_equal, 0.0, -3, -4)}, [vw("bI", 0, 4), two("c02"), two("c10"), two("c16"), two("c00"), four("cs"), four("cc")],
        [full("ET", 520)])
    for k in range(4): quant("EQ", 128 * k, "ET", 3 - k)
    for a in (0, 33): fill(vw("TV", a, 960, PW), 0.0, q="S")
    quant("LC", 32, "TT", 0)
    for k in range(4):
        mm(k, "EQ", 128 * k, "LC", 32)
        cp(vw("TV", PW * k + 1, PW * k + 33), vw("ps", 512 * k, 512 * k + 32), "S", -1.0)
    cp(two(OCC[0]), two("flI"))
    iota(full("ix", 48), [[1, 48]], 0, 0)
    ts(full("wa", 48), full("ix", 48), vw("nW", 0), 512.0, OP.is_equal, OP.mult)
    ts(full("wb", 48), full("ix", 48), vw("nW", 1), None, OP.is_equal)
    tt(full("WJ", 48), full("wa", 48), full("wb", 48), OP.subtract)
    fill(full("stp", C), -1.0 / 512, q="S")
    iota(full("kF", 4), [[1, 4]], 3456, 0)
    ts(full("cA", 4), full("kF", 4), -0.25, None, OP.mult)
    ts(full("cB", 4), full("kF", 4), 1.0 / 2048, None, OP.mult)
    fill(vw("ZS", 1408, 1424), 0.0, q="S")
    fill(vw("FP", 1408, 1424), 0.0, q="S")
    fill(vw("CLT", 128, 512), 0.0, q="S")
    iota(full("MB", 33), [[1, 33]], -1, 0)
    iota(vw("MB", 33), [[0, 1]], -1, 0)
    quant("QV", 0, "VT", 0)

    def came(t):
        fw, tv = "fw%d" % t, 4 * PW * t
        for s in range(2): ts(vw(OCC[t + 1], s), vw(fw, s), vw(OCC[t], s), None, OP.is_le)
        for s in range(2):
            ts(vw("tk", s), vw(OCC[t], s), 1.0 - CAME, vw("nW", s), OP.mult, OP.add)
            ts(vw("UL", s), vw(OCC[t + 1], s), CAME - 1.0, vw("tk", s), OP.mult, OP.add)
        lv, off = ((0, 0), (64, 96), (96, 96))[t]
        for k in range(4):
            b = 512 * (4 + k) + off
            mm(4 + k, "EQ", 128 * k, "LC", lv)
            cp(vw("TV", tv + PW * k + CAME, tv + PW * k + CAME + 32), vw("ps", b, b + 32), "S", -1.0)
            win = ind(vw("TV", tv + PW * k, tv + PW * k + CAME + 32), "UL", 0, 2)
            if t < 2: cp(vw("TV", tv + PW * (k + 4) + 1, tv + PW * (k + 4) + 33), win, "VS")
            else: cp(vw("RT", k, 128, 4), win, "VS", -64.0)

    def filled(fw, a):
        tt(vw("RW", 64 * a, 64 * a + 64), ind(full("WN", 16), fw, 0, 4), vw("RW", 64 * a, 64 * a + 64), OP.mult)
        spread(a)

    def turn(a):
        cp(full("AM", 64), ind(full("O", 2 * PS), "R1", 0, 4))
        turn32(full("TB", 64), full("AM", 64))
        turn32(vw("AM", 64, 96), vw("TB", 16, 48))
        moves = [(2, 64, 0, 64), (1, 96, 0, 32), (1, 0, 32, 32), (3, 32, 0, 32), (3, 64, 32, 32), (2, 0, 64, 32), (1, 32, 64, 32), (3, 96, 64, 32)]
        for k, (x, p0, p1, np_) in enumerate(moves):
            b = 72 + 24 * x
            if p1 // 64 == a: move((T and T.AM[p1:p1 + np_, b:b + 24], T and T.AM[p0:p0 + np_, 48 + 8 * a:72 + 8 * a]), [vw("AM", 48, 96), vw("AM", 100)], [vw("mv", k)])

    def lists(lst):
        cp(full(lst, 32), ind(full("AM", 360), "R2", 0, 2), more=[full("mv", 11)])

    def flags(t, lst, jk, cnt, rem, wn, land, sem):
        cp(full(jk, C), ind(full("WJ", 34), lst, 0, 22), "S", acc=one(cnt))
        ts(two(rem + "0"), two("cM"), one(cnt), None, OP.add)
        ts(two(rem), two(rem + "0"), one("cN"), None, OP.add)
        ts(vw(wn, 0, 4, 2), two("c00"), one(cnt), vw(OCC[t], 0), OP.is_ge, OP.max)
        ts(vw(wn, 1, 4, 2), two(rem), one(cnt), vw(OCC[t], 1), OP.is_equal, OP.max)
        send(four(land), four(wn), sem)

    def images(t):
        for j, n in CH: quant("QX", j, "XT", 4 * j, n)
        for c in range(3):
            mm(4 + c, "QX", SL[c], "QU", 0)
            ab, pv = vw("AB", 128 * c, 128 * c + 117), vw("ps", 512 * (4 + c), 512 * (4 + c) + 117)
            add({"S": 117 * CYC}, {"S": lambda ab=ab, pv=pv: g.scalar.activation(ap(ab), ap(pv), AF.Sign, bias=-1e-36)}, [pv], [ab])
            scan(vw("SC", 144 * c, 144 * c + 117), ab, full("hd" if t else "h0", 117), 0.0, OP.add, OP.mult)
        for k in range(4):
            mm(k, "EQ", 128 * k, "QX", 0, C)
            if k < NF[t] or t == 2:
                for j, n in CH: cp(vw("FP", C * k + j, C * k + j + n), vw("ps", 512 * k + j, 512 * k + j + n), "S")

    def level(t, p, l):
        n = 8 - l
        o0, b0, b1 = 72 * p + l * (17 - l), PS * p + 16 * (l - 1) * (18 - l), PS * p + 16 * l * (17 - l)
        if t == 0 and l == 0:
            go, s0 = full("GO%d" % p, 256), 288 * p
            for s in range(2 - p): ts(vw("OF", o0 + s, o0 + 14, 2), vw("SC", s0 + 144 * s + 20, s0 + 144 * s + 117, 16), vw("SC", s0 + 144 * s + 4), 511.5, OP.add, OP.add)
            ts(vw("OF", o0 + 14, o0 + 16 - p), vw("SC", s0 + 4, s0 + 149 - 144 * p, 144), 0.03125, 16.5, OP.mult, OP.add)
            ts(vw(go[0], 0, 224), ind(full("TI", 1024), "OF", o0, o0 + 14), 1.0, None, OP.add)
            ops[-1]["R"].append(two("tj"))
            cp(vw(go[0], 224, 256), ind(full("TK", 33), "OF", o0 + 14, o0 + 16), "S")
            turn32(vw("O", b1, b1 + 256), go)
            return
        for s in range(2):
            if p == 1 and s == 1 and l % 2 == 0: continue
            out = vw("OF", o0 + s, o0 + 2 * n, 2)
            if l == 0:
                s0 = 144 * (2 * p + s)
                ts(out, vw("SC", s0 + 20, s0 + 133, 16), vw("SC", s0 + 4), 544.5, OP.add, OP.add)
            else:
                a = b0 + 16 * s + IP[l - 1]
                ts(out, vw("O", a + 32, a + 32 * n + 1, 32), 32.0, vw("O", a), OP.mult, OP.add)
            if t and l == DUE: ops[-1]["R"].append(vw("CQ%d" % (t - 1), 0))
        go, h = full("GO%d" % p, 32 * n), n - SPLIT[p][l]
        if h: cp(vw(go[0], 0, 32 * h), ind(full("TAB", TW), "OF", o0, o0 + 2 * h), "S", more=[full("tb", 6)])
        if h < n: cp(vw(go[0], 32 * h, 32 * n), ind(full("TAB", TW), "OF", o0 + 2 * h, o0 + 2 * n), "V", more=[full("tb", 6)])
        if l < 6: turn32(vw("O", b1, b1 + 32 * n), go)
        else:
            cp(vw(go[0], 64, 80), ind(full("TAB", TW), "OF", o0, o0 + 1), "VS", more=[full("tb", 6)])
            turn32(vw("CW", 128 * p, 128 * p + 64), go)
            turn32(vw("CW", 128 * p + 64, 128 * p + 128), vw(go[0], 16, 80))
            for x in range(4):
                a, b, c = 168 + 48 * x + 24 * p, 96 - 32 * x, 128 * p
                add({"V": 64 * CYC}, {"V": lambda a=a, b=b, c=c: g.vector.tensor_tensor(T.AM[96:128, a:a + 24], T.CW[b:b + 32, c + 3:c + 96:4], T.CW[b:b + 32, c + 35:c + 128:4], OP.max)},
                    [vw("CW", c, c + 128)], [vw("AM", a, a + 24)])

    def layer(t):
        tv = 4 * PW * t
        for j, n, _ in ZC:
            for k in range(4):
                tg, z, b = vw("TG", C * k + j, C * k + j + n), vw("ZS", 4 * j + k, 4 * j + 4 * n, 4), 512 * k + j
                pick = ind(vw("TV", tv + PW * k, tv + PW * k + CAME), "L", j // 16, (j + n) // 16)
                if k < NF[t]: tt(z, pick, vw("FP", C * k + j, C * k + j + n), OP.add)
                else:
                    cp(tg, pick, "S")
                    tt(z, vw("ps", b, b + n), tg, OP.add)
            quant("QZ", j, "ZS", 4 * (j - max(128 - n, 0)), max(n, 128))
            cp(vw("ZP", 4 * j, 4 * j + 4 * n), vw("ZS", 4 * j, 4 * j + 4 * n), "VS", 64.0)
        for j, n, banks in ZC:
            for k, b in enumerate(banks):
                mm(b, "WC", 128 * k, "QZ", j, max(n, 128))
                a = 512 * b + max(128 - n, 0)
                tt(vw("XT", 4 * j + k, 4 * j + 4 * n, 4), vw("ps", a, a + n), vw("ZP", 4 * j + k, 4 * j + 4 * n, 4), OP.add)

    for t in range(3):
        images(t)
        if t:
            came(t - 1)
            filled("fa%d" % (t - 1), 0)
        for l in range(7):
            if l == 4: turn(0)
            if l == 4 and t < 2:
                lists("LA")
                flags(t, "LA", "JKA", "cna", "rea", "wa%d" % t, "fa%d" % t, "ra%d" % t)
            if l == 4 and t: filled("fw%d" % (t - 1), 1)
            if l == 6: turn(1)
            for p in range(2): level(t, p, l)
        lists("L")
        if t < 2: flags(t, "L", "JK", "cnt", "rem", "w_%d" % t, "fw%d" % t, "rf%d" % t)
        else:
            cp(vw("JK", 0, 160), ind(full("WJ", 34), "L", 0, 10), "S")
            cp(vw("JK", 160, C), ind(full("WJ", 34), "L", 10, 22), "S")
        layer(t)

        for a in range(0, C, PC[t]):
            b = min(a + PC[t], C)
            scan(vw("SA", a, b), vw("JK", a, b), vw("one", a, b), vw("SA", a - 1) if a else 160.0, OP.max, OP.add)
            scan(vw("SB", a, b), vw("JK", a, b), vw("stp", a, b), vw("SB", a - 1) if a else -160.0 / 512, OP.min, OP.add)
        if t < 2:
            ts(vw("CL", 0, 8, 2), full("cA", 4), vw("SA", C - 1), -4.0, OP.add, OP.mult)
            ts(vw("CL", 1, 8, 2), full("cB", 4), vw("SB", C - 1), 2048.0, OP.add, OP.mult)
            for k in range(4): cp(vw("CLT", k, 128, 4), ind(full("ZS", 1412), "CL", 2 * k, 2 * k + 2), "VS", 64.0)
        else:
            ts(vw("w_2", 0), vw("SA", C - 1), 512.0, vw(OCC[t], 0), OP.is_le, OP.max)
            ts(vw("w_2", 1), vw("SB", C - 1), -1.0, vw(OCC[t], 1), OP.is_ge, OP.max)
            send(two("fw2"), two("w_2"), "rf2")
            ts(vw("CL", 0), vw("SA", C - 1), -1.0, 864.0, OP.mult, OP.add)
            ts(vw("CL", 1), vw("SB", C - 1), 512.0, 864.0, OP.mult, OP.add)
            for k in range(4): cp(vw("CLT", k, 128, 4), ind(vw("FP", C * k, C * k + C + 1), "CL", 0, 2), "VS", 64.0)
        cq, la = "CQ%d" % t, (0, 160, 192)[t]
        quant(cq, 0, "CLT", 0)
        if t < 2:
            send(vw("LC", la, la + 32) + ("c",), vw(cq, 0, 32) + ("c",), "rc%d" % t)
            send(vw("LCs", la, la + 32), vw(cq + "s", 0, 32), "rc%d" % t)
        else: send2([vw("LC", la, la + 32) + ("c",), vw("LCs", la, la + 128)], [vw(cq, 0, 32) + ("c",), vw(cq + "s", 0, 128)], "rc%d" % t)

    came(2)
    cp(full("BPO", C), ind(full("MB", 34), "L", 0, 22), "S")
    ld("Y", lambda: [(T.bp[:, 0:C], T.BPO[0:128:16, :])], [full("BPO", C)], [])
    ld("Y", lambda: [(T.bp[:, C + 16 * s:C + 16 * s + 16], ap(vw(OCC[3], s))) for s in range(2)], [two(OCC[3])], [], 2)
    ld("Y", lambda: [(T.rt[:], T.RT[:])], [full("RT")], [])
    for c, (j, n) in enumerate(CH):
        quant("QX", j, "XT", 4 * j, n)
        mm(c, "QV", 0, "QX", j, n)
        cp(vw("YO", j, j + n), vw("ps", 512 * c, 512 * c + n), "VS")
        ld("Y", lambda j=j, n=n: [(T.y[:, j:j + n], T.YO[:, j:j + n])], [vw("YO", j, j + n)], [])
        ld("Y", lambda j=j, n=n: [(T.oc[:, 4 * j:4 * j + 4 * n], T.QX[:, j:j + n].bitcast(dt.uint8))], [vw("QX", j, j + n)], [])
    ld("Y", lambda: [(T.osc[4 * k:4 * k + 4, :], T.QXs[32 * k:32 * k + 4, 0:C]) for k in range(4)], [full("QXs", C)], [], 4)
    return ops


def rank_program(g, core, T, topo):
    rank = T.rank_of(core)
    if rank is None: return
    ops = build(g, core, T, topo, T.cores[(rank + 1) % len(T.cores)])
    if "o" not in PLAN: PLAN["o"] = plan(ops)
    order, deps, _ = PLAN["o"]
    eng = {"V": g.vector, "S": g.scalar, "T": g.tensor, "G": g, "Y": g.sync}
    cnt, done, snap, know, nd = {}, {}, {}, {q: {} for q in eng}, 0
    for k, q, _ in order:
        o, kn = ops[k], know[q]
        for (s, v), d in sorted(((done[d], d) for d in deps[k]), key=lambda x: -x[0][1]):
            if kn.get(s, 0) < v:
                eng[q].wait_ge(T.sem[s], v)
                for s2, v2 in list(snap[d].items()) + [(s, v)]: kn[s2] = max(kn.get(s2, 0), v2)
        r = o["fn"][q]()
        if o["kind"] == "c":
            s = "s" + q
            cnt[s] = cnt.get(s, 0) + 1
            r.then_inc(T.sem[s], 1)
        elif o["kind"] == "d":
            s = "d%d" % nd
            nd += 1
            for i in (r if isinstance(r, list) else [r]): i.then_inc(T.sem[s], 16)
            cnt[s] = 16 * o["nd"]
        else:
            s, ne = o["nd"]
            cnt[s] = cnt.get(s, 0) + ne
            cnt["sent"] = cnt.get("sent", 0) + ne
        done[k] = (s, cnt[s])
        snap[k] = dict(kn) if o["kind"] != "n" else {}
    for s in sorted(cnt):
        if know["G"].get(s, 0) < cnt[s]: g.wait_ge(T.sem[s], cnt[s])
